import numpy as np
import ml_dtypes


def mxq(x, axis, fmt="e4m3"):
    dtype, down = {"e4m3": (ml_dtypes.float8_e4m3fn, 7), "e5m2": (ml_dtypes.float8_e5m2, 14)}[fmt]
    v = np.moveaxis(np.asarray(x, np.float32).astype(ml_dtypes.bfloat16).astype(np.float64), axis, -1)
    blocks = v.reshape(v.shape[:-1] + (-1, 32))
    amax = np.abs(blocks).max(-1, keepdims=True)
    byte = np.maximum(np.where(amax > 0, np.frexp(amax)[1] - 1 + 127, 0) - down, 1)
    scale = np.exp2(byte - 127.0)
    codes = (blocks / scale).astype(np.float32).astype(dtype).astype(np.float64)
    return np.moveaxis((codes * scale).reshape(v.shape), -1, axis)


WIDE = False


def mx_kscale(k):
    if not WIDE:
        return np.ones(k)
    levels = np.array([10, -10, 5, -5, 0])
    if k % 512:
        return np.exp2(np.random.permutation(np.resize(levels, k // 32))).repeat(32)
    a = np.empty((k // 512, 16))
    for p in range(k // 512):
        a[p, :8] = np.random.permutation(np.resize(levels, 8))
        for g in range(8):
            far = levels[np.abs(levels - a[p, g]) >= 10]
            a[p, g + 8] = far[np.random.randint(len(far))]
    return np.exp2(a.ravel()).repeat(32)


BF16 = ml_dtypes.bfloat16


def bf(x):
    return np.asarray(x, np.float32).astype(BF16)


def f64(x):
    return np.asarray(x).astype(np.float64)


E2M1 = np.array([0.0, 0.5, 1.0, 1.5, 2.0, 3.0, 4.0, 6.0, -0.0, -0.5, -1.0, -1.5, -2.0, -3.0, -4.0, -6.0])


def pack_weight(w, fmt):
    k, n = w.shape
    w = f64(bf(w)).reshape(k // 32, 32, n)
    amax = np.abs(w).max(1)
    if fmt == "e4m3":
        byte = np.frexp(amax)[1] - 1 + 127 - 7
    else:
        mant, ex = np.frexp(amax / 6.0)
        byte = np.where(mant > 0.5, ex, ex - 1) + 127
    byte = np.clip(np.where(amax > 0, byte, 1), 1, 254)
    scaled = (w * np.exp2(127.0 - byte)[:, None, :]).reshape(k, n).astype(np.float32)
    by_word = np.ascontiguousarray(scaled.reshape(k // 512, 128, 4, n).transpose(0, 1, 3, 2))
    if fmt == "e4m3":
        words = by_word.astype(ml_dtypes.float8_e4m3fn).view(np.uint8)
    else:
        c = by_word.astype(ml_dtypes.float4_e2m1fn).view(np.uint8) & 0xF
        words = c[..., 0::2] | (c[..., 1::2] << 4)
    return np.ascontiguousarray(words), np.ascontiguousarray(byte.astype(np.uint8).reshape(k // 512, 16, n))


def unpack_weight(words, scales, fmt):
    g, p, n, _ = words.shape
    if fmt == "e4m3":
        vals = np.ascontiguousarray(words).view(ml_dtypes.float8_e4m3fn).astype(np.float64)
    else:
        nib = np.empty((g, p, n, 4), np.uint8)
        nib[..., 0::2] = words & 0xF
        nib[..., 1::2] = words >> 4
        vals = E2M1[nib]
    vals = vals * np.repeat(np.exp2(scales.astype(np.float64) - 127.0), 8, axis=1)[..., None]
    return vals.transpose(0, 1, 3, 2).reshape(g * 512, n)
def pack4(w):
    words, scales = pack_weight(w, "e2m1")
    return words.reshape(words.shape[0], 128, -1), scales


def unpack4(words, scales):
    return unpack_weight(words.reshape(words.shape[0], 128, -1, 2), scales, "e2m1")


M, K, N, R = 2048, 1024, 2048, 256


def draw0():
    s = mx_kscale(K)
    u = mx_kscale(M)
    keep = 1.0 * (np.fft.rfft(np.random.standard_normal(K)).real > 0)
    flip = np.sign(np.random.standard_normal((K, 1)))
    both = np.concatenate([np.eye(K), np.random.standard_normal((K, R)) / np.sqrt(K)], axis=1)
    both = flip * np.fft.irfft(keep[:, None] * np.fft.rfft(flip * both, axis=0), axis=0)
    e_words, e_scales = pack4(np.random.standard_normal((M, R)) / np.sqrt(M) / u[:, None])
    d_words, d_scales = pack4(np.random.standard_normal((M, N)) / np.sqrt(M) / u[:, None])
    return {"x": bf(np.random.standard_normal((M, K)) * s),
            "proj": bf(both[:, :K] / s[:, None]),
            "a": bf(both[:, K:] / s[:, None]),
            "r": bf((1 + 0.3 * np.random.standard_normal(M)) * u),
            "e_words": e_words, "e_scales": e_scales,
            "d_words": d_words, "d_scales": d_scales}


def core(x, proj, a, r, e_words, e_scales, d_words, d_scales):
    xq = mxq(f64(x), 1, "e4m3")
    rw = f64(r)[:, None]
    xh = (xq @ mxq(f64(proj), 0, "e4m3")) * rw
    z = (xq @ mxq(f64(a), 0, "e4m3")) * rw
    grad_a = mxq(xh, 0, "e4m3").T @ unpack4(e_words, e_scales)
    grad_b = mxq(z, 0, "e4m3").T @ unpack4(d_words, d_scales)
    return grad_a, grad_b


def e4m3fn_bytes(y):
    return np.clip(np.asarray(y, np.float64), -448.0, 448.0).astype(np.float32).astype(ml_dtypes.float8_e4m3fn).view(np.uint8)


def e4m3fn_values(b):
    return np.asarray(b, np.uint8).view(ml_dtypes.float8_e4m3fn).astype(np.float64)


def setup_inputs():
    d = draw0()
    x0 = np.asarray(d['x']).astype(np.float64)
    s = (np.max(np.abs(x0), axis=(0,), keepdims=True) / 448.0).astype(np.float32)
    out = {}
    for k, v in d.items():
        if k == 'x':
            out['x_bytes'] = e4m3fn_bytes(x0 / s.astype(np.float64))
            out['x_scale'] = s
        else:
            out[k] = v
    return out


def reference(x_bytes, x_scale, proj, a, r, e_words, e_scales, d_words, d_scales):
    return core(e4m3fn_values(x_bytes) * x_scale.astype(np.float64), proj, a, r, e_words, e_scales, d_words, d_scales)

@@ -1,0 +1,444 @@
+from contextlib import ExitStack
+
+import concourse.mybir as mybir
+from concourse.masks import make_identity
+
+M, K, N, R = 2048, 1024, 2048, 256
+FLOPS = 2 * M * K * (K + R) + 2 * K * M * R + 2 * R * M * N
+
+F32 = mybir.dt.float32
+BF16 = mybir.dt.bfloat16
+I32 = mybir.dt.int32
+U32 = mybir.dt.uint32
+U8 = mybir.dt.uint8
+E4M3 = mybir.dt.float8_e4m3fn
+E4M3X4 = mybir.dt.float8_e4m3fn_x4
+E2M1X4 = mybir.dt.float4_e2m1fn_x4
+MULT = mybir.AluOpType.mult
+COPY = mybir.ActivationFunctionType.Copy
+
+P = 128
+T4 = 4
+GROUP = P * T4
+GROUPS = M // GROUP
+KP = K // GROUP
+HALF = 512
+
+
+ORDER = """
+XS:0 PI:00.V.- PT:01.0 PT:01.1 PE:01.0 PE:01.1 PQ:00 PI:a.S.0 XM:0 XM:1 TR:0 TR:1 PI:a.S.1 PI:a.S.2
+PT:10.0 PI:a.S.3 PQ:01 PE:10.0 EV:0 PT:10.1 PT:11.0 XM:2 EV:1 XM:3 PT:11.1 PE:10.1 XM:4 XQ:0 PE:11.0
+PE:11.1 TR:2 PQ:a EV:2 TR:3 TR:4 XQ:1 EV:3 H:0.0 Z:0 XE:0.0 H:1.0 Z:1 PQ:10 XE:1.0 PQ:11 H:0.1 XQ:2
+XQ:3 XM:5 Z:2 H:1.1 XE:0.1 EV:4 XM:6 XM:7 H:2.0 XM:8 H:3.0 Z:3 XE:2.0 TR:5 TR:6 XE:1.1 H:2.1 EV:5
+H:3.1 TR:7 XM:9 XQ:4 ZE:0.0 TR:8 ZE:0.1 EV:6 TR:9 XE:2.1 XE:3.0 H:4.0 EV:7 EV:8 XQ:5 H:4.1 Z:4 XQ:6
+XQ:7 XE:3.1 XE:4.0 H:5.0 XM:10 Z:5 XE:4.1 H:6.0 Z:6 H:5.1 Z:7 EV:9 XM:11 TR:10 XE:5.0 TR:11 XE:5.1
+XM:12 ZE:1.0 XM:13 XQ:8 EV:10 ZE:1.1 EV:11 XQ:9 TR:12 H:7.0 XE:6.0 H:6.1 XE:7.0 H:7.1 ZQ:0 XE:6.1
+XQ:10 H:8.1 Z:8 ZQ:1 H:9.1 Z:9 XE:7.1 EV:12 XE:8.1 XE:9.1 H:10.1 XM:14 XQ:11 Z:10 XE:10.1 H:8.0
+XE:8.0 XQ:12 Z:11 H:11.1 H:9.0 XM:15 ZE:2.0 TR:13 XE:9.0 EV:13 XE:11.1 TR:14 XI:0.0 ZE:2.1 XQ:13
+EV:14 TR:15 H:10.0 Z:12 H:11.0 XE:10.0 EV:15 Z:13 XQ:14 H:12.0 Z:14 XE:11.0 ZQ:2 XE:12.0 H:13.0
+XQ:15 Z:15 H:12.1 H:14.0 XE:13.0 XI:0.1 H:13.1 XE:12.1 ZE:3.0 XE:14.0 H:15.0 ZE:3.1 XE:13.1 XE:15.0
+HQ:0.0 H:14.1 ZQ:3 XE:14.1 GB:0 HQ:0.1 GBO:0.S GB:1 H:15.1 XI:1.0 GB:2 GBO:1.S XE:15.1 XI:2.1.0
+GBO:2.S GB:3 XI:2.1.1 XI:2.0 HQ:1.0 HQ:2.0 GB:4 XI:2.1.2 GB:5 GBO:3.S GBO:4.S XI:3.0 GBO:5.S GB:6
+HQ:3.0 GA:0 XI:1.1 XI:2.1.3 GB:7 HQ:1.1 GAO:0.S GA:1 XI:3.1a GBO:6.S XI:3.1b HQ:2.1 HQ:3.1a GA:2
+HQ:3.1b GBO:7.S GA:3a GA:3b GAO:1.V GAO:2.S GAO:3a.V GAO:3b.S
+"""
+
+
+def tile_protected_adapter_gradients_s13_kernel(
+    tc, x_bytes, x_scale, proj, a, r, e_words, e_scales, d_words, d_scales, out_0, out_1
+):
+    nc = tc.nc
+    with ExitStack() as ctx:
+        keep = ctx.enter_context(tc.tile_pool(name="keep", bufs=1))
+        xbp = ctx.enter_context(tc.tile_pool(name="xbp", bufs=8))
+        xgp = ctx.enter_context(tc.tile_pool(name="xgp", bufs=8))
+        hpl = ctx.enter_context(tc.tile_pool(name="hpl", bufs=3))
+        grp = ctx.enter_context(tc.tile_pool(name="grp", bufs=2))
+        outp = ctx.enter_context(tc.tile_pool(name="outp", bufs=6))
+        ps_tr = ctx.enter_context(tc.psum_pool(name="ps_tr", bufs=3))
+        ps_z = ctx.enter_context(tc.psum_pool(name="ps_z", bufs=1))
+        ps_mm = ctx.enter_context(tc.psum_pool(name="ps_mm", bufs=3))
+
+        warm = keep.tile([P, 1], F32, name="warm")
+        nc.gpsimd.memset(warm[:], 0.0)
+        nc.scalar.activation(out=warm[:], in_=warm[:], func=COPY)
+        ident = keep.tile([P, P], F32, name="ident")
+        make_identity(nc, ident[:])
+        ident16 = keep.tile([P, P], BF16, name="ident16")
+        nc.gpsimd.tensor_copy(out=ident16[:], in_=ident[:])
+        es = keep.tile([P, GROUPS, R], U8, name="es", align_bytes=64)
+        ds = keep.tile([P, GROUPS, N], U8, name="ds", align_bytes=64)
+        nc.gpsimd.memset(es[:].rearrange("p g n -> p (g n)").bitcast(I32), 0)
+        nc.gpsimd.memset(ds[:].rearrange("p g n -> p (g n)").bitcast(I32), 0)
+
+        sc_rows = keep.tile([P, P], F32, name="sc_rows")
+        nc.vector.memset(sc_rows[:], 0.0)
+
+        r16 = keep.tile([P, GROUPS, T4], BF16, name="r16")
+        nc.scalar.dma_start(out=r16[:], in_=r.rearrange("(g p t) -> p g t", p=P, t=T4))
+        r32 = keep.tile([P, GROUPS, T4], F32, name="r32")
+        nc.gpsimd.tensor_copy(out=r32[:], in_=r16[:])
+
+        proj_v = proj.rearrange("(a p j) n -> a p j n", p=P, j=T4)
+        xb_v = x_bytes.rearrange("(g p t) k -> g p t k", p=P, t=T4)
+        praw = {}
+
+        def load_proj(c, kp):
+            w = keep.tile([P, T4, HALF], BF16, name="praw%d%d" % (c, kp))
+            nc.sync.dma_start(out=w[:], in_=proj_v[kp, :, :, c * HALF : (c + 1) * HALF])
+            praw[c, kp] = w
+
+        xs = keep.tile([P, 2, HALF], F32, name="xs")
+        sc_col = keep.tile([P, K // P], F32, name="sc_col")
+
+        def spread_scales():
+            bank = ps_tr.tile([P, P], F32, name="bank_tr")
+            nc.tensor.transpose(bank[:], sc_rows[:], ident[:])
+            nc.scalar.copy(out=sc_col[:], in_=bank[:, 0 : K // P])
+            for b in range(2):
+                bank = ps_mm.tile([P, HALF], F32, name="bank_mm")
+                for j in range(HALF // P):
+                    m = b * (HALF // P) + j
+                    nc.tensor.transpose(
+                        bank[:, j * P : (j + 1) * P], sc_col[:, m : m + 1].to_broadcast([P, P]), ident[:]
+                    )
+                nc.scalar.copy(out=xs[:, b, :], in_=bank[:])
+
+        x_in = {}
+
+        def load_x(g):
+            xt = keep.tile([P, T4, K], U8, name="x_in%d" % g)
+            nc.sync.dma_start(out=xt[:], in_=xb_v[g])
+            for t in range(T4):
+                x_in[g, t] = xt[:, t, :]
+
+        nc.sync.dma_start(out=sc_rows[0 : K // P, :], in_=x_scale.rearrange("o (m p) -> (o m) p", p=P))
+        load_proj(0, 0)
+        for b in range(2):
+            xt = keep.tile([P, 2, K], U8, name="x_in0%d" % b)
+            nc.sync.dma_start(out=xt[:], in_=xb_v[0, :, 2 * b : 2 * b + 2, :])
+            for t in range(2):
+                x_in[0, 2 * b + t] = xt[:, t, :]
+            if b == 0:
+                load_proj(0, 1)
+        araw = keep.tile([P, KP, T4, R], BF16, name="araw")
+        nc.sync.dma_start(out=araw[:], in_=a.rearrange("(a p j) n -> p a j n", p=P, j=T4))
+        load_proj(1, 0)
+        load_proj(1, 1)
+        for g in range(1, GROUPS):
+            load_x(g)
+        ew = keep.tile([P, GROUPS, 2 * R], U8, name="ew", align_bytes=64)
+        dw = keep.tile([P, GROUPS, 2 * N], U8, name="dw", align_bytes=64)
+        for g in range(GROUPS):
+            nc.sync.dma_start(out=dw[:, g, :].bitcast(I32), in_=d_words[g].bitcast(I32))
+        nc.sync.dma_start(out=ew[:].bitcast(I32), in_=e_words.bitcast(I32).rearrange("g p n -> p g n"))
+        for q in range(4):
+            nc.sync.dma_start(
+                out=ds[32 * q : 32 * q + 4].bitcast(I32),
+                in_=d_scales[:, 4 * q : 4 * q + 4, :].bitcast(I32).rearrange("g q n -> q g n"),
+            )
+            nc.sync.dma_start(
+                out=es[32 * q : 32 * q + 4].bitcast(I32),
+                in_=e_scales[:, 4 * q : 4 * q + 4, :].bitcast(I32).rearrange("g q n -> q g n"),
+            )
+
+        pq = keep.tile([P, 2, KP, HALF], U32, name="pq", align_bytes=64)
+        pqs = keep.tile([P, 2, KP, HALF], U8, name="pqs", align_bytes=64)
+        aq = keep.tile([P, KP, R], U32, name="aq", align_bytes=64)
+        aqs = keep.tile([P, KP, R], U8, name="aqs", align_bytes=64)
+        xq = keep.tile([P, GROUPS, T4, KP, P], U32, name="xq", align_bytes=64)
+        xqs = keep.tile([P, GROUPS, T4, KP, P], U8, name="xqs", align_bytes=64)
+        zq = keep.tile([P, GROUPS, R], U32, name="zq", align_bytes=64)
+        zqs = keep.tile([P, GROUPS, R], U8, name="zqs", align_bytes=64)
+        hq = keep.tile([P, GROUPS, K], U32, name="hq", align_bytes=64)
+        hqs = keep.tile([P, GROUPS, K], U8, name="hqs", align_bytes=64)
+
+        def mx(out, lhs, lhs_s, rhs, rhs_s, start, stop, rdt=E4M3X4):
+            nc.tensor.matmul_mx(
+                out=out,
+                lhsT=lhs.bitcast(E4M3X4),
+                lhsT_scale=lhs_s,
+                rhs=rhs.bitcast(rdt),
+                rhs_scale=rhs_s,
+                start=start,
+                stop=stop,
+            )
+
+        pgr = {}
+
+        pt_bank = {}
+
+        def weave(key, planes):
+            bank = ps_mm.tile([P, 2, P, T4], BF16, name="bank_mm")
+            for b in range(2):
+                nc.tensor.matmul(
+                    out=bank[:, b], lhsT=ident16[:], rhs=planes[b].rearrange("p j n -> p n j"), start=True, stop=True
+                )
+            pt_bank[key] = bank
+
+        a_gr = keep.tile([P, KP, R, T4], BF16, name="a_gr", align_bytes=64)
+        for c in range(2):
+            for kp in range(KP):
+                w = keep.tile([P, HALF, T4], BF16, name="pgr%d%d" % (c, kp), align_bytes=64)
+                pgr[c, kp] = w
+
+        def proj_inter(u, eng, part):
+            f = nc.vector.tensor_copy if eng == "V" else nc.scalar.copy
+            if part == "-":
+                c, kp = int(u[0]), int(u[1])
+                f(out=pgr[c, kp][:], in_=praw[c, kp][:].rearrange("p j n -> p n j"))
+            elif u == "a":
+                kp, h = divmod(int(part), 2)
+                n0, n1 = h * P, (h + 1) * P
+                f(out=a_gr[:, kp, n0:n1, :], in_=araw[:, kp, :, n0:n1].rearrange("p j n -> p n j"))
+            else:
+                c, kp = int(u[0]), int(u[1])
+                n0, n1 = int(part) * P, (int(part) + 1) * P
+                f(out=pgr[c, kp][:, n0:n1, :], in_=praw[c, kp][:, :, n0:n1].rearrange("p j n -> p n j"))
+
+        def proj_weave(u, b):
+            if u == "a":
+                weave((u, b), [araw[:, b, :, 128 * i : 128 * (i + 1)] for i in range(2)])
+            else:
+                c, kp = int(u[0]), int(u[1])
+                weave((u, b), [praw[c, kp][:, :, 256 * b + 128 * i : 256 * b + 128 * (i + 1)] for i in range(2)])
+
+        def proj_out(u, b):
+            if u == "a":
+                w = a_gr[:, b]
+            else:
+                c, kp = int(u[0]), int(u[1])
+                w = pgr[c, kp][:, 256 * b : 256 * (b + 1), :]
+            nc.scalar.copy(out=w.rearrange("p (b n) j -> p b n j", b=2), in_=pt_bank[u, b][:])
+
+        def proj_quant(u):
+            if u == "a":
+                nc.vector.quantize_mx(
+                    out=aq[:].rearrange("p a n -> p (a n)").bitcast(E4M3X4),
+                    scales=aqs[:].rearrange("p a n -> p (a n)"),
+                    in_=a_gr[:].rearrange("p a n j -> p (a n j)"),
+                )
+                return
+            c, kp = int(u[0]), int(u[1])
+            nc.vector.quantize_mx(
+                out=pq[:, c, kp, :].bitcast(E4M3X4),
+                scales=pqs[:, c, kp, :],
+                in_=pgr[c, kp][:].rearrange("p n j -> p (n j)"),
+            )
+
+        x_bf = {}
+
+        def x_mult(g, t):
+            w = xbp.tile([P, K], BF16, name="x_bf")
+            nc.vector.tensor_tensor(out=w[:], in0=x_in[g, t].bitcast(E4M3), in1=xs[:].rearrange("p b k -> p (b k)"), op=MULT)
+            x_bf[g, t] = w
+
+        x_gr = {}
+        tr_bank = {}
+
+        def x_turn(g, t):
+            bank = ps_tr.tile([P, KP, 2, P], F32, name="bank_tr")
+            tr_bank[g, t] = bank
+            words = x_bf[g, t][:].bitcast(F32)
+            for kp in range(KP):
+                for u in range(2):
+                    nc.tensor.transpose(bank[:, kp, u, :], words[:, 256 * kp + u : 256 * (kp + 1) : 2], ident[:])
+
+        def x_out(g, t):
+            bank = tr_bank[g, t]
+            w = xgp.tile([P, KP, P, T4], BF16, name="x_gr", align_bytes=64)
+            nc.scalar.copy(
+                out=w[:].rearrange("p a r j -> p (a r j)").bitcast(F32).rearrange("p (a r u) -> p a r u", a=KP, u=2),
+                in_=bank[:].rearrange("p a u r -> p a r u"),
+            )
+            x_gr[g, t] = w
+
+        def x_quant(g, t):
+            nc.vector.quantize_mx(
+                out=xq[:, g, t].rearrange("p a r -> p (a r)").bitcast(E4M3X4),
+                scales=xqs[:, g, t].rearrange("p a r -> p (a r)"),
+                in_=x_gr[g, t][:].rearrange("p a r j -> p (a r j)"),
+            )
+
+        z_bank = {}
+
+        def z_mm(g, t):
+            for h in range(2):
+                if t == 0:
+                    z_bank[h] = ps_z.tile([P, T4, P], F32, name="z_bank%d" % h)
+                for kp in range(KP):
+                    mx(
+                        z_bank[h][:, t, :],
+                        xq[:, g, t, kp, :],
+                        xqs[:, g, t, kp, :],
+                        aq[:, kp, h * P : (h + 1) * P],
+                        aqs[:, kp, h * P : (h + 1) * P],
+                        kp == 0,
+                        kp == KP - 1,
+                    )
+
+        z_gr = {}
+
+        def z_out(g, h):
+            if h == 0:
+                z_gr[g] = grp.tile([P, R, T4], BF16, name="z_gr", align_bytes=64)
+            w = z_gr[g]
+            if True:
+                nc.vector.tensor_tensor(
+                    out=w[:, h * P : (h + 1) * P, :],
+                    in0=z_bank[h][:].rearrange("p t n -> p n t"),
+                    in1=r32[:, g : g + 1, :].to_broadcast([P, P, T4]),
+                    op=MULT,
+                )
+
+        def z_quant(g):
+            nc.vector.quantize_mx(
+                out=zq[:, g, :].bitcast(E4M3X4), scales=zqs[:, g, :], in_=z_gr[g][:].rearrange("p n t -> p (n t)")
+            )
+
+        h_pl = {}
+        h_bank = {}
+
+        def h_mm(g, t, c):
+            bank = ps_mm.tile([P, HALF], F32, name="bank_mm")
+            for kp in range(KP):
+                mx(
+                    bank[:],
+                    xq[:, g, t, kp, :],
+                    xqs[:, g, t, kp, :],
+                    pq[:, c, kp, :],
+                    pqs[:, c, kp, :],
+                    kp == 0,
+                    kp == KP - 1,
+                )
+            h_bank[g, t, c] = bank
+
+        def h_out(g, t, c):
+            bank = h_bank[g, t, c]
+            if (g, c) not in h_pl:
+                h_pl[g, c] = hpl.tile([P, T4, HALF], BF16, name="h_pl%d" % c)
+            nc.scalar.activation(out=h_pl[g, c][:, t, :], in_=bank[:], func=COPY, scale=r32[:, g, t : t + 1])
+
+        h_gr = {}
+
+        def h_inter(g, c, part):
+            if (g, c) not in h_gr:
+                h_gr[g, c] = grp.tile([P, HALF, T4], BF16, name="h_gr%d" % c, align_bytes=64)
+            f = nc.vector.tensor_copy
+            if part in "0123" and part:
+                f = nc.scalar.copy
+                n0, n1 = int(part) * P, (int(part) + 1) * P
+            else:
+                n0, n1 = {"": (0, HALF), "a": (0, HALF // 2), "b": (HALF // 2, HALF)}[part]
+            f(
+                out=h_gr[g, c][:, n0:n1, :].rearrange("p (n i) t -> p n t i", i=4),
+                in_=h_pl[g, c][:, :, n0:n1].rearrange("p t (n i) -> p n t i", i=4),
+            )
+
+        def h_quant(g, c, part):
+            n0, n1 = {"": (0, HALF), "a": (0, HALF // 2), "b": (HALF // 2, HALF)}[part]
+            nc.vector.quantize_mx(
+                out=hq[:, g, c * HALF + n0 : c * HALF + n1].bitcast(E4M3X4),
+                scales=hqs[:, g, c * HALF + n0 : c * HALF + n1],
+                in_=h_gr[g, c][:, n0:n1, :].rearrange("p n t -> p (n t)"),
+            )
+
+        gb_bank = {}
+
+        def gb_mm(u):
+            rb, nb = divmod(u, N // HALF)
+            bank = ps_mm.tile([P, HALF], F32, name="bank_mm")
+            for g in range(GROUPS):
+                mx(
+                    bank[:],
+                    zq[:, g, rb * P : (rb + 1) * P],
+                    zqs[:, g, rb * P : (rb + 1) * P],
+                    dw[:, g, 2 * HALF * nb : 2 * HALF * (nb + 1)],
+                    ds[:, g, HALF * nb : HALF * (nb + 1)],
+                    g == 0,
+                    g == GROUPS - 1,
+                    E2M1X4,
+                )
+            gb_bank[u] = bank
+
+        def gb_out(u, eng):
+            rb, nb = divmod(u, N // HALF)
+            w = outp.tile([P, HALF], F32, name="res")
+            (nc.scalar.copy if eng == "S" else nc.vector.tensor_copy)(out=w[:], in_=gb_bank[u][:])
+            nc.sync.dma_start(out=out_1[rb * P : (rb + 1) * P, nb * HALF : (nb + 1) * HALF], in_=w[:])
+
+        ga_bank = {}
+
+        def ga_blocks(u):
+            k0 = int(u[0]) * 2
+            return {"": [k0, k0 + 1], "a": [k0], "b": [k0 + 1]}[u[1:]]
+
+        def ga_mm(u):
+            blocks = ga_blocks(u)
+            bank = ps_mm.tile([P, len(blocks), R], F32, name="bank_mm")
+            for b, kb in enumerate(blocks):
+                for h in range(2):
+                    for g in range(GROUPS):
+                        mx(
+                            bank[:, b, h * P : (h + 1) * P],
+                            hq[:, g, kb * P : (kb + 1) * P],
+                            hqs[:, g, kb * P : (kb + 1) * P],
+                            ew[:, g, 2 * P * h : 2 * P * (h + 1)],
+                            es[:, g, P * h : P * (h + 1)],
+                            g == 0,
+                            g == GROUPS - 1,
+                            E2M1X4,
+                        )
+            ga_bank[u] = bank
+
+        def ga_out(u, eng):
+            blocks = ga_blocks(u)
+            w = outp.tile([P, len(blocks), R], F32, name="res")
+            (nc.scalar.copy if eng == "S" else nc.vector.tensor_copy)(out=w[:], in_=ga_bank[u][:])
+            nc.sync.dma_start(
+                out=out_0[blocks[0] * P : (blocks[-1] + 1) * P, :].rearrange("(b p) n -> p b n", p=P), in_=w[:]
+            )
+
+        with tc.manual_schedule():
+            for token in ORDER.split():
+                kind, args = token.split(":")[0], token.split(":")[1].split(".")
+                if kind == "PI":
+                    proj_inter(args[0], args[1], args[2])
+                elif kind == "PT":
+                    proj_weave(args[0], int(args[1]))
+                elif kind == "PE":
+                    proj_out(args[0], int(args[1]))
+                elif kind == "PQ":
+                    proj_quant(args[0])
+                elif kind == "XS":
+                    spread_scales()
+                elif kind == "GBO":
+                    gb_out(int(args[0]), args[1])
+                elif kind == "GAO":
+                    ga_out(args[0], args[1])
+                elif kind == "GB":
+                    gb_mm(int(args[0]))
+                elif kind == "GA":
+                    ga_mm(args[0])
+                elif kind == "ZE":
+                    z_out(int(args[0]), int(args[1]))
+                elif kind == "ZQ":
+                    z_quant(int(args[0]))
+                elif kind == "XI":
+                    h_inter(int(args[0]), int(args[1][0]), args[1][1:] + "".join(args[2:]))
+                elif kind == "HQ":
+                    h_quant(int(args[0]), int(args[1][0]), args[1][1:])
+                elif kind == "H":
+                    h_mm(int(args[0]) // 4, int(args[0]) % 4, int(args[1]))
+                elif kind == "XE":
+                    h_out(int(args[0]) // 4, int(args[0]) % 4, int(args[1]))
+                elif kind == "Z":
+                    z_mm(int(args[0]) // 4, int(args[0]) % 4)
+                elif kind == "XM":
+                    x_mult(int(args[0]) // 4, int(args[0]) % 4)
+                elif kind == "TR":
+                    x_turn(int(args[0]) // 4, int(args[0]) % 4)
+                elif kind == "EV":
+                    x_out(int(args[0]) // 4, int(args[0]) % 4)
+                elif kind == "XQ":
+                    x_quant(int(args[0]) // 4, int(args[0]) % 4)

@@ -19,29 +19,17 @@ COPY = mybir.ActivationFunctionType.Copy
 
 P = 128
 T4 = 4
-GROUP = P * T4
-GROUPS = M // GROUP
-KP = K // GROUP
+PASS = P * T4
+GROUPS = M // PASS
+TILES = GROUPS * T4
+PAIRS = TILES // 2
+KP = K // PASS
 HALF = 512
+PIECE = 256
 
 
-ORDER = """
-XS:0 PI:00.V.- PT:01.0 PT:01.1 PE:01.0 PE:01.1 PQ:00 PI:a.S.0 XM:0 XM:1 TR:0 TR:1 PI:a.S.1 PI:a.S.2
-PT:10.0 PI:a.S.3 PQ:01 PE:10.0 EV:0 PT:10.1 PT:11.0 XM:2 EV:1 XM:3 PT:11.1 PE:10.1 XM:4 XQ:0 PE:11.0
-PE:11.1 TR:2 PQ:a EV:2 TR:3 TR:4 XQ:1 EV:3 H:0.0 Z:0 XE:0.0 H:1.0 Z:1 PQ:10 XE:1.0 PQ:11 H:0.1 XQ:2
-XQ:3 XM:5 Z:2 H:1.1 XE:0.1 EV:4 XM:6 XM:7 H:2.0 XM:8 H:3.0 Z:3 XE:2.0 TR:5 TR:6 XE:1.1 H:2.1 EV:5
-H:3.1 TR:7 XM:9 XQ:4 ZE:0.0 TR:8 ZE:0.1 EV:6 TR:9 XE:2.1 XE:3.0 H:4.0 EV:7 EV:8 XQ:5 H:4.1 Z:4 XQ:6
-XQ:7 XE:3.1 XE:4.0 H:5.0 XM:10 Z:5 XE:4.1 H:6.0 Z:6 H:5.1 Z:7 EV:9 XM:11 TR:10 XE:5.0 TR:11 XE:5.1
-XM:12 ZE:1.0 XM:13 XQ:8 EV:10 ZE:1.1 EV:11 XQ:9 TR:12 H:7.0 XE:6.0 H:6.1 XE:7.0 H:7.1 ZQ:0 XE:6.1
-XQ:10 H:8.1 Z:8 ZQ:1 H:9.1 Z:9 XE:7.1 EV:12 XE:8.1 XE:9.1 H:10.1 XM:14 XQ:11 Z:10 XE:10.1 H:8.0
-XE:8.0 XQ:12 Z:11 H:11.1 H:9.0 XM:15 ZE:2.0 TR:13 XE:9.0 EV:13 XE:11.1 TR:14 XI:0.0 ZE:2.1 XQ:13
-EV:14 TR:15 H:10.0 Z:12 H:11.0 XE:10.0 EV:15 Z:13 XQ:14 H:12.0 Z:14 XE:11.0 ZQ:2 XE:12.0 H:13.0
-XQ:15 Z:15 H:12.1 H:14.0 XE:13.0 XI:0.1 H:13.1 XE:12.1 ZE:3.0 XE:14.0 H:15.0 ZE:3.1 XE:13.1 XE:15.0
-HQ:0.0 H:14.1 ZQ:3 XE:14.1 GB:0 HQ:0.1 GBO:0.S GB:1 H:15.1 XI:1.0 GB:2 GBO:1.S XE:15.1 XI:2.1.0
-GBO:2.S GB:3 XI:2.1.1 XI:2.0 HQ:1.0 HQ:2.0 GB:4 XI:2.1.2 GB:5 GBO:3.S GBO:4.S XI:3.0 GBO:5.S GB:6
-HQ:3.0 GA:0 XI:1.1 XI:2.1.3 GB:7 HQ:1.1 GAO:0.S GA:1 XI:3.1a GBO:6.S XI:3.1b HQ:2.1 HQ:3.1a GA:2
-HQ:3.1b GBO:7.S GA:3a GA:3b GAO:1.V GAO:2.S GAO:3a.V GAO:3b.S
-"""
+SCALAR_PIECES = 3
+PER_STEP = [0, 0, 0, 1, 1, 1, 2, 1]
 
 
 def tile_protected_adapter_gradients_s13_kernel(
@@ -50,83 +38,55 @@ def tile_protected_adapter_gradients_s13_kernel(
     nc = tc.nc
     with ExitStack() as ctx:
         keep = ctx.enter_context(tc.tile_pool(name="keep", bufs=1))
-        xbp = ctx.enter_context(tc.tile_pool(name="xbp", bufs=8))
-        xgp = ctx.enter_context(tc.tile_pool(name="xgp", bufs=8))
-        hpl = ctx.enter_context(tc.tile_pool(name="hpl", bufs=3))
-        grp = ctx.enter_context(tc.tile_pool(name="grp", bufs=2))
+        ring = ctx.enter_context(tc.tile_pool(name="ring", bufs=4))
         outp = ctx.enter_context(tc.tile_pool(name="outp", bufs=6))
-        ps_tr = ctx.enter_context(tc.psum_pool(name="ps_tr", bufs=3))
-        ps_z = ctx.enter_context(tc.psum_pool(name="ps_z", bufs=1))
-        ps_mm = ctx.enter_context(tc.psum_pool(name="ps_mm", bufs=3))
+        psum = ctx.enter_context(tc.psum_pool(name="psum", bufs=8))
+        ctx.enter_context(tc.manual_schedule())
 
-        warm = keep.tile([P, 1], F32, name="warm")
-        nc.gpsimd.memset(warm[:], 0.0)
-        nc.scalar.activation(out=warm[:], in_=warm[:], func=COPY)
+        proj_v = proj.rearrange("(a p j) n -> a p j n", p=P, j=T4)
+        xb_v = x_bytes.rearrange("(g p t) k -> g p t k", p=P, t=T4)
+        p_raw = {}
+        x_in = {}
+
+        def load_proj(c, kp):
+            w = keep.tile([P, T4, HALF], BF16, name="p_raw%d%d" % (c, kp))
+            nc.sync.dma_start(out=w[:], in_=proj_v[kp, :, :, c * HALF : (c + 1) * HALF])
+            p_raw[c, kp] = w
+
+        def load_x(first, count):
+            g, t0 = divmod(first, T4)
+            xt = keep.tile([P, count, K], U8, name="x_in%d" % first)
+            nc.sync.dma_start(out=xt[:], in_=xb_v[g, :, t0 : t0 + count, :])
+            for t in range(count):
+                x_in[first + t] = xt[:, t, :]
+
+        sc_col = keep.tile([P, KP, T4], F32, name="sc_col")
+        nc.sync.dma_start(out=sc_col[:], in_=x_scale.rearrange("o (a p j) -> p (o a) j", p=P, j=T4))
+        r16 = keep.tile([P, GROUPS, T4], BF16, name="r16")
+        nc.scalar.dma_start(out=r16[:], in_=r.rearrange("(g p t) -> p g t", p=P, t=T4))
+        load_proj(0, 0)
+        load_x(0, 2)
+        load_proj(0, 1)
+        load_x(2, 2)
+        load_proj(1, 0)
+        load_proj(1, 1)
+        load_x(4, 4)
+        a_raw = keep.tile([P, KP, T4, R], BF16, name="a_raw")
+        nc.sync.dma_start(out=a_raw[:], in_=a.rearrange("(a p j) n -> p a j n", p=P, j=T4))
+        for g in range(2, GROUPS):
+            load_x(T4 * g, T4)
+
         ident = keep.tile([P, P], F32, name="ident")
         make_identity(nc, ident[:])
         ident16 = keep.tile([P, P], BF16, name="ident16")
         nc.gpsimd.tensor_copy(out=ident16[:], in_=ident[:])
         es = keep.tile([P, GROUPS, R], U8, name="es", align_bytes=64)
         ds = keep.tile([P, GROUPS, N], U8, name="ds", align_bytes=64)
-        nc.gpsimd.memset(es[:].rearrange("p g n -> p (g n)").bitcast(I32), 0)
-        nc.gpsimd.memset(ds[:].rearrange("p g n -> p (g n)").bitcast(I32), 0)
-
-        sc_rows = keep.tile([P, P], F32, name="sc_rows")
-        nc.vector.memset(sc_rows[:], 0.0)
-
-        r16 = keep.tile([P, GROUPS, T4], BF16, name="r16")
-        nc.scalar.dma_start(out=r16[:], in_=r.rearrange("(g p t) -> p g t", p=P, t=T4))
+        nc.vector.memset(es[:].rearrange("p g n -> p (g n)").bitcast(I32), 0)
+        nc.vector.memset(ds[:].rearrange("p g n -> p (g n)").bitcast(I32), 0)
         r32 = keep.tile([P, GROUPS, T4], F32, name="r32")
-        nc.gpsimd.tensor_copy(out=r32[:], in_=r16[:])
+        nc.scalar.activation(out=r32[:], in_=r16[:], func=COPY)
 
-        proj_v = proj.rearrange("(a p j) n -> a p j n", p=P, j=T4)
-        xb_v = x_bytes.rearrange("(g p t) k -> g p t k", p=P, t=T4)
-        praw = {}
-
-        def load_proj(c, kp):
-            w = keep.tile([P, T4, HALF], BF16, name="praw%d%d" % (c, kp))
-            nc.sync.dma_start(out=w[:], in_=proj_v[kp, :, :, c * HALF : (c + 1) * HALF])
-            praw[c, kp] = w
-
-        xs = keep.tile([P, 2, HALF], F32, name="xs")
-        sc_col = keep.tile([P, K // P], F32, name="sc_col")
-
-        def spread_scales():
-            bank = ps_tr.tile([P, P], F32, name="bank_tr")
-            nc.tensor.transpose(bank[:], sc_rows[:], ident[:])
-            nc.scalar.copy(out=sc_col[:], in_=bank[:, 0 : K // P])
-            for b in range(2):
-                bank = ps_mm.tile([P, HALF], F32, name="bank_mm")
-                for j in range(HALF // P):
-                    m = b * (HALF // P) + j
-                    nc.tensor.transpose(
-                        bank[:, j * P : (j + 1) * P], sc_col[:, m : m + 1].to_broadcast([P, P]), ident[:]
-                    )
-                nc.scalar.copy(out=xs[:, b, :], in_=bank[:])
-
-        x_in = {}
-
-        def load_x(g):
-            xt = keep.tile([P, T4, K], U8, name="x_in%d" % g)
-            nc.sync.dma_start(out=xt[:], in_=xb_v[g])
-            for t in range(T4):
-                x_in[g, t] = xt[:, t, :]
-
-        nc.sync.dma_start(out=sc_rows[0 : K // P, :], in_=x_scale.rearrange("o (m p) -> (o m) p", p=P))
-        load_proj(0, 0)
-        for b in range(2):
-            xt = keep.tile([P, 2, K], U8, name="x_in0%d" % b)
-            nc.sync.dma_start(out=xt[:], in_=xb_v[0, :, 2 * b : 2 * b + 2, :])
-            for t in range(2):
-                x_in[0, 2 * b + t] = xt[:, t, :]
-            if b == 0:
-                load_proj(0, 1)
-        araw = keep.tile([P, KP, T4, R], BF16, name="araw")
-        nc.sync.dma_start(out=araw[:], in_=a.rearrange("(a p j) n -> p a j n", p=P, j=T4))
-        load_proj(1, 0)
-        load_proj(1, 1)
-        for g in range(1, GROUPS):
-            load_x(g)
         ew = keep.tile([P, GROUPS, 2 * R], U8, name="ew", align_bytes=64)
         dw = keep.tile([P, GROUPS, 2 * N], U8, name="dw", align_bytes=64)
         for g in range(GROUPS):
@@ -142,303 +102,280 @@ def tile_protected_adapter_gradients_s13_kernel(
                 in_=e_scales[:, 4 * q : 4 * q + 4, :].bitcast(I32).rearrange("g q n -> q g n"),
             )
 
-        pq = keep.tile([P, 2, KP, HALF], U32, name="pq", align_bytes=64)
-        pqs = keep.tile([P, 2, KP, HALF], U8, name="pqs", align_bytes=64)
-        aq = keep.tile([P, KP, R], U32, name="aq", align_bytes=64)
-        aqs = keep.tile([P, KP, R], U8, name="aqs", align_bytes=64)
-        xq = keep.tile([P, GROUPS, T4, KP, P], U32, name="xq", align_bytes=64)
-        xqs = keep.tile([P, GROUPS, T4, KP, P], U8, name="xqs", align_bytes=64)
-        zq = keep.tile([P, GROUPS, R], U32, name="zq", align_bytes=64)
-        zqs = keep.tile([P, GROUPS, R], U8, name="zqs", align_bytes=64)
-        hq = keep.tile([P, GROUPS, K], U32, name="hq", align_bytes=64)
-        hqs = keep.tile([P, GROUPS, K], U8, name="hqs", align_bytes=64)
+        def new_bank(shape, dtype=F32):
+            return psum.tile(shape, dtype, name="bank")
 
-        def mx(out, lhs, lhs_s, rhs, rhs_s, start, stop, rdt=E4M3X4):
+        def quantise(name, grouped, width):
+            codes = keep.tile([P, width], U32, name=name + "_q", align_bytes=64)
+            scales = keep.tile([P, width], U8, name=name + "_s", align_bytes=64)
+            nc.vector.quantize_mx(out=codes[:].bitcast(E4M3X4), scales=scales[:], in_=grouped)
+            return codes, scales
+
+        def mx(out, lhs, lcols, rhs, rhs_scale, start, stop):
             nc.tensor.matmul_mx(
                 out=out,
-                lhsT=lhs.bitcast(E4M3X4),
-                lhsT_scale=lhs_s,
-                rhs=rhs.bitcast(rdt),
-                rhs_scale=rhs_s,
+                lhsT=lhs[0][:, lcols].bitcast(E4M3X4),
+                lhsT_scale=lhs[1][:, lcols],
+                rhs=rhs,
+                rhs_scale=rhs_scale,
                 start=start,
                 stop=stop,
             )
 
-        pgr = {}
-
-        pt_bank = {}
-
-        def weave(key, planes):
-            bank = ps_mm.tile([P, 2, P, T4], BF16, name="bank_mm")
-            for b in range(2):
-                nc.tensor.matmul(
-                    out=bank[:, b], lhsT=ident16[:], rhs=planes[b].rearrange("p j n -> p n j"), start=True, stop=True
-                )
-            pt_bank[key] = bank
-
-        a_gr = keep.tile([P, KP, R, T4], BF16, name="a_gr", align_bytes=64)
-        for c in range(2):
-            for kp in range(KP):
-                w = keep.tile([P, HALF, T4], BF16, name="pgr%d%d" % (c, kp), align_bytes=64)
-                pgr[c, kp] = w
-
-        def proj_inter(u, eng, part):
-            f = nc.vector.tensor_copy if eng == "V" else nc.scalar.copy
-            if part == "-":
-                c, kp = int(u[0]), int(u[1])
-                f(out=pgr[c, kp][:], in_=praw[c, kp][:].rearrange("p j n -> p n j"))
-            elif u == "a":
-                kp, h = divmod(int(part), 2)
-                n0, n1 = h * P, (h + 1) * P
-                f(out=a_gr[:, kp, n0:n1, :], in_=araw[:, kp, :, n0:n1].rearrange("p j n -> p n j"))
-            else:
-                c, kp = int(u[0]), int(u[1])
-                n0, n1 = int(part) * P, (int(part) + 1) * P
-                f(out=pgr[c, kp][:, n0:n1, :], in_=praw[c, kp][:, :, n0:n1].rearrange("p j n -> p n j"))
-
-        def proj_weave(u, b):
-            if u == "a":
-                weave((u, b), [araw[:, b, :, 128 * i : 128 * (i + 1)] for i in range(2)])
-            else:
-                c, kp = int(u[0]), int(u[1])
-                weave((u, b), [praw[c, kp][:, :, 256 * b + 128 * i : 256 * b + 128 * (i + 1)] for i in range(2)])
-
-        def proj_out(u, b):
-            if u == "a":
-                w = a_gr[:, b]
-            else:
-                c, kp = int(u[0]), int(u[1])
-                w = pgr[c, kp][:, 256 * b : 256 * (b + 1), :]
-            nc.scalar.copy(out=w.rearrange("p (b n) j -> p b n j", b=2), in_=pt_bank[u, b][:])
-
-        def proj_quant(u):
-            if u == "a":
-                nc.vector.quantize_mx(
-                    out=aq[:].rearrange("p a n -> p (a n)").bitcast(E4M3X4),
-                    scales=aqs[:].rearrange("p a n -> p (a n)"),
-                    in_=a_gr[:].rearrange("p a n j -> p (a n j)"),
-                )
-                return
-            c, kp = int(u[0]), int(u[1])
-            nc.vector.quantize_mx(
-                out=pq[:, c, kp, :].bitcast(E4M3X4),
-                scales=pqs[:, c, kp, :],
-                in_=pgr[c, kp][:].rearrange("p n j -> p (n j)"),
+        def interleave(copy, out, in_):
+            copy(
+                out=out.rearrange("p (n i) t -> p n t i", i=4),
+                in_=in_.rearrange("p t (n i) -> p n t i", i=4),
             )
 
+        xs = keep.tile([P, K], F32, name="xs")
+
+        def spread_scales(kp):
+            bank = new_bank([P, T4, P])
+            for j in range(T4):
+                nc.tensor.transpose(bank[:, j, :], sc_col[:, kp, j : j + 1].to_broadcast([P, P]), ident[:])
+            nc.scalar.copy(out=xs[:, kp * PASS : (kp + 1) * PASS].rearrange("p (n j) -> p n j", j=T4), in_=bank[:].rearrange("p j n -> p n j"))
+
+        p_gr = {}
+        pq = {}
+
+        def proj_tile(c, kp):
+            p_gr[c, kp] = keep.tile([P, HALF, T4], BF16, name="p_gr%d%d" % (c, kp), align_bytes=64)
+            return p_gr[c, kp]
+
+        def proj_weave(c, kp, halves=(0, 1)):
+            w = p_gr[c, kp] if (c, kp) in p_gr else proj_tile(c, kp)
+            for b in halves:
+                bank = new_bank([P, 2, P, T4], BF16)
+                for i in range(2):
+                    n0 = (2 * b + i) * P
+                    nc.tensor.matmul(
+                        out=bank[:, i],
+                        lhsT=ident16[:],
+                        rhs=p_raw[c, kp][:, :, n0 : n0 + P].rearrange("p j n -> p n j"),
+                        start=True,
+                        stop=True,
+                    )
+                nc.scalar.copy(
+                    out=w[:, 2 * P * b : 2 * P * (b + 1), :].rearrange("p n j -> p (n j)"),
+                    in_=bank[:].rearrange("p b n j -> p (b n j)"),
+                )
+
+        def proj_quant(c, kp):
+            pq[c, kp] = quantise("p%d%d" % (c, kp), p_gr[c, kp][:].rearrange("p n j -> p (n j)"), HALF)
+
+        a_gr = keep.tile([P, KP, R, T4], BF16, name="a_gr", align_bytes=64)
+        aq = []
+
+        def a_inter(kp):
+            interleave(nc.vector.tensor_copy, a_gr[:, kp], a_raw[:, kp])
+
+        def a_quant():
+            aq.extend(quantise("a", a_gr[:].rearrange("p a n j -> p (a n j)"), KP * R))
+
         x_bf = {}
-
-        def x_mult(g, t):
-            w = xbp.tile([P, K], BF16, name="x_bf")
-            nc.vector.tensor_tensor(out=w[:], in0=x_in[g, t].bitcast(E4M3), in1=xs[:].rearrange("p b k -> p (b k)"), op=MULT)
-            x_bf[g, t] = w
-
         x_gr = {}
-        tr_bank = {}
+        xq = {}
 
-        def x_turn(g, t):
-            bank = ps_tr.tile([P, KP, 2, P], F32, name="bank_tr")
-            tr_bank[g, t] = bank
-            words = x_bf[g, t][:].bitcast(F32)
+        def x_mult(i, parts=1):
+            x_bf[i] = ring.tile([P, K], BF16, name="x_bf")
+            for part in range(parts):
+                cols = slice(part * K // parts, (part + 1) * K // parts)
+                nc.vector.tensor_tensor(
+                    out=x_bf[i][:, cols], in0=x_in[i][:, cols].bitcast(E4M3), in1=xs[:, cols], op=MULT
+                )
+
+        def x_turn(i, copy=nc.scalar.copy):
+            bank = new_bank([P, KP, 2, P])
+            words = x_bf[i][:].bitcast(F32)
             for kp in range(KP):
                 for u in range(2):
                     nc.tensor.transpose(bank[:, kp, u, :], words[:, 256 * kp + u : 256 * (kp + 1) : 2], ident[:])
-
-        def x_out(g, t):
-            bank = tr_bank[g, t]
-            w = xgp.tile([P, KP, P, T4], BF16, name="x_gr", align_bytes=64)
-            nc.scalar.copy(
-                out=w[:].rearrange("p a r j -> p (a r j)").bitcast(F32).rearrange("p (a r u) -> p a r u", a=KP, u=2),
+            x_gr[i] = ring.tile([P, KP * P * T4], BF16, name="x_gr", align_bytes=64)
+            copy(
+                out=x_gr[i][:].bitcast(F32).rearrange("p (a r u) -> p a r u", a=KP, u=2),
                 in_=bank[:].rearrange("p a u r -> p a r u"),
             )
-            x_gr[g, t] = w
 
-        def x_quant(g, t):
-            nc.vector.quantize_mx(
-                out=xq[:, g, t].rearrange("p a r -> p (a r)").bitcast(E4M3X4),
-                scales=xqs[:, g, t].rearrange("p a r -> p (a r)"),
-                in_=x_gr[g, t][:].rearrange("p a r j -> p (a r j)"),
-            )
+        def x_quant(i):
+            xq[i] = quantise("x%d" % i, x_gr[i][:], KP * P)
 
-        z_bank = {}
+        h_pl = {}
 
-        def z_mm(g, t):
-            for h in range(2):
-                if t == 0:
-                    z_bank[h] = ps_z.tile([P, T4, P], F32, name="z_bank%d" % h)
+        def h_mm(i, c):
+            g, t = divmod(i, T4)
+            bank = new_bank([P, HALF])
+            for kp in range(KP):
+                codes, scales = pq[c, kp]
+                mx(bank[:], xq[i], slice(kp * P, (kp + 1) * P), codes[:].bitcast(E4M3X4), scales[:], kp == 0, kp == KP - 1)
+            if t == 0:
+                h_pl[g, c] = keep.tile([P, T4, HALF], BF16, name="h_pl%d%d" % (g, c))
+            nc.scalar.activation(out=h_pl[g, c][:, t, :], in_=bank[:], func=COPY, scale=r32[:, g, t : t + 1])
+
+        z_pl = {}
+        z_gr = {}
+        zq = {}
+
+        def z_mm(s, on_vector=False):
+            g, t0 = divmod(2 * s, T4)
+            bank = new_bank([P, 2, R])
+            for b in range(2):
                 for kp in range(KP):
+                    cols = slice(kp * R, (kp + 1) * R)
                     mx(
-                        z_bank[h][:, t, :],
-                        xq[:, g, t, kp, :],
-                        xqs[:, g, t, kp, :],
-                        aq[:, kp, h * P : (h + 1) * P],
-                        aqs[:, kp, h * P : (h + 1) * P],
+                        bank[:, b, :],
+                        xq[2 * s + b],
+                        slice(kp * P, (kp + 1) * P),
+                        aq[0][:, cols].bitcast(E4M3X4),
+                        aq[1][:, cols],
                         kp == 0,
                         kp == KP - 1,
                     )
+            if t0 == 0:
+                z_pl[g] = keep.tile([P, T4, R], BF16, name="z_pl%d" % g)
+            for b in range(2):
+                t = t0 + b
+                if on_vector:
+                    nc.vector.tensor_scalar(
+                        out=z_pl[g][:, t, :], in0=bank[:, b, :], scalar1=r32[:, g, t : t + 1], scalar2=None, op0=MULT
+                    )
+                else:
+                    nc.scalar.activation(out=z_pl[g][:, t, :], in_=bank[:, b, :], func=COPY, scale=r32[:, g, t : t + 1])
 
-        z_gr = {}
-
-        def z_out(g, h):
-            if h == 0:
-                z_gr[g] = grp.tile([P, R, T4], BF16, name="z_gr", align_bytes=64)
-            w = z_gr[g]
-            if True:
-                nc.vector.tensor_tensor(
-                    out=w[:, h * P : (h + 1) * P, :],
-                    in0=z_bank[h][:].rearrange("p t n -> p n t"),
-                    in1=r32[:, g : g + 1, :].to_broadcast([P, P, T4]),
-                    op=MULT,
-                )
+        def z_inter(g):
+            z_gr[g] = ring.tile([P, R, T4], BF16, name="z_gr", align_bytes=64, bufs=2)
+            interleave(nc.vector.tensor_copy, z_gr[g][:], z_pl[g][:])
 
         def z_quant(g):
-            nc.vector.quantize_mx(
-                out=zq[:, g, :].bitcast(E4M3X4), scales=zqs[:, g, :], in_=z_gr[g][:].rearrange("p n t -> p (n t)")
-            )
-
-        h_pl = {}
-        h_bank = {}
-
-        def h_mm(g, t, c):
-            bank = ps_mm.tile([P, HALF], F32, name="bank_mm")
-            for kp in range(KP):
-                mx(
-                    bank[:],
-                    xq[:, g, t, kp, :],
-                    xqs[:, g, t, kp, :],
-                    pq[:, c, kp, :],
-                    pqs[:, c, kp, :],
-                    kp == 0,
-                    kp == KP - 1,
-                )
-            h_bank[g, t, c] = bank
-
-        def h_out(g, t, c):
-            bank = h_bank[g, t, c]
-            if (g, c) not in h_pl:
-                h_pl[g, c] = hpl.tile([P, T4, HALF], BF16, name="h_pl%d" % c)
-            nc.scalar.activation(out=h_pl[g, c][:, t, :], in_=bank[:], func=COPY, scale=r32[:, g, t : t + 1])
+            zq[g] = quantise("z%d" % g, z_gr[g][:].rearrange("p n t -> p (n t)"), R)
 
         h_gr = {}
+        hq = {}
 
-        def h_inter(g, c, part):
-            if (g, c) not in h_gr:
-                h_gr[g, c] = grp.tile([P, HALF, T4], BF16, name="h_gr%d" % c, align_bytes=64)
-            f = nc.vector.tensor_copy
-            if part in "0123" and part:
-                f = nc.scalar.copy
-                n0, n1 = int(part) * P, (int(part) + 1) * P
-            else:
-                n0, n1 = {"": (0, HALF), "a": (0, HALF // 2), "b": (HALF // 2, HALF)}[part]
-            f(
-                out=h_gr[g, c][:, n0:n1, :].rearrange("p (n i) t -> p n t i", i=4),
-                in_=h_pl[g, c][:, :, n0:n1].rearrange("p t (n i) -> p n t i", i=4),
-            )
+        def h_inter(g, b):
+            c, n0 = divmod(b * PIECE, HALF)
+            h_gr[g, b] = ring.tile([P, PIECE, T4], BF16, name="h_gr", align_bytes=64)
+            interleave(nc.vector.tensor_copy, h_gr[g, b][:], h_pl[g, c][:, :, n0 : n0 + PIECE])
 
-        def h_quant(g, c, part):
-            n0, n1 = {"": (0, HALF), "a": (0, HALF // 2), "b": (HALF // 2, HALF)}[part]
-            nc.vector.quantize_mx(
-                out=hq[:, g, c * HALF + n0 : c * HALF + n1].bitcast(E4M3X4),
-                scales=hqs[:, g, c * HALF + n0 : c * HALF + n1],
-                in_=h_gr[g, c][:, n0:n1, :].rearrange("p n t -> p (n t)"),
-            )
+        def h_inter_scalar(g, b, half):
+            c, n0 = divmod(b * PIECE + half * P, HALF)
+            if half == 0:
+                h_gr[g, b] = keep.tile([P, PIECE, T4], BF16, name="h_gs%d" % g, align_bytes=64)
+            interleave(nc.scalar.copy, h_gr[g, b][:, half * P : (half + 1) * P], h_pl[g, c][:, :, n0 : n0 + P])
 
-        gb_bank = {}
+        def h_quant(g, b):
+            hq[g, b] = quantise("h%d%d" % (g, b), h_gr[g, b][:].rearrange("p n t -> p (n t)"), PIECE)
 
-        def gb_mm(u):
-            rb, nb = divmod(u, N // HALF)
-            bank = ps_mm.tile([P, HALF], F32, name="bank_mm")
+        last_b = K // PIECE - 1
+        by_scalar = [(g, last_b) for g in range(GROUPS - SCALAR_PIECES, GROUPS)]
+        pieces = [(g, b) for g in range(GROUPS) for b in range(K // PIECE) if (g, b) not in by_scalar]
+        taken = []
+
+        def h_pieces(chosen):
+            for g, b in chosen:
+                h_inter(g, b)
+                if taken:
+                    h_quant(*taken[-1])
+                taken.append((g, b))
+
+        def store(bank, dst, copy):
+            w = outp.tile(list(bank.shape), F32, name="res")
+            copy(out=w[:], in_=bank[:])
+            nc.sync.dma_start(out=dst, in_=w[:])
+
+        def gb_mm(units):
+            banks = [new_bank([P, HALF]) for u in units]
+            for groups in (range(GROUPS - 1), (GROUPS - 1,)):
+                for u, bank in zip(units, banks):
+                    rb, nb = divmod(u, N // HALF)
+                    for g in groups:
+                        mx(
+                            bank[:],
+                            zq[g],
+                            slice(rb * P, (rb + 1) * P),
+                            dw[:, g, 2 * HALF * nb : 2 * HALF * (nb + 1)].bitcast(E2M1X4),
+                            ds[:, g, HALF * nb : HALF * (nb + 1)],
+                            g == 0,
+                            g == GROUPS - 1,
+                        )
+            for u, bank in zip(units, banks):
+                rb, nb = divmod(u, N // HALF)
+                store(bank, out_1[rb * P : (rb + 1) * P, nb * HALF : (nb + 1) * HALF], nc.scalar.copy)
+
+        def ga_mm(kb):
+            b, n0 = divmod(kb * P, PIECE)
+            bank = new_bank([P, R])
             for g in range(GROUPS):
                 mx(
                     bank[:],
-                    zq[:, g, rb * P : (rb + 1) * P],
-                    zqs[:, g, rb * P : (rb + 1) * P],
-                    dw[:, g, 2 * HALF * nb : 2 * HALF * (nb + 1)],
-                    ds[:, g, HALF * nb : HALF * (nb + 1)],
+                    hq[g, b],
+                    slice(n0, n0 + P),
+                    ew[:, g, :].bitcast(E2M1X4),
+                    es[:, g, :],
                     g == 0,
                     g == GROUPS - 1,
-                    E2M1X4,
                 )
-            gb_bank[u] = bank
+            store(bank, out_0[kb * P : (kb + 1) * P, :], nc.scalar.copy)
 
-        def gb_out(u, eng):
-            rb, nb = divmod(u, N // HALF)
-            w = outp.tile([P, HALF], F32, name="res")
-            (nc.scalar.copy if eng == "S" else nc.vector.tensor_copy)(out=w[:], in_=gb_bank[u][:])
-            nc.sync.dma_start(out=out_1[rb * P : (rb + 1) * P, nb * HALF : (nb + 1) * HALF], in_=w[:])
+        for kp in range(KP):
+            spread_scales(kp)
+        interleave(nc.vector.tensor_copy, proj_tile(0, 0)[:, : 2 * P], p_raw[0, 0][:, :, : 2 * P])
+        proj_weave(0, 0, (1,))
+        x_mult(0, KP)
+        x_mult(1)
+        proj_quant(0, 0)
+        proj_weave(0, 1)
+        x_turn(0)
+        x_turn(1)
+        proj_weave(1, 0)
+        x_mult(2)
+        proj_quant(0, 1)
+        x_quant(0)
+        x_quant(1)
+        x_mult(3)
+        proj_quant(1, 0)
+        proj_weave(1, 1)
+        h_mm(0, 0)
+        h_mm(1, 0)
 
-        ga_bank = {}
+        for s in range(PAIRS):
+            now, ahead, far = [[i for i in (2 * k, 2 * k + 1) if i < TILES] for k in (s, s + 1, s + 2)]
+            for i in ahead:
+                x_turn(i, nc.scalar.copy if far else nc.vector.tensor_copy)
+            for i in far:
+                x_mult(i)
+                if i == 4:
+                    proj_quant(1, 1)
+            if s == 1:
+                a_inter(0)
+            if s == 2:
+                a_inter(1)
+            z_pairs = [k for k in range(PAIRS) if max(k, 3 + k // 2) == s]
+            for k in z_pairs:
+                z_mm(k, not ahead)
+            for c in range(2):
+                for i in now:
+                    if s > 0 or c > 0:
+                        h_mm(i, c)
+            for i in ahead:
+                x_quant(i)
+            if s == 2:
+                a_quant()
+            z_groups = [k // 2 for k in z_pairs if k % 2]
+            for g in z_groups:
+                z_inter(g)
+            h_pieces(pieces[len(taken) : len(taken) + PER_STEP[s]])
+            for g in z_groups:
+                z_quant(g)
 
-        def ga_blocks(u):
-            k0 = int(u[0]) * 2
-            return {"": [k0, k0 + 1], "a": [k0], "b": [k0 + 1]}[u[1:]]
-
-        def ga_mm(u):
-            blocks = ga_blocks(u)
-            bank = ps_mm.tile([P, len(blocks), R], F32, name="bank_mm")
-            for b, kb in enumerate(blocks):
-                for h in range(2):
-                    for g in range(GROUPS):
-                        mx(
-                            bank[:, b, h * P : (h + 1) * P],
-                            hq[:, g, kb * P : (kb + 1) * P],
-                            hqs[:, g, kb * P : (kb + 1) * P],
-                            ew[:, g, 2 * P * h : 2 * P * (h + 1)],
-                            es[:, g, P * h : P * (h + 1)],
-                            g == 0,
-                            g == GROUPS - 1,
-                            E2M1X4,
-                        )
-            ga_bank[u] = bank
-
-        def ga_out(u, eng):
-            blocks = ga_blocks(u)
-            w = outp.tile([P, len(blocks), R], F32, name="res")
-            (nc.scalar.copy if eng == "S" else nc.vector.tensor_copy)(out=w[:], in_=ga_bank[u][:])
-            nc.sync.dma_start(
-                out=out_0[blocks[0] * P : (blocks[-1] + 1) * P, :].rearrange("(b p) n -> p b n", p=P), in_=w[:]
-            )
-
-        with tc.manual_schedule():
-            for token in ORDER.split():
-                kind, args = token.split(":")[0], token.split(":")[1].split(".")
-                if kind == "PI":
-                    proj_inter(args[0], args[1], args[2])
-                elif kind == "PT":
-                    proj_weave(args[0], int(args[1]))
-                elif kind == "PE":
-                    proj_out(args[0], int(args[1]))
-                elif kind == "PQ":
-                    proj_quant(args[0])
-                elif kind == "XS":
-                    spread_scales()
-                elif kind == "GBO":
-                    gb_out(int(args[0]), args[1])
-                elif kind == "GAO":
-                    ga_out(args[0], args[1])
-                elif kind == "GB":
-                    gb_mm(int(args[0]))
-                elif kind == "GA":
-                    ga_mm(args[0])
-                elif kind == "ZE":
-                    z_out(int(args[0]), int(args[1]))
-                elif kind == "ZQ":
-                    z_quant(int(args[0]))
-                elif kind == "XI":
-                    h_inter(int(args[0]), int(args[1][0]), args[1][1:] + "".join(args[2:]))
-                elif kind == "HQ":
-                    h_quant(int(args[0]), int(args[1][0]), args[1][1:])
-                elif kind == "H":
-                    h_mm(int(args[0]) // 4, int(args[0]) % 4, int(args[1]))
-                elif kind == "XE":
-                    h_out(int(args[0]) // 4, int(args[0]) % 4, int(args[1]))
-                elif kind == "Z":
-                    z_mm(int(args[0]) // 4, int(args[0]) % 4)
-                elif kind == "XM":
-                    x_mult(int(args[0]) // 4, int(args[0]) % 4)
-                elif kind == "TR":
-                    x_turn(int(args[0]) // 4, int(args[0]) % 4)
-                elif kind == "EV":
-                    x_out(int(args[0]) // 4, int(args[0]) % 4)
-                elif kind == "XQ":
-                    x_quant(int(args[0]) // 4, int(args[0]) % 4)
+        halves = [(g, b, half) for g, b in by_scalar for half in range(2)]
+        gb_mm((0, 1))
+        for u in range(2, 2 * N // HALF):
+            if u - 2 < len(halves):
+                h_inter_scalar(*halves[u - 2])
+            gb_mm((u,))
+        h_pieces(sorted(pieces[len(taken) :], key=lambda piece: piece[1]))
+        for piece in taken[-1:] + by_scalar:
+            h_quant(*piece)
+        for kb in range(K // P):
+            ga_mm(kb)

@@ -39,7 +39,7 @@ def tile_protected_adapter_gradients_s13_kernel(
     with ExitStack() as ctx:
         keep = ctx.enter_context(tc.tile_pool(name="keep", bufs=1))
         ring = ctx.enter_context(tc.tile_pool(name="ring", bufs=4))
-        outp = ctx.enter_context(tc.tile_pool(name="outp", bufs=6))
+        outp = ctx.enter_context(tc.tile_pool(name="outp", bufs=5))
         psum = ctx.enter_context(tc.psum_pool(name="psum", bufs=8))
         ctx.enter_context(tc.manual_schedule())
 
@@ -60,10 +60,10 @@ def tile_protected_adapter_gradients_s13_kernel(
             for t in range(count):
                 x_in[first + t] = xt[:, t, :]
 
-        sc_col = keep.tile([P, KP, T4], F32, name="sc_col")
-        nc.sync.dma_start(out=sc_col[:], in_=x_scale.rearrange("o (a p j) -> p (o a) j", p=P, j=T4))
-        r16 = keep.tile([P, GROUPS, T4], BF16, name="r16")
-        nc.scalar.dma_start(out=r16[:], in_=r.rearrange("(g p t) -> p g t", p=P, t=T4))
+        sc_col = keep.tile([P, KP, 2 * T4], F32, name="sc_col")
+        nc.sync.dma_start(out=sc_col[:, :, :T4], in_=x_scale.rearrange("o (a p j) -> p (o a) j", p=P, j=T4))
+        r16 = keep.tile([P, GROUPS, 4 * T4], BF16, name="r16")
+        nc.scalar.dma_start(out=r16[:, :, :T4], in_=r.rearrange("(g p t) -> p g t", p=P, t=T4))
         load_proj(0, 0)
         load_x(0, 2)
         load_proj(0, 1)
@@ -77,15 +77,13 @@ def tile_protected_adapter_gradients_s13_kernel(
             load_x(T4 * g, T4)
 
         ident = keep.tile([P, P], F32, name="ident")
-        make_identity(nc, ident[:])
-        ident16 = keep.tile([P, P], BF16, name="ident16")
-        nc.gpsimd.tensor_copy(out=ident16[:], in_=ident[:])
+        nc.vector.memset(ident[:], 0.0)
+        make_identity(nc, ident[:], nomemset=True)
         es = keep.tile([P, GROUPS, R], U8, name="es", align_bytes=64)
         ds = keep.tile([P, GROUPS, N], U8, name="ds", align_bytes=64)
         nc.vector.memset(es[:].rearrange("p g n -> p (g n)").bitcast(I32), 0)
         nc.vector.memset(ds[:].rearrange("p g n -> p (g n)").bitcast(I32), 0)
         r32 = keep.tile([P, GROUPS, T4], F32, name="r32")
-        nc.scalar.activation(out=r32[:], in_=r16[:], func=COPY)
 
         ew = keep.tile([P, GROUPS, 2 * R], U8, name="ew", align_bytes=64)
         dw = keep.tile([P, GROUPS, 2 * N], U8, name="dw", align_bytes=64)
@@ -134,7 +132,11 @@ def tile_protected_adapter_gradients_s13_kernel(
             bank = new_bank([P, T4, P])
             for j in range(T4):
                 nc.tensor.transpose(bank[:, j, :], sc_col[:, kp, j : j + 1].to_broadcast([P, P]), ident[:])
-            nc.scalar.copy(out=xs[:, kp * PASS : (kp + 1) * PASS].rearrange("p (n j) -> p n j", j=T4), in_=bank[:].rearrange("p j n -> p n j"))
+            nc.scalar.activation(
+                out=xs[:, kp * PASS : (kp + 1) * PASS].rearrange("p (n j) -> p n j", j=T4),
+                in_=bank[:].rearrange("p j n -> p n j"),
+                func=COPY,
+            )
 
         p_gr = {}
         pq = {}
@@ -143,23 +145,10 @@ def tile_protected_adapter_gradients_s13_kernel(
             p_gr[c, kp] = keep.tile([P, HALF, T4], BF16, name="p_gr%d%d" % (c, kp), align_bytes=64)
             return p_gr[c, kp]
 
-        def proj_weave(c, kp, halves=(0, 1)):
+        def proj_inter(c, kp, copy, quarters):
             w = p_gr[c, kp] if (c, kp) in p_gr else proj_tile(c, kp)
-            for b in halves:
-                bank = new_bank([P, 2, P, T4], BF16)
-                for i in range(2):
-                    n0 = (2 * b + i) * P
-                    nc.tensor.matmul(
-                        out=bank[:, i],
-                        lhsT=ident16[:],
-                        rhs=p_raw[c, kp][:, :, n0 : n0 + P].rearrange("p j n -> p n j"),
-                        start=True,
-                        stop=True,
-                    )
-                nc.scalar.copy(
-                    out=w[:, 2 * P * b : 2 * P * (b + 1), :].rearrange("p n j -> p (n j)"),
-                    in_=bank[:].rearrange("p b n j -> p (b n j)"),
-                )
+            cols = slice(quarters[0] * P, (quarters[-1] + 1) * P)
+            interleave(copy, w[:, cols], p_raw[c, kp][:, :, cols])
 
         def proj_quant(c, kp):
             pq[c, kp] = quantise("p%d%d" % (c, kp), p_gr[c, kp][:].rearrange("p n j -> p (n j)"), HALF)
@@ -279,7 +268,7 @@ def tile_protected_adapter_gradients_s13_kernel(
                 taken.append((g, b))
 
         def store(bank, dst, copy):
-            w = outp.tile(list(bank.shape), F32, name="res")
+            w = outp.tile(list(bank.shape), F32, name="res%d" % bank.shape[1], bufs=5 * HALF // bank.shape[1] - 1)
             copy(out=w[:], in_=bank[:])
             nc.sync.dma_start(out=dst, in_=w[:])
 
@@ -317,25 +306,31 @@ def tile_protected_adapter_gradients_s13_kernel(
                 )
             store(bank, out_0[kb * P : (kb + 1) * P, :], nc.scalar.copy)
 
+        on_v, on_s = nc.vector.tensor_copy, nc.scalar.copy
         for kp in range(KP):
             spread_scales(kp)
-        interleave(nc.vector.tensor_copy, proj_tile(0, 0)[:, : 2 * P], p_raw[0, 0][:, :, : 2 * P])
-        proj_weave(0, 0, (1,))
-        x_mult(0, KP)
-        x_mult(1)
+        nc.scalar.activation(out=r32[:], in_=r16[:, :, :T4], func=COPY)
+        proj_inter(0, 0, on_v, (0, 3))
+        x_mult(0)
         proj_quant(0, 0)
-        proj_weave(0, 1)
+        x_mult(1)
+        for q in range(4):
+            proj_inter(0, 1, on_s, (q,))
         x_turn(0)
+        proj_inter(1, 0, on_s, (3,))
         x_turn(1)
-        proj_weave(1, 0)
         x_mult(2)
         proj_quant(0, 1)
         x_quant(0)
+        proj_inter(1, 0, on_v, (0, 2))
         x_quant(1)
         x_mult(3)
         proj_quant(1, 0)
-        proj_weave(1, 1)
+        for q in range(2):
+            proj_inter(1, 1, on_s, (q,))
         h_mm(0, 0)
+        for q in range(2, 4):
+            proj_inter(1, 1, on_s, (q,))
         h_mm(1, 0)
 
         for s in range(PAIRS):

@@ -29,7 +29,7 @@ PIECE = 256
 
 
 SCALAR_PIECES = 3
-PER_STEP = [0, 0, 0, 1, 1, 1, 2, 1]
+PER_STEP = [0, 0, 0, 1, 0, 0, 1, 1]
 
 
 def tile_protected_adapter_gradients_s13_kernel(
@@ -61,7 +61,7 @@ def tile_protected_adapter_gradients_s13_kernel(
                 x_in[first + t] = xt[:, t, :]
 
         sc_col = keep.tile([P, KP, 2 * T4], F32, name="sc_col")
-        nc.sync.dma_start(out=sc_col[:, :, :T4], in_=x_scale.rearrange("o (a p j) -> p (o a) j", p=P, j=T4))
+        nc.scalar.dma_start(out=sc_col[:, :, :T4], in_=x_scale.rearrange("o (a p j) -> p (o a) j", p=P, j=T4))
         r16 = keep.tile([P, GROUPS, 4 * T4], BF16, name="r16")
         nc.scalar.dma_start(out=r16[:, :, :T4], in_=r.rearrange("(g p t) -> p g t", p=P, t=T4))
         load_proj(0, 0)
@@ -126,18 +126,6 @@ def tile_protected_adapter_gradients_s13_kernel(
                 in_=in_.rearrange("p t (n i) -> p n t i", i=4),
             )
 
-        xs = keep.tile([P, K], F32, name="xs")
-
-        def spread_scales(kp):
-            bank = new_bank([P, T4, P])
-            for j in range(T4):
-                nc.tensor.transpose(bank[:, j, :], sc_col[:, kp, j : j + 1].to_broadcast([P, P]), ident[:])
-            nc.scalar.activation(
-                out=xs[:, kp * PASS : (kp + 1) * PASS].rearrange("p (n j) -> p n j", j=T4),
-                in_=bank[:].rearrange("p j n -> p n j"),
-                func=COPY,
-            )
-
         p_gr = {}
         pq = {}
 
@@ -166,25 +154,28 @@ def tile_protected_adapter_gradients_s13_kernel(
         x_gr = {}
         xq = {}
 
-        def x_mult(i, parts=1):
-            x_bf[i] = ring.tile([P, K], BF16, name="x_bf")
-            for part in range(parts):
-                cols = slice(part * K // parts, (part + 1) * K // parts)
-                nc.vector.tensor_tensor(
-                    out=x_bf[i][:, cols], in0=x_in[i][:, cols].bitcast(E4M3), in1=xs[:, cols], op=MULT
-                )
+        x_bank = {}
 
-        def x_turn(i, copy=nc.scalar.copy):
-            bank = new_bank([P, KP, 2, P])
+        def x_widen(i):
+            x_bf[i] = ring.tile([P, K], BF16, name="x_bf")
+            nc.scalar.copy(out=x_bf[i][:], in_=x_in[i].bitcast(E4M3))
+
+        def x_turn(i):
+            x_bank[i] = new_bank([P, KP, 2, P])
             words = x_bf[i][:].bitcast(F32)
             for kp in range(KP):
                 for u in range(2):
-                    nc.tensor.transpose(bank[:, kp, u, :], words[:, 256 * kp + u : 256 * (kp + 1) : 2], ident[:])
+                    nc.tensor.transpose(x_bank[i][:, kp, u, :], words[:, 256 * kp + u : 256 * (kp + 1) : 2], ident[:])
+
+        def x_mult(i):
             x_gr[i] = ring.tile([P, KP * P * T4], BF16, name="x_gr", align_bytes=64)
-            copy(
-                out=x_gr[i][:].bitcast(F32).rearrange("p (a r u) -> p a r u", a=KP, u=2),
-                in_=bank[:].rearrange("p a u r -> p a r u"),
-            )
+            for kp in range(KP):
+                nc.vector.tensor_tensor(
+                    out=x_gr[i][:, kp * PASS : (kp + 1) * PASS].rearrange("p (r u e) -> p r u e", u=2, e=2),
+                    in0=x_bank[i][:, kp].bitcast(BF16).rearrange("p u (r e) -> p r u e", e=2),
+                    in1=sc_col[:, kp : kp + 1, :T4].rearrange("p o (u e) -> p o u e", e=2).to_broadcast([P, P, 2, 2]),
+                    op=MULT,
+                )
 
         def x_quant(i):
             xq[i] = quantise("x%d" % i, x_gr[i][:], KP * P)
@@ -307,59 +298,56 @@ def tile_protected_adapter_gradients_s13_kernel(
             store(bank, out_0[kb * P : (kb + 1) * P, :], nc.scalar.copy)
 
         on_v, on_s = nc.vector.tensor_copy, nc.scalar.copy
-        for kp in range(KP):
-            spread_scales(kp)
         nc.scalar.activation(out=r32[:], in_=r16[:, :, :T4], func=COPY)
         proj_inter(0, 0, on_v, (0, 3))
-        x_mult(0)
-        proj_quant(0, 0)
-        x_mult(1)
-        for q in range(4):
-            proj_inter(0, 1, on_s, (q,))
+        x_widen(0)
+        x_widen(1)
         x_turn(0)
-        proj_inter(1, 0, on_s, (3,))
         x_turn(1)
-        x_mult(2)
+        proj_inter(0, 1, on_v, (0, 1))
+        for q in (2, 3):
+            proj_inter(0, 1, on_s, (q,))
+        proj_quant(0, 0)
+        x_widen(2)
+        x_widen(3)
+        x_mult(0)
         proj_quant(0, 1)
         x_quant(0)
-        proj_inter(1, 0, on_v, (0, 2))
+        x_mult(1)
+        for q in range(4):
+            proj_inter(1, 0, on_s, (q,))
         x_quant(1)
-        x_mult(3)
+        proj_inter(1, 1, on_v, (0, 3))
         proj_quant(1, 0)
-        for q in range(2):
-            proj_inter(1, 1, on_s, (q,))
-        h_mm(0, 0)
-        for q in range(2, 4):
-            proj_inter(1, 1, on_s, (q,))
-        h_mm(1, 0)
 
         for s in range(PAIRS):
             now, ahead, far = [[i for i in (2 * k, 2 * k + 1) if i < TILES] for k in (s, s + 1, s + 2)]
             for i in ahead:
-                x_turn(i, nc.scalar.copy if far else nc.vector.tensor_copy)
-            for i in far:
+                x_turn(i)
+            if s == 0:
+                proj_quant(1, 1)
+            for i in ahead:
                 x_mult(i)
-                if i == 4:
-                    proj_quant(1, 1)
-            if s == 1:
-                a_inter(0)
-            if s == 2:
-                a_inter(1)
+            for i in far:
+                x_widen(i)
             z_pairs = [k for k in range(PAIRS) if max(k, 3 + k // 2) == s]
             for k in z_pairs:
                 z_mm(k, not ahead)
             for c in range(2):
                 for i in now:
-                    if s > 0 or c > 0:
-                        h_mm(i, c)
+                    h_mm(i, c)
             for i in ahead:
                 x_quant(i)
-            if s == 2:
-                a_quant()
+            if s == 1:
+                a_inter(0)
+            if s == 1:
+                a_inter(1)
             z_groups = [k // 2 for k in z_pairs if k % 2]
             for g in z_groups:
                 z_inter(g)
             h_pieces(pieces[len(taken) : len(taken) + PER_STEP[s]])
+            if s == 1:
+                a_quant()
             for g in z_groups:
                 z_quant(g)
 

@@ -15,6 +15,7 @@ E4M3 = mybir.dt.float8_e4m3fn
 E4M3X4 = mybir.dt.float8_e4m3fn_x4
 E2M1X4 = mybir.dt.float4_e2m1fn_x4
 MULT = mybir.AluOpType.mult
+ADD = mybir.AluOpType.add
 COPY = mybir.ActivationFunctionType.Copy
 
 P = 128
@@ -28,8 +29,17 @@ HALF = 512
 PIECE = 256
 
 
-SCALAR_PIECES = 3
-PER_STEP = [0, 0, 0, 1, 0, 0, 1, 1]
+GB_OPEN = 2
+SCALAR_PIECES = 4
+S_STEP = [0, 0, 0, 0, 0, 0, 2, 0]
+S_LATE = 1
+SQ = 2
+SORTED = [0, 1, 1, 1, 1, 1]
+Z0 = 3
+MM_BANKS = 4
+Z_RUN = 3
+XB = 8
+PER_STEP = [0, 0, 0, 0, 0, 0, 1, 1]
 
 
 def tile_protected_adapter_gradients_s13_kernel(
@@ -40,7 +50,7 @@ def tile_protected_adapter_gradients_s13_kernel(
         keep = ctx.enter_context(tc.tile_pool(name="keep", bufs=1))
         ring = ctx.enter_context(tc.tile_pool(name="ring", bufs=4))
         outp = ctx.enter_context(tc.tile_pool(name="outp", bufs=5))
-        psum = ctx.enter_context(tc.psum_pool(name="psum", bufs=8))
+        psum = ctx.enter_context(tc.psum_pool(name="psum", bufs=MM_BANKS))
         ctx.enter_context(tc.manual_schedule())
 
         proj_v = proj.rearrange("(a p j) n -> a p j n", p=P, j=T4)
@@ -60,14 +70,14 @@ def tile_protected_adapter_gradients_s13_kernel(
             for t in range(count):
                 x_in[first + t] = xt[:, t, :]
 
-        sc_col = keep.tile([P, KP, 2 * T4], F32, name="sc_col")
-        nc.scalar.dma_start(out=sc_col[:, :, :T4], in_=x_scale.rearrange("o (a p j) -> p (o a) j", p=P, j=T4))
         r16 = keep.tile([P, GROUPS, 4 * T4], BF16, name="r16")
         nc.scalar.dma_start(out=r16[:, :, :T4], in_=r.rearrange("(g p t) -> p g t", p=P, t=T4))
-        load_proj(0, 0)
+        sc_col = keep.tile([P, KP, 2 * T4], F32, name="sc_col")
+        nc.scalar.dma_start(out=sc_col[:, :, :T4], in_=x_scale.rearrange("o (a p j) -> p (o a) j", p=P, j=T4))
         load_x(0, 2)
-        load_proj(0, 1)
+        load_proj(0, 0)
         load_x(2, 2)
+        load_proj(0, 1)
         load_proj(1, 0)
         load_proj(1, 1)
         load_x(4, 4)
@@ -79,6 +89,8 @@ def tile_protected_adapter_gradients_s13_kernel(
         ident = keep.tile([P, P], F32, name="ident")
         nc.vector.memset(ident[:], 0.0)
         make_identity(nc, ident[:], nomemset=True)
+        one = keep.tile([P, 1], F32, name="one")
+        nc.vector.memset(one[:], 1.0)
         es = keep.tile([P, GROUPS, R], U8, name="es", align_bytes=64)
         ds = keep.tile([P, GROUPS, N], U8, name="ds", align_bytes=64)
         nc.vector.memset(es[:].rearrange("p g n -> p (g n)").bitcast(I32), 0)
@@ -126,11 +138,19 @@ def tile_protected_adapter_gradients_s13_kernel(
                 in_=in_.rearrange("p t (n i) -> p n t i", i=4),
             )
 
+        def pool_interleave(in_):
+            w = keep.tile([P, PIECE, T4], BF16, name="pool_gr", align_bytes=64)
+            nc.gpsimd.tensor_scalar(
+                out=w[:], in0=in_.rearrange("p t n -> p n t"), scalar1=1.0, scalar2=0.0, op0=MULT, op1=ADD
+            )
+            return w[:].rearrange("p n t -> p (n t)")
+
         p_gr = {}
         pq = {}
 
         def proj_tile(c, kp):
-            p_gr[c, kp] = keep.tile([P, HALF, T4], BF16, name="p_gr%d%d" % (c, kp), align_bytes=64)
+            tag = "pool_gr" if (c, kp) == (1, KP - 1) else "p_gr%d%d" % (c, kp)
+            p_gr[c, kp] = keep.tile([P, HALF, T4], BF16, name=tag, align_bytes=64)
             return p_gr[c, kp]
 
         def proj_inter(c, kp, copy, quarters):
@@ -141,14 +161,7 @@ def tile_protected_adapter_gradients_s13_kernel(
         def proj_quant(c, kp):
             pq[c, kp] = quantise("p%d%d" % (c, kp), p_gr[c, kp][:].rearrange("p n j -> p (n j)"), HALF)
 
-        a_gr = keep.tile([P, KP, R, T4], BF16, name="a_gr", align_bytes=64)
-        aq = []
-
-        def a_inter(kp):
-            interleave(nc.vector.tensor_copy, a_gr[:, kp], a_raw[:, kp])
-
-        def a_quant():
-            aq.extend(quantise("a", a_gr[:].rearrange("p a n j -> p (a n j)"), KP * R))
+        aq = {}
 
         x_bf = {}
         x_gr = {}
@@ -156,26 +169,45 @@ def tile_protected_adapter_gradients_s13_kernel(
 
         x_bank = {}
 
-        def x_widen(i):
-            x_bf[i] = ring.tile([P, K], BF16, name="x_bf")
-            nc.scalar.copy(out=x_bf[i][:], in_=x_in[i].bitcast(E4M3))
+        x_words = {}
 
-        def x_turn(i):
-            x_bank[i] = new_bank([P, KP, 2, P])
+        def x_widen(i):
+            x_bf[i] = ring.tile([P, K], BF16, name="x_bf", bufs=XB)
+            nc.scalar.copy(out=x_bf[i][:], in_=x_in[i].bitcast(E4M3))
             words = x_bf[i][:].bitcast(F32)
             for kp in range(KP):
                 for u in range(2):
-                    nc.tensor.transpose(x_bank[i][:, kp, u, :], words[:, 256 * kp + u : 256 * (kp + 1) : 2], ident[:])
+                    x_words[i, kp, u] = words[:, 2 * P * kp + u : 2 * P * (kp + 1) : 2]
 
-        def x_mult(i):
-            x_gr[i] = ring.tile([P, KP * P * T4], BF16, name="x_gr", align_bytes=64)
+        def x_widen_sorted(i):
+            x_bf[i] = ring.tile([P, K], BF16, name="x_bf", bufs=XB)
+            nc.vector.tensor_scalar(
+                out=x_bf[i][:].rearrange("p (u w e) -> p w u e", u=2, e=2),
+                in0=x_in[i].bitcast(E4M3),
+                scalar1=one[:],
+                scalar2=None,
+                op0=MULT,
+            )
+            words = x_bf[i][:].bitcast(F32)
             for kp in range(KP):
-                nc.vector.tensor_tensor(
-                    out=x_gr[i][:, kp * PASS : (kp + 1) * PASS].rearrange("p (r u e) -> p r u e", u=2, e=2),
-                    in0=x_bank[i][:, kp].bitcast(BF16).rearrange("p u (r e) -> p r u e", e=2),
-                    in1=sc_col[:, kp : kp + 1, :T4].rearrange("p o (u e) -> p o u e", e=2).to_broadcast([P, P, 2, 2]),
-                    op=MULT,
-                )
+                for u in range(2):
+                    x_words[i, kp, u] = words[:, (u * KP + kp) * P : (u * KP + kp + 1) * P]
+
+        def x_turn(i):
+            x_bank[i] = psum.tile([P, KP, 2, P], F32, name="x_bank", bufs=8 - MM_BANKS)
+            for kp in range(KP):
+                for u in range(2):
+                    nc.tensor.transpose(x_bank[i][:, kp, u, :], x_words[i, kp, u], ident[:])
+
+        def x_mult(i, kp):
+            if kp == 0:
+                x_gr[i] = ring.tile([P, KP * P * T4], BF16, name="x_gr", align_bytes=64, bufs=2)
+            nc.vector.tensor_tensor(
+                out=x_gr[i][:, kp * PASS : (kp + 1) * PASS].rearrange("p (r u e) -> p r u e", u=2, e=2),
+                in0=x_bank[i][:, kp].bitcast(BF16).rearrange("p u (r e) -> p r u e", e=2),
+                in1=sc_col[:, kp : kp + 1, :T4].rearrange("p o (u e) -> p o u e", e=2).to_broadcast([P, P, 2, 2]),
+                op=MULT,
+            )
 
         def x_quant(i):
             xq[i] = quantise("x%d" % i, x_gr[i][:], KP * P)
@@ -201,13 +233,12 @@ def tile_protected_adapter_gradients_s13_kernel(
             bank = new_bank([P, 2, R])
             for b in range(2):
                 for kp in range(KP):
-                    cols = slice(kp * R, (kp + 1) * R)
                     mx(
                         bank[:, b, :],
                         xq[2 * s + b],
                         slice(kp * P, (kp + 1) * P),
-                        aq[0][:, cols].bitcast(E4M3X4),
-                        aq[1][:, cols],
+                        aq[kp][0][:].bitcast(E4M3X4),
+                        aq[kp][1][:],
                         kp == 0,
                         kp == KP - 1,
                     )
@@ -240,14 +271,14 @@ def tile_protected_adapter_gradients_s13_kernel(
         def h_inter_scalar(g, b, half):
             c, n0 = divmod(b * PIECE + half * P, HALF)
             if half == 0:
-                h_gr[g, b] = keep.tile([P, PIECE, T4], BF16, name="h_gs%d" % g, align_bytes=64)
+                h_gr[g, b] = keep.tile([P, PIECE, T4], BF16, name="h_gs%d%d" % (g, b), align_bytes=64)
             interleave(nc.scalar.copy, h_gr[g, b][:, half * P : (half + 1) * P], h_pl[g, c][:, :, n0 : n0 + P])
 
         def h_quant(g, b):
             hq[g, b] = quantise("h%d%d" % (g, b), h_gr[g, b][:].rearrange("p n t -> p (n t)"), PIECE)
 
         last_b = K // PIECE - 1
-        by_scalar = [(g, last_b) for g in range(GROUPS - SCALAR_PIECES, GROUPS)]
+        by_scalar = [(g, b) for b in (last_b, last_b - 1) for g in range(GROUPS)][:SCALAR_PIECES]
         pieces = [(g, b) for g in range(GROUPS) for b in range(K // PIECE) if (g, b) not in by_scalar]
         taken = []
 
@@ -298,64 +329,98 @@ def tile_protected_adapter_gradients_s13_kernel(
             store(bank, out_0[kb * P : (kb + 1) * P, :], nc.scalar.copy)
 
         on_v, on_s = nc.vector.tensor_copy, nc.scalar.copy
-        nc.scalar.activation(out=r32[:], in_=r16[:, :, :T4], func=COPY)
-        proj_inter(0, 0, on_v, (0, 3))
-        x_widen(0)
-        x_widen(1)
-        x_turn(0)
-        x_turn(1)
-        proj_inter(0, 1, on_v, (0, 1))
-        for q in (2, 3):
-            proj_inter(0, 1, on_s, (q,))
-        proj_quant(0, 0)
-        x_widen(2)
-        x_widen(3)
-        x_mult(0)
-        proj_quant(0, 1)
-        x_quant(0)
-        x_mult(1)
-        for q in range(4):
-            proj_inter(1, 0, on_s, (q,))
-        x_quant(1)
-        proj_inter(1, 1, on_v, (0, 3))
-        proj_quant(1, 0)
+        halves = [(g, b, half) for g, b in by_scalar for half in range(2)]
 
-        for s in range(PAIRS):
+        def scalar_halves(count):
+            for half in halves[:count]:
+                h_inter_scalar(*half)
+                halves.remove(half)
+
+        def vector_pieces(count):
+            h_pieces(pieces[len(taken) : len(taken) + count])
+
+        nc.scalar.activation(out=r32[:], in_=r16[:, :, :T4], func=COPY)
+        for i in range(4):
+            x_widen(i)
+            x_turn(i)
+        proj_inter(0, 0, on_v, (0, 3))
+        for c, kp, q in [(0, 1, q) for q in range(4)] + [(1, 0, q) for q in range(4)] + [(1, 1, q) for q in range(4 - SQ, 4)]:
+            proj_inter(c, kp, on_s, (q,))
+        x_mult(0, 0)
+        x_mult(0, 1)
+        proj_quant(0, 0)
+        x_quant(0)
+        for i in (1, 2):
+            x_mult(i, 0)
+            x_mult(i, 1)
+        proj_quant(0, 1)
+        x_quant(1)
+        x_mult(3, 0)
+        x_quant(2)
+        x_mult(3, 1)
+        x_widen(4)
+        x_widen(5)
+        for i in range(3):
+            h_mm(i, 0)
+        proj_inter(1, 1, on_v, (0, 3 - SQ))
+        x_quant(3)
+        proj_quant(1, 0)
+        proj_quant(1, 1)
+
+        z_ready = []
+        for s in range(1, PAIRS):
             now, ahead, far = [[i for i in (2 * k, 2 * k + 1) if i < TILES] for k in (s, s + 1, s + 2)]
             for i in ahead:
                 x_turn(i)
-            if s == 0:
-                proj_quant(1, 1)
-            for i in ahead:
-                x_mult(i)
+            if s <= KP:
+                pooled = pool_interleave(a_raw[:, s - 1])
+            elif ahead:
+                zg = z_ready.pop(0) if z_ready else None
+                if zg is None:
+                    g, b = pieces.pop(0)
+                    c, n0 = divmod(b * PIECE, HALF)
+                    pooled = pool_interleave(h_pl[g, c][:, :, n0 : n0 + PIECE])
+                else:
+                    pooled = pool_interleave(z_pl[zg][:])
             for i in far:
-                x_widen(i)
-            z_pairs = [k for k in range(PAIRS) if max(k, 3 + k // 2) == s]
+                if i % 2 < 2 - SORTED[s]:
+                    x_widen(i)
+                else:
+                    x_widen_sorted(i)
+            scalar_halves(S_STEP[s])
+            for i in ahead:
+                x_mult(i, 0)
+                x_mult(i, 1)
+            z_pairs = [k for k in range(PAIRS) if max(k, Z0 + k // 2) == s]
             for k in z_pairs:
-                z_mm(k, not ahead)
-            for c in range(2):
-                for i in now:
-                    h_mm(i, c)
+                z_mm(k)
+            z_ready.extend(k // 2 for k in z_pairs if k % 2)
+            if s == 1:
+                h_mm(3, 0)
+                for i in range(4):
+                    h_mm(i, 1)
+            else:
+                for c in range(2):
+                    for i in now:
+                        h_mm(i, c)
             for i in ahead:
                 x_quant(i)
-            if s == 1:
-                a_inter(0)
-            if s == 1:
-                a_inter(1)
-            z_groups = [k // 2 for k in z_pairs if k % 2]
-            for g in z_groups:
-                z_inter(g)
-            h_pieces(pieces[len(taken) : len(taken) + PER_STEP[s]])
-            if s == 1:
-                a_quant()
-            for g in z_groups:
-                z_quant(g)
+            vector_pieces(PER_STEP[s])
+            if s <= KP:
+                aq[s - 1] = quantise("a%d" % s, pooled, R)
+            elif ahead and zg is None:
+                hq[g, b] = quantise("h%d%d" % (g, b), pooled, PIECE)
+            elif ahead:
+                zq[zg] = quantise("z%d" % zg, pooled, R)
+        for g in z_ready:
+            z_inter(g)
+            vector_pieces(1)
+            z_quant(g)
+        scalar_halves(S_LATE)
 
-        halves = [(g, b, half) for g, b in by_scalar for half in range(2)]
-        gb_mm((0, 1))
-        for u in range(2, 2 * N // HALF):
-            if u - 2 < len(halves):
-                h_inter_scalar(*halves[u - 2])
+        gb_mm(range(GB_OPEN))
+        for u in range(GB_OPEN, 2 * N // HALF):
+            scalar_halves(1)
             gb_mm((u,))
         h_pieces(sorted(pieces[len(taken) :], key=lambda piece: piece[1]))
         for piece in taken[-1:] + by_scalar:

@@ -29,14 +29,14 @@ HALF = 512
 PIECE = 256
 
 
-GB_OPEN = 2
-SCALAR_PIECES = 4
-S_STEP = [0, 0, 0, 0, 0, 0, 2, 0]
+GB_OPEN = 3
+SCALAR_PIECES = 3
+S_STEP = [0, 0, 0, 0, 0, 0, 1, 0]
 S_LATE = 1
 SQ = 2
-SORTED = [0, 1, 1, 1, 1, 1]
+SORTED = [0, 1, 1, 1, 2, 2]
 Z0 = 3
-MM_BANKS = 4
+MM_BANKS = 5
 Z_RUN = 3
 XB = 8
 PER_STEP = [0, 0, 0, 0, 0, 0, 1, 1]
@@ -138,18 +138,21 @@ def tile_protected_adapter_gradients_s13_kernel(
                 in_=in_.rearrange("p t (n i) -> p n t i", i=4),
             )
 
+        def pool_copy(out, in_):
+            nc.gpsimd.tensor_scalar(
+                out=out, in0=in_.rearrange("p t n -> p n t"), scalar1=1.0, scalar2=0.0, op0=MULT, op1=ADD
+            )
+
         def pool_interleave(in_):
             w = keep.tile([P, PIECE, T4], BF16, name="pool_gr", align_bytes=64)
-            nc.gpsimd.tensor_scalar(
-                out=w[:], in0=in_.rearrange("p t n -> p n t"), scalar1=1.0, scalar2=0.0, op0=MULT, op1=ADD
-            )
+            pool_copy(w[:], in_)
             return w[:].rearrange("p n t -> p (n t)")
 
         p_gr = {}
         pq = {}
 
         def proj_tile(c, kp):
-            tag = "pool_gr" if (c, kp) == (1, KP - 1) else "p_gr%d%d" % (c, kp)
+            tag = "pool_gr" if (c, kp) == (1, KP - 1) else "p_gr%d" % kp
             p_gr[c, kp] = keep.tile([P, HALF, T4], BF16, name=tag, align_bytes=64)
             return p_gr[c, kp]
 
@@ -340,16 +343,24 @@ def tile_protected_adapter_gradients_s13_kernel(
             h_pieces(pieces[len(taken) : len(taken) + count])
 
         nc.scalar.activation(out=r32[:], in_=r16[:, :, :T4], func=COPY)
-        for i in range(4):
-            x_widen(i)
+        x_widen_sorted(0)
+        x_widen_sorted(1)
+        proj_inter(0, 0, on_s, (3,))
+        x_widen(2)
+        x_widen(3)
+        for i in range(3):
             x_turn(i)
-        proj_inter(0, 0, on_v, (0, 3))
-        for c, kp, q in [(0, 1, q) for q in range(4)] + [(1, 0, q) for q in range(4)] + [(1, 1, q) for q in range(4 - SQ, 4)]:
-            proj_inter(c, kp, on_s, (q,))
+        proj_inter(0, 0, on_v, (0, 2))
+        for q in range(4):
+            proj_inter(0, 1, on_s, (q,))
         x_mult(0, 0)
         x_mult(0, 1)
+        x_turn(3)
         proj_quant(0, 0)
         x_quant(0)
+        pool_copy(proj_tile(1, 0)[:, : 2 * P], p_raw[1, 0][:, :, : 2 * P])
+        for q in (2, 3):
+            proj_inter(1, 0, on_s, (q,))
         for i in (1, 2):
             x_mult(i, 0)
             x_mult(i, 1)
@@ -360,6 +371,8 @@ def tile_protected_adapter_gradients_s13_kernel(
         x_mult(3, 1)
         x_widen(4)
         x_widen(5)
+        for q in range(4 - SQ, 4):
+            proj_inter(1, 1, on_s, (q,))
         for i in range(3):
             h_mm(i, 0)
         proj_inter(1, 1, on_v, (0, 3 - SQ))
@@ -382,29 +395,34 @@ def tile_protected_adapter_gradients_s13_kernel(
                     pooled = pool_interleave(h_pl[g, c][:, :, n0 : n0 + PIECE])
                 else:
                     pooled = pool_interleave(z_pl[zg][:])
-            for i in far:
-                if i % 2 < 2 - SORTED[s]:
-                    x_widen(i)
-                else:
+            for i in far[:1]:
+                if SORTED[s]:
                     x_widen_sorted(i)
+                else:
+                    x_widen(i)
+            for i in far[1:]:
+                if SORTED[s] < 2:
+                    x_widen(i)
             scalar_halves(S_STEP[s])
             for i in ahead:
                 x_mult(i, 0)
                 x_mult(i, 1)
             z_pairs = [k for k in range(PAIRS) if max(k, Z0 + k // 2) == s]
+            z_ready.extend(k // 2 for k in z_pairs if k % 2)
+            first_half = [(3, 0)] if s == 1 else [(i, 0) for i in now]
+            second_half = [(i, 1) for i in (range(4) if s == 1 else now)]
+            if ahead:
+                for i, c in first_half:
+                    h_mm(i, c)
             for k in z_pairs:
                 z_mm(k)
-            z_ready.extend(k // 2 for k in z_pairs if k % 2)
-            if s == 1:
-                h_mm(3, 0)
-                for i in range(4):
-                    h_mm(i, 1)
-            else:
-                for c in range(2):
-                    for i in now:
-                        h_mm(i, c)
+            for i, c in second_half if ahead else first_half + second_half:
+                h_mm(i, c)
             for i in ahead:
                 x_quant(i)
+            for i in far[1:]:
+                if SORTED[s] == 2:
+                    x_widen_sorted(i)
             vector_pieces(PER_STEP[s])
             if s <= KP:
                 aq[s - 1] = quantise("a%d" % s, pooled, R)

@@ -34,7 +34,7 @@ SCALAR_PIECES = 3
 S_STEP = [0, 0, 0, 0, 0, 0, 1, 0]
 S_LATE = 1
 SQ = 2
-SORTED = [0, 1, 1, 1, 2, 2]
+SORTED = [0, 0, 1, 1, 1, 1]
 Z0 = 3
 MM_BANKS = 5
 Z_RUN = 3
@@ -344,7 +344,7 @@ def tile_protected_adapter_gradients_s13_kernel(
 
         nc.scalar.activation(out=r32[:], in_=r16[:, :, :T4], func=COPY)
         x_widen_sorted(0)
-        x_widen_sorted(1)
+        x_widen(1)
         proj_inter(0, 0, on_s, (3,))
         x_widen(2)
         x_widen(3)

@@ -39,7 +39,7 @@ Z0 = 3
 MM_BANKS = 5
 Z_RUN = 3
 XB = 8
-PER_STEP = [0, 0, 0, 0, 0, 0, 1, 1]
+PER_STEP = [0, 0, 0, 0, 0, 1, 1, 1]
 
 
 def tile_protected_adapter_gradients_s13_kernel(
@@ -58,10 +58,11 @@ def tile_protected_adapter_gradients_s13_kernel(
         p_raw = {}
         x_in = {}
 
-        def load_proj(c, kp):
-            w = keep.tile([P, T4, HALF], BF16, name="p_raw%d%d" % (c, kp))
-            nc.sync.dma_start(out=w[:], in_=proj_v[kp, :, :, c * HALF : (c + 1) * HALF])
-            p_raw[c, kp] = w
+        def load_proj(kp):
+            w = keep.tile([P, T4, K], BF16, name="p_raw%d" % kp)
+            nc.sync.dma_start(out=w[:], in_=proj_v[kp])
+            for c in range(2):
+                p_raw[c, kp] = w[:, :, c * HALF : (c + 1) * HALF]
 
         def load_x(first, count):
             g, t0 = divmod(first, T4)
@@ -74,12 +75,9 @@ def tile_protected_adapter_gradients_s13_kernel(
         nc.scalar.dma_start(out=r16[:, :, :T4], in_=r.rearrange("(g p t) -> p g t", p=P, t=T4))
         sc_col = keep.tile([P, KP, 2 * T4], F32, name="sc_col")
         nc.scalar.dma_start(out=sc_col[:, :, :T4], in_=x_scale.rearrange("o (a p j) -> p (o a) j", p=P, j=T4))
-        load_x(0, 2)
-        load_proj(0, 0)
-        load_x(2, 2)
-        load_proj(0, 1)
-        load_proj(1, 0)
-        load_proj(1, 1)
+        load_x(0, 4)
+        load_proj(0)
+        load_proj(1)
         load_x(4, 4)
         a_raw = keep.tile([P, KP, T4, R], BF16, name="a_raw")
         nc.sync.dma_start(out=a_raw[:], in_=a.rearrange("(a p j) n -> p a j n", p=P, j=T4))
@@ -152,7 +150,7 @@ def tile_protected_adapter_gradients_s13_kernel(
         pq = {}
 
         def proj_tile(c, kp):
-            tag = "pool_gr" if (c, kp) == (1, KP - 1) else "p_gr%d" % kp
+            tag = "pool_gr" if kp == KP - 1 else "p_gr%d" % c
             p_gr[c, kp] = keep.tile([P, HALF, T4], BF16, name=tag, align_bytes=64)
             return p_gr[c, kp]
 
@@ -197,18 +195,17 @@ def tile_protected_adapter_gradients_s13_kernel(
                     x_words[i, kp, u] = words[:, (u * KP + kp) * P : (u * KP + kp + 1) * P]
 
         def x_turn(i):
-            x_bank[i] = psum.tile([P, KP, 2, P], F32, name="x_bank", bufs=8 - MM_BANKS)
+            x_bank[i] = psum.tile([P, 2, KP, P], F32, name="x_bank", bufs=8 - MM_BANKS)
             for kp in range(KP):
                 for u in range(2):
-                    nc.tensor.transpose(x_bank[i][:, kp, u, :], x_words[i, kp, u], ident[:])
+                    nc.tensor.transpose(x_bank[i][:, u, kp, :], x_words[i, kp, u], ident[:])
 
-        def x_mult(i, kp):
-            if kp == 0:
-                x_gr[i] = ring.tile([P, KP * P * T4], BF16, name="x_gr", align_bytes=64, bufs=2)
+        def x_mult(i):
+            x_gr[i] = ring.tile([P, KP * P * T4], BF16, name="x_gr", align_bytes=64, bufs=2)
             nc.vector.tensor_tensor(
-                out=x_gr[i][:, kp * PASS : (kp + 1) * PASS].rearrange("p (r u e) -> p r u e", u=2, e=2),
-                in0=x_bank[i][:, kp].bitcast(BF16).rearrange("p u (r e) -> p r u e", e=2),
-                in1=sc_col[:, kp : kp + 1, :T4].rearrange("p o (u e) -> p o u e", e=2).to_broadcast([P, P, 2, 2]),
+                out=x_gr[i][:].rearrange("p (a r u e) -> p a r u e", a=KP, u=2, e=2),
+                in0=x_bank[i][:].bitcast(BF16).rearrange("p u a (r e) -> p a r u e", e=2),
+                in1=sc_col[:, :, :T4].rearrange("p a (o u e) -> p a o u e", o=1, e=2).to_broadcast([P, KP, P, 2, 2]),
                 op=MULT,
             )
 
@@ -293,7 +290,7 @@ def tile_protected_adapter_gradients_s13_kernel(
                 taken.append((g, b))
 
         def store(bank, dst, copy):
-            w = outp.tile(list(bank.shape), F32, name="res%d" % bank.shape[1], bufs=5 * HALF // bank.shape[1] - 1)
+            w = outp.tile(list(bank.shape), F32, name="res%d" % bank.shape[1], bufs={HALF: 4, R: 7, P: 2}[bank.shape[1]])
             copy(out=w[:], in_=bank[:])
             nc.sync.dma_start(out=dst, in_=w[:])
 
@@ -316,20 +313,20 @@ def tile_protected_adapter_gradients_s13_kernel(
                 rb, nb = divmod(u, N // HALF)
                 store(bank, out_1[rb * P : (rb + 1) * P, nb * HALF : (nb + 1) * HALF], nc.scalar.copy)
 
-        def ga_mm(kb):
+        def ga_mm(kb, c0=0, width=R, copy=nc.scalar.copy):
             b, n0 = divmod(kb * P, PIECE)
-            bank = new_bank([P, R])
+            bank = new_bank([P, width])
             for g in range(GROUPS):
                 mx(
                     bank[:],
                     hq[g, b],
                     slice(n0, n0 + P),
-                    ew[:, g, :].bitcast(E2M1X4),
-                    es[:, g, :],
+                    ew[:, g, 2 * c0 : 2 * (c0 + width)].bitcast(E2M1X4),
+                    es[:, g, c0 : c0 + width],
                     g == 0,
                     g == GROUPS - 1,
                 )
-            store(bank, out_0[kb * P : (kb + 1) * P, :], nc.scalar.copy)
+            store(bank, out_0[kb * P : (kb + 1) * P, c0 : c0 + width], copy)
 
         on_v, on_s = nc.vector.tensor_copy, nc.scalar.copy
         halves = [(g, b, half) for g, b in by_scalar for half in range(2)]
@@ -344,41 +341,41 @@ def tile_protected_adapter_gradients_s13_kernel(
 
         nc.scalar.activation(out=r32[:], in_=r16[:, :, :T4], func=COPY)
         x_widen_sorted(0)
-        x_widen(1)
-        proj_inter(0, 0, on_s, (3,))
+        x_widen_sorted(1)
         x_widen(2)
         x_widen(3)
         for i in range(3):
             x_turn(i)
-        proj_inter(0, 0, on_v, (0, 2))
-        for q in range(4):
-            proj_inter(0, 1, on_s, (q,))
-        x_mult(0, 0)
-        x_mult(0, 1)
+        pool_copy(proj_tile(0, 0)[:, : 2 * P], p_raw[0, 0][:, :, : 2 * P])
+        for q in (2, 3):
+            proj_inter(0, 0, on_s, (q,))
+        for i in (0, 1):
+            x_mult(i)
         x_turn(3)
         proj_quant(0, 0)
         x_quant(0)
-        pool_copy(proj_tile(1, 0)[:, : 2 * P], p_raw[1, 0][:, :, : 2 * P])
+        proj_inter(0, 1, on_v, (0, 1))
         for q in (2, 3):
             proj_inter(1, 0, on_s, (q,))
-        for i in (1, 2):
-            x_mult(i, 0)
-            x_mult(i, 1)
+        for q in range(2, 4):
+            proj_inter(0, 1, on_s, (q,))
         proj_quant(0, 1)
         x_quant(1)
-        x_mult(3, 0)
-        x_quant(2)
-        x_mult(3, 1)
+        pool_copy(proj_tile(1, 1)[:, : 2 * P], p_raw[1, 1][:, :, : 2 * P])
         x_widen(4)
         x_widen(5)
-        for q in range(4 - SQ, 4):
+        for q in (0, 1):
+            proj_inter(1, 0, on_s, (q,))
+        for q in (2, 3):
             proj_inter(1, 1, on_s, (q,))
-        for i in range(3):
+        for i in (2, 3):
+            x_mult(i)
+        for i in range(2):
             h_mm(i, 0)
-        proj_inter(1, 1, on_v, (0, 3 - SQ))
+        x_quant(2)
         x_quant(3)
-        proj_quant(1, 0)
         proj_quant(1, 1)
+        proj_quant(1, 0)
 
         z_ready = []
         for s in range(1, PAIRS):
@@ -405,11 +402,10 @@ def tile_protected_adapter_gradients_s13_kernel(
                     x_widen(i)
             scalar_halves(S_STEP[s])
             for i in ahead:
-                x_mult(i, 0)
-                x_mult(i, 1)
+                x_mult(i)
             z_pairs = [k for k in range(PAIRS) if max(k, Z0 + k // 2) == s]
             z_ready.extend(k // 2 for k in z_pairs if k % 2)
-            first_half = [(3, 0)] if s == 1 else [(i, 0) for i in now]
+            first_half = [(2, 0), (3, 0)] if s == 1 else [(i, 0) for i in now]
             second_half = [(i, 1) for i in (range(4) if s == 1 else now)]
             if ahead:
                 for i, c in first_half:
@@ -423,13 +419,13 @@ def tile_protected_adapter_gradients_s13_kernel(
             for i in far[1:]:
                 if SORTED[s] == 2:
                     x_widen_sorted(i)
-            vector_pieces(PER_STEP[s])
             if s <= KP:
                 aq[s - 1] = quantise("a%d" % s, pooled, R)
             elif ahead and zg is None:
                 hq[g, b] = quantise("h%d%d" % (g, b), pooled, PIECE)
             elif ahead:
                 zq[zg] = quantise("z%d" % zg, pooled, R)
+            vector_pieces(PER_STEP[s])
         for g in z_ready:
             z_inter(g)
             vector_pieces(1)
@@ -443,5 +439,7 @@ def tile_protected_adapter_gradients_s13_kernel(
         h_pieces(sorted(pieces[len(taken) :], key=lambda piece: piece[1]))
         for piece in taken[-1:] + by_scalar:
             h_quant(*piece)
-        for kb in range(K // P):
+        for kb in range(K // P - 1):
             ga_mm(kb)
+        ga_mm(K // P - 1, 0, P)
+        ga_mm(K // P - 1, P, P, nc.vector.tensor_copy)

@@ -38,7 +38,7 @@ SORTED = [0, 0, 1, 1, 1, 1]
 Z0 = 3
 MM_BANKS = 5
 Z_RUN = 3
-XB = 8
+XB = 6
 PER_STEP = [0, 0, 0, 0, 0, 1, 1, 1]
 
 
@@ -89,14 +89,14 @@ def tile_protected_adapter_gradients_s13_kernel(
         make_identity(nc, ident[:], nomemset=True)
         one = keep.tile([P, 1], F32, name="one")
         nc.vector.memset(one[:], 1.0)
-        es = keep.tile([P, GROUPS, R], U8, name="es", align_bytes=64)
-        ds = keep.tile([P, GROUPS, N], U8, name="ds", align_bytes=64)
+        es = keep.tile([P, GROUPS, R], U8, name="es", align_bytes=256)
+        ds = keep.tile([P, GROUPS, N], U8, name="ds", align_bytes=256)
         nc.vector.memset(es[:].rearrange("p g n -> p (g n)").bitcast(I32), 0)
         nc.vector.memset(ds[:].rearrange("p g n -> p (g n)").bitcast(I32), 0)
         r32 = keep.tile([P, GROUPS, T4], F32, name="r32")
 
-        ew = keep.tile([P, GROUPS, 2 * R], U8, name="ew", align_bytes=64)
-        dw = keep.tile([P, GROUPS, 2 * N], U8, name="dw", align_bytes=64)
+        ew = keep.tile([P, GROUPS, 2 * R], U8, name="ew", align_bytes=256)
+        dw = keep.tile([P, GROUPS, 2 * N], U8, name="dw", align_bytes=256)
         for g in range(GROUPS):
             nc.sync.dma_start(out=dw[:, g, :].bitcast(I32), in_=d_words[g].bitcast(I32))
         nc.sync.dma_start(out=ew[:].bitcast(I32), in_=e_words.bitcast(I32).rearrange("g p n -> p g n"))
@@ -114,8 +114,8 @@ def tile_protected_adapter_gradients_s13_kernel(
             return psum.tile(shape, dtype, name="bank")
 
         def quantise(name, grouped, width):
-            codes = keep.tile([P, width], U32, name=name + "_q", align_bytes=64)
-            scales = keep.tile([P, width], U8, name=name + "_s", align_bytes=64)
+            codes = keep.tile([P, width], U32, name=name + "_q", align_bytes=256)
+            scales = keep.tile([P, width], U8, name=name + "_s", align_bytes=256)
             nc.vector.quantize_mx(out=codes[:].bitcast(E4M3X4), scales=scales[:], in_=grouped)
             return codes, scales
 
@@ -254,7 +254,7 @@ def tile_protected_adapter_gradients_s13_kernel(
                     nc.scalar.activation(out=z_pl[g][:, t, :], in_=bank[:, b, :], func=COPY, scale=r32[:, g, t : t + 1])
 
         def z_inter(g):
-            z_gr[g] = ring.tile([P, R, T4], BF16, name="z_gr", align_bytes=64, bufs=2)
+            z_gr[g] = ring.tile([P, R, T4], BF16, name="z_gr", align_bytes=64, bufs=1)
             interleave(nc.vector.tensor_copy, z_gr[g][:], z_pl[g][:])
 
         def z_quant(g):
@@ -265,7 +265,7 @@ def tile_protected_adapter_gradients_s13_kernel(
 
         def h_inter(g, b):
             c, n0 = divmod(b * PIECE, HALF)
-            h_gr[g, b] = ring.tile([P, PIECE, T4], BF16, name="h_gr", align_bytes=64)
+            h_gr[g, b] = ring.tile([P, PIECE, T4], BF16, name="h_gr", align_bytes=64, bufs=3)
             interleave(nc.vector.tensor_copy, h_gr[g, b][:], h_pl[g, c][:, :, n0 : n0 + PIECE])
 
         def h_inter_scalar(g, b, half):

@@ -23,23 +23,27 @@ T4 = 4
 PASS = P * T4
 GROUPS = M // PASS
 TILES = GROUPS * T4
-PAIRS = TILES // 2
 KP = K // PASS
 HALF = 512
 PIECE = 256
+BANKS = 8
 
-
-GB_OPEN = 3
+WEAVE_BUFS = {"weave_v": 3, "weave_s": 4, "weave_g": 1, "weave_first": 1}
+XBF_BUFS = {1: 2, 2: 2}
+SORTED_BUFS = 2
+SORT_BUFS = 2
+CUT0 = 256
+CUTV = 384
+CUT1 = 256
+CUT2 = 128
+TURN_FIRST = 1
+SORT_PAIRS = (5, 6, 7)
+Z_AFTER = {4: (0, 2, 4), 5: (6,)}
+RES_BUFS = {HALF: 4, R: 7, P: 2}
+MM_BANKS = (4, 5, 2, 3)
+TURN_BANK = {2: 4, 3: 0, 4: 6, 5: 0, 6: 6, 7: 0}
 SCALAR_PIECES = 3
-S_STEP = [0, 0, 0, 0, 0, 0, 1, 0]
-S_LATE = 1
-SQ = 2
-SORTED = [0, 0, 1, 1, 1, 1]
-Z0 = 3
-MM_BANKS = 5
-Z_RUN = 3
-XB = 6
-PER_STEP = [0, 0, 0, 0, 0, 1, 1, 1]
+SORT_FROM = 4
 
 
 def tile_protected_adapter_gradients_s13_kernel(
@@ -48,76 +52,85 @@ def tile_protected_adapter_gradients_s13_kernel(
     nc = tc.nc
     with ExitStack() as ctx:
         keep = ctx.enter_context(tc.tile_pool(name="keep", bufs=1))
-        ring = ctx.enter_context(tc.tile_pool(name="ring", bufs=4))
-        outp = ctx.enter_context(tc.tile_pool(name="outp", bufs=5))
-        psum = ctx.enter_context(tc.psum_pool(name="psum", bufs=MM_BANKS))
+        ring = ctx.enter_context(tc.tile_pool(name="ring", bufs=2))
+        psum = ctx.enter_context(tc.psum_pool(name="psum", bufs=1))
         ctx.enter_context(tc.manual_schedule())
+        on_v, on_s = nc.vector.tensor_copy, nc.scalar.copy
 
         proj_v = proj.rearrange("(a p j) n -> a p j n", p=P, j=T4)
         xb_v = x_bytes.rearrange("(g p t) k -> g p t k", p=P, t=T4)
         p_raw = {}
         x_in = {}
 
-        def load_proj(kp):
-            w = keep.tile([P, T4, K], BF16, name="p_raw%d" % kp)
-            nc.sync.dma_start(out=w[:], in_=proj_v[kp])
-            for c in range(2):
-                p_raw[c, kp] = w[:, :, c * HALF : (c + 1) * HALF]
+        def load_proj(c, kp):
+            w = keep.tile([P, T4, HALF], BF16, name="p_raw%d%d" % (c, kp))
+            nc.sync.dma_start(out=w[:], in_=proj_v[kp][:, :, c * HALF : (c + 1) * HALF])
+            p_raw[c, kp] = w
+
+        def load_a():
+            w = keep.tile([P, KP, T4, R], BF16, name="a_raw")
+            nc.sync.dma_start(out=w[:], in_=a.rearrange("(a p j) n -> p a j n", p=P, j=T4))
+            for kp in range(KP):
+                src["a", kp] = w[:, kp]
+                dst["a", kp] = (aq[kp], 0)
 
         def load_x(first, count):
             g, t0 = divmod(first, T4)
-            xt = keep.tile([P, count, K], U8, name="x_in%d" % first)
-            nc.sync.dma_start(out=xt[:], in_=xb_v[g, :, t0 : t0 + count, :])
+            xt = keep.tile([P, count * K], U8, name="x_in%d" % first)
+            nc.sync.dma_start(out=xt[:].rearrange("p (t k) -> p t k", k=K), in_=xb_v[g, :, t0 : t0 + count, :])
             for t in range(count):
-                x_in[first + t] = xt[:, t, :]
+                x_in[first + t] = (xt, t)
+
+        def x_bytes_of(i, count):
+            xt, t = x_in[i]
+            return xt[:, t * K : (t + count) * K].bitcast(E4M3)
 
         r16 = keep.tile([P, GROUPS, 4 * T4], BF16, name="r16")
-        nc.scalar.dma_start(out=r16[:, :, :T4], in_=r.rearrange("(g p t) -> p g t", p=P, t=T4))
         sc_col = keep.tile([P, KP, 2 * T4], F32, name="sc_col")
-        nc.scalar.dma_start(out=sc_col[:, :, :T4], in_=x_scale.rearrange("o (a p j) -> p (o a) j", p=P, j=T4))
-        load_x(0, 4)
-        load_proj(0)
-        load_proj(1)
-        load_x(4, 4)
-        a_raw = keep.tile([P, KP, T4, R], BF16, name="a_raw")
-        nc.sync.dma_start(out=a_raw[:], in_=a.rearrange("(a p j) n -> p a j n", p=P, j=T4))
-        for g in range(2, GROUPS):
-            load_x(T4 * g, T4)
-
         ident = keep.tile([P, P], F32, name="ident")
-        nc.vector.memset(ident[:], 0.0)
-        make_identity(nc, ident[:], nomemset=True)
         one = keep.tile([P, 1], F32, name="one")
-        nc.vector.memset(one[:], 1.0)
         es = keep.tile([P, GROUPS, R], U8, name="es", align_bytes=256)
         ds = keep.tile([P, GROUPS, N], U8, name="ds", align_bytes=256)
-        nc.vector.memset(es[:].rearrange("p g n -> p (g n)").bitcast(I32), 0)
-        nc.vector.memset(ds[:].rearrange("p g n -> p (g n)").bitcast(I32), 0)
         r32 = keep.tile([P, GROUPS, T4], F32, name="r32")
-
         ew = keep.tile([P, GROUPS, 2 * R], U8, name="ew", align_bytes=256)
         dw = keep.tile([P, GROUPS, 2 * N], U8, name="dw", align_bytes=256)
-        for g in range(GROUPS):
-            nc.sync.dma_start(out=dw[:, g, :].bitcast(I32), in_=d_words[g].bitcast(I32))
-        nc.sync.dma_start(out=ew[:].bitcast(I32), in_=e_words.bitcast(I32).rearrange("g p n -> p g n"))
-        for q in range(4):
-            nc.sync.dma_start(
-                out=ds[32 * q : 32 * q + 4].bitcast(I32),
-                in_=d_scales[:, 4 * q : 4 * q + 4, :].bitcast(I32).rearrange("g q n -> q g n"),
-            )
-            nc.sync.dma_start(
-                out=es[32 * q : 32 * q + 4].bitcast(I32),
-                in_=e_scales[:, 4 * q : 4 * q + 4, :].bitcast(I32).rearrange("g q n -> q g n"),
-            )
 
-        def new_bank(shape, dtype=F32):
-            return psum.tile(shape, dtype, name="bank")
+        def load_small():
+            nc.scalar.dma_start(out=sc_col[:, :, :T4], in_=x_scale.rearrange("o (a p j) -> p (o a) j", p=P, j=T4))
+            nc.scalar.dma_start(out=r16[:, :, :T4], in_=r.rearrange("(g p t) -> p g t", p=P, t=T4))
 
-        def quantise(name, grouped, width):
+        def constants():
+            nc.vector.memset(ident[:], 0.0)
+            make_identity(nc, ident[:], nomemset=True)
+            nc.vector.memset(one[:], 1.0)
+            nc.vector.memset(es[:].rearrange("p g n -> p (g n)").bitcast(I32), 0)
+            nc.vector.memset(ds[:].rearrange("p g n -> p (g n)").bitcast(I32), 0)
+
+        def load_second_stage():
+            for g in range(GROUPS):
+                nc.sync.dma_start(out=dw[:, g, :].bitcast(I32), in_=d_words[g].bitcast(I32))
+            nc.sync.dma_start(out=ew[:].bitcast(I32), in_=e_words.bitcast(I32).rearrange("g p n -> p g n"))
+            for q in range(4):
+                nc.sync.dma_start(
+                    out=ds[32 * q : 32 * q + 4].bitcast(I32),
+                    in_=d_scales[:, 4 * q : 4 * q + 4, :].bitcast(I32).rearrange("g q n -> q g n"),
+                )
+                nc.sync.dma_start(
+                    out=es[32 * q : 32 * q + 4].bitcast(I32),
+                    in_=e_scales[:, 4 * q : 4 * q + 4, :].bitcast(I32).rearrange("g q n -> q g n"),
+                )
+
+        def bank_tile(b, shape):
+            return psum.tile(shape, F32, name="bank%d" % b)
+
+        def mx_tiles(name, width):
             codes = keep.tile([P, width], U32, name=name + "_q", align_bytes=256)
             scales = keep.tile([P, width], U8, name=name + "_s", align_bytes=256)
-            nc.vector.quantize_mx(out=codes[:].bitcast(E4M3X4), scales=scales[:], in_=grouped)
             return codes, scales
+
+        def quantise(dst, c0, grouped):
+            cols = slice(c0, c0 + grouped.shape[1] // T4)
+            nc.vector.quantize_mx(out=dst[0][:, cols].bitcast(E4M3X4), scales=dst[1][:, cols], in_=grouped)
 
         def mx(out, lhs, lcols, rhs, rhs_scale, start, stop):
             nc.tensor.matmul_mx(
@@ -141,163 +154,188 @@ def tile_protected_adapter_gradients_s13_kernel(
                 out=out, in0=in_.rearrange("p t n -> p n t"), scalar1=1.0, scalar2=0.0, op0=MULT, op1=ADD
             )
 
-        def pool_interleave(in_):
-            w = keep.tile([P, PIECE, T4], BF16, name="pool_gr", align_bytes=64)
-            pool_copy(w[:], in_)
-            return w[:].rearrange("p n t -> p (n t)")
+        def flat(w):
+            return w.rearrange("p n t -> p (n t)")
 
-        p_gr = {}
-        pq = {}
+        src = {}
+        dst = {}
+        woven = {}
 
-        def proj_tile(c, kp):
-            tag = "pool_gr" if kp == KP - 1 else "p_gr%d" % c
-            p_gr[c, kp] = keep.tile([P, HALF, T4], BF16, name=tag, align_bytes=64)
-            return p_gr[c, kp]
+        def weave(key, who, tag=None, part=None):
+            n = src[key].shape[2]
+            if key not in woven:
+                tag = tag or {"v": "weave_v", "s": "weave_s", "g": "weave_g"}[who]
+                woven[key] = ring.tile([P, n, T4], BF16, name=tag, align_bytes=64, bufs=WEAVE_BUFS[tag])
+            cols = slice(0, n) if part is None else slice(part[0], part[1])
+            if who == "g":
+                pool_copy(woven[key][:, cols], src[key][:, :, cols])
+            else:
+                interleave(on_v if who == "v" else on_s, woven[key][:, cols], src[key][:, :, cols])
 
-        def proj_inter(c, kp, copy, quarters):
-            w = p_gr[c, kp] if (c, kp) in p_gr else proj_tile(c, kp)
-            cols = slice(quarters[0] * P, (quarters[-1] + 1) * P)
-            interleave(copy, w[:, cols], p_raw[c, kp][:, :, cols])
+        def quant(key):
+            quantise(dst[key][0], dst[key][1], flat(woven[key][:]))
 
-        def proj_quant(c, kp):
-            pq[c, kp] = quantise("p%d%d" % (c, kp), p_gr[c, kp][:].rearrange("p n j -> p (n j)"), HALF)
+        pq = {(c, kp): mx_tiles("p%d%d" % (c, kp), HALF) for c in range(2) for kp in range(KP)}
+        aq = {kp: mx_tiles("a%d" % kp, R) for kp in range(KP)}
+        hq = {g: mx_tiles("h%d" % g, K) for g in range(GROUPS)}
+        zq = {g: mx_tiles("z%d" % g, R) for g in range(GROUPS)}
 
-        aq = {}
+        def proj_part(c, kp, lo, hi):
+            key = ("p", c, kp, lo)
+            src[key] = p_raw[c, kp][:, :, lo:hi]
+            dst[key] = (pq[c, kp], lo)
+            return key
 
-        x_bf = {}
+        x_words = {}
+        x_wide = {}
+        x_bank = {}
         x_gr = {}
         xq = {}
 
-        x_bank = {}
+        def x_widen(i, count=1):
+            w = ring.tile([P, count * K], BF16, name="x_bf%d" % count, bufs=XBF_BUFS[count])
+            nc.scalar.copy(out=w[:], in_=x_bytes_of(i, count))
+            x_wide[i] = w[:]
+            words = w[:].bitcast(F32)
+            for j in range(count):
+                for kp in range(KP):
+                    for u in range(2):
+                        w0 = 2 * P * (KP * j + kp)
+                        x_words[i + j, kp, u] = words[:, w0 + u : w0 + 2 * P : 2]
 
-        x_words = {}
-
-        def x_widen(i):
-            x_bf[i] = ring.tile([P, K], BF16, name="x_bf", bufs=XB)
-            nc.scalar.copy(out=x_bf[i][:], in_=x_in[i].bitcast(E4M3))
-            words = x_bf[i][:].bitcast(F32)
-            for kp in range(KP):
-                for u in range(2):
-                    x_words[i, kp, u] = words[:, 2 * P * kp + u : 2 * P * (kp + 1) : 2]
+        def x_sort(i, count):
+            w = ring.tile([P, 2, count * K // 2], BF16, name="x_sort%d" % count, bufs=SORT_BUFS)
+            nc.vector.tensor_copy(
+                out=w[:].rearrange("p u (w e) -> p u w e", e=2),
+                in_=x_wide[i].rearrange("p (w u e) -> p u w e", u=2, e=2),
+            )
+            for j in range(count):
+                for kp in range(KP):
+                    for u in range(2):
+                        w0 = P * (KP * j + kp)
+                        x_words[i + j, kp, u] = w[:, u].bitcast(F32)[:, w0 : w0 + P]
 
         def x_widen_sorted(i):
-            x_bf[i] = ring.tile([P, K], BF16, name="x_bf", bufs=XB)
+            w = ring.tile([P, K], BF16, name="x_sorted", bufs=SORTED_BUFS)
             nc.vector.tensor_scalar(
-                out=x_bf[i][:].rearrange("p (u w e) -> p w u e", u=2, e=2),
-                in0=x_in[i].bitcast(E4M3),
+                out=w[:].rearrange("p (u w e) -> p w u e", u=2, e=2),
+                in0=x_bytes_of(i, 1),
                 scalar1=one[:],
                 scalar2=None,
                 op0=MULT,
             )
-            words = x_bf[i][:].bitcast(F32)
+            words = w[:].bitcast(F32)
             for kp in range(KP):
                 for u in range(2):
                     x_words[i, kp, u] = words[:, (u * KP + kp) * P : (u * KP + kp + 1) * P]
 
-        def x_turn(i):
-            x_bank[i] = psum.tile([P, 2, KP, P], F32, name="x_bank", bufs=8 - MM_BANKS)
+        def x_widen_sorted_pass(i, kp):
+            w = keep.tile([P, PASS], BF16, name="x_first%d" % kp)
+            nc.vector.tensor_scalar(
+                out=w[:].rearrange("p (u w e) -> p w u e", u=2, e=2),
+                in0=x_bytes_of(i, 1)[:, kp * PASS : (kp + 1) * PASS],
+                scalar1=one[:],
+                scalar2=None,
+                op0=MULT,
+            )
+            for u in range(2):
+                x_words[i, kp, u] = w[:].bitcast(F32)[:, u * P : (u + 1) * P]
+
+        def x_turn(i, b):
+            x_bank[i] = bank_tile(b, [P, 2, KP, P])
             for kp in range(KP):
                 for u in range(2):
                     nc.tensor.transpose(x_bank[i][:, u, kp, :], x_words[i, kp, u], ident[:])
 
         def x_mult(i):
-            x_gr[i] = ring.tile([P, KP * P * T4], BF16, name="x_gr", align_bytes=64, bufs=2)
+            if i % 2 == 0:
+                x_gr[i // 2] = ring.tile([P, 2, KP * P * T4], BF16, name="x_gr", align_bytes=64, bufs=2)
+                xq[i // 2] = mx_tiles("x%d" % i, 2 * KP * P)
             nc.vector.tensor_tensor(
-                out=x_gr[i][:].rearrange("p (a r u e) -> p a r u e", a=KP, u=2, e=2),
+                out=x_gr[i // 2][:, i % 2].rearrange("p (a r u e) -> p a r u e", a=KP, u=2, e=2),
                 in0=x_bank[i][:].bitcast(BF16).rearrange("p u a (r e) -> p a r u e", e=2),
                 in1=sc_col[:, :, :T4].rearrange("p a (o u e) -> p a o u e", o=1, e=2).to_broadcast([P, KP, P, 2, 2]),
                 op=MULT,
             )
 
-        def x_quant(i):
-            xq[i] = quantise("x%d" % i, x_gr[i][:], KP * P)
+        def x_quant(i, count=2):
+            j = i % 2
+            quantise(xq[i // 2], j * KP * P, x_gr[i // 2][:, j : j + count].rearrange("p a n -> p (a n)"))
+
+        def x_cols(i, kp):
+            c0 = ((i % 2) * KP + kp) * P
+            return slice(c0, c0 + P)
 
         h_pl = {}
+        z_pl = {}
 
-        def h_mm(i, c):
-            g, t = divmod(i, T4)
-            bank = new_bank([P, HALF])
+        h_bank = {}
+
+        def h_pass(i, c, kp, b=None):
+            if kp == 0:
+                h_bank[i, c] = bank_tile(b, [P, HALF])
+            codes, scales = pq[c, kp]
+            mx(h_bank[i, c][:], xq[i // 2], x_cols(i, kp), codes[:].bitcast(E4M3X4), scales[:], kp == 0, kp == KP - 1)
+
+        def h_mm(i, c, b):
             for kp in range(KP):
-                codes, scales = pq[c, kp]
-                mx(bank[:], xq[i], slice(kp * P, (kp + 1) * P), codes[:].bitcast(E4M3X4), scales[:], kp == 0, kp == KP - 1)
-            if t == 0:
+                h_pass(i, c, kp, b)
+            h_out(i, c)
+
+        def h_out(i, c):
+            g, t = divmod(i, T4)
+            bank = h_bank[i, c]
+            if (g, c) not in h_pl:
                 h_pl[g, c] = keep.tile([P, T4, HALF], BF16, name="h_pl%d%d" % (g, c))
+                for h in range(2):
+                    src["h", g, 2 * c + h] = h_pl[g, c][:, :, h * PIECE : (h + 1) * PIECE]
+                    dst["h", g, 2 * c + h] = (hq[g], (2 * c + h) * PIECE)
             nc.scalar.activation(out=h_pl[g, c][:, t, :], in_=bank[:], func=COPY, scale=r32[:, g, t : t + 1])
 
-        z_pl = {}
-        z_gr = {}
-        zq = {}
-
-        def z_mm(s, on_vector=False):
-            g, t0 = divmod(2 * s, T4)
-            bank = new_bank([P, 2, R])
-            for b in range(2):
+        def z_mm(i, b):
+            g, t0 = divmod(i, T4)
+            bank = bank_tile(b, [P, 2, R])
+            for j in range(2):
                 for kp in range(KP):
-                    mx(
-                        bank[:, b, :],
-                        xq[2 * s + b],
-                        slice(kp * P, (kp + 1) * P),
-                        aq[kp][0][:].bitcast(E4M3X4),
-                        aq[kp][1][:],
-                        kp == 0,
-                        kp == KP - 1,
-                    )
-            if t0 == 0:
+                    mx(bank[:, j, :], xq[i // 2], x_cols(i + j, kp), aq[kp][0][:].bitcast(E4M3X4), aq[kp][1][:], kp == 0, kp == KP - 1)
+            if g not in z_pl:
                 z_pl[g] = keep.tile([P, T4, R], BF16, name="z_pl%d" % g)
-            for b in range(2):
-                t = t0 + b
-                if on_vector:
-                    nc.vector.tensor_scalar(
-                        out=z_pl[g][:, t, :], in0=bank[:, b, :], scalar1=r32[:, g, t : t + 1], scalar2=None, op0=MULT
-                    )
-                else:
-                    nc.scalar.activation(out=z_pl[g][:, t, :], in_=bank[:, b, :], func=COPY, scale=r32[:, g, t : t + 1])
+                src["z", g] = z_pl[g][:]
+                dst["z", g] = (zq[g], 0)
+            for j in range(2):
+                t = t0 + j
+                nc.scalar.activation(out=z_pl[g][:, t, :], in_=bank[:, j, :], func=COPY, scale=r32[:, g, t : t + 1])
 
-        def z_inter(g):
-            z_gr[g] = ring.tile([P, R, T4], BF16, name="z_gr", align_bytes=64, bufs=1)
-            interleave(nc.vector.tensor_copy, z_gr[g][:], z_pl[g][:])
+        z_bank = {}
 
-        def z_quant(g):
-            zq[g] = quantise("z%d" % g, z_gr[g][:].rearrange("p n t -> p (n t)"), R)
+        def z_mm_direct(g, h, b):
+            z_bank[g, h] = bank_tile(b, [P, T4, P])
+            cols = slice(h * P, (h + 1) * P)
+            for t in range(T4):
+                i = T4 * g + t
+                for kp in range(KP):
+                    mx(z_bank[g, h][:, t, :], xq[i // 2], x_cols(i, kp), aq[kp][0][:, cols].bitcast(E4M3X4), aq[kp][1][:, cols], kp == 0, kp == KP - 1)
 
-        h_gr = {}
-        hq = {}
+        def z_out_direct(g, h):
+            if h == 0:
+                woven["z", g] = ring.tile([P, R, T4], BF16, name="z_direct", align_bytes=64, bufs=2)
+                dst["z", g] = (zq[g], 0)
+            nc.vector.tensor_tensor(
+                out=woven["z", g][:, h * P : (h + 1) * P, :],
+                in0=z_bank[g, h][:].rearrange("p t n -> p n t"),
+                in1=r32[:, g : g + 1, :].to_broadcast([P, P, T4]),
+                op=MULT,
+            )
 
-        def h_inter(g, b):
-            c, n0 = divmod(b * PIECE, HALF)
-            h_gr[g, b] = ring.tile([P, PIECE, T4], BF16, name="h_gr", align_bytes=64, bufs=3)
-            interleave(nc.vector.tensor_copy, h_gr[g, b][:], h_pl[g, c][:, :, n0 : n0 + PIECE])
-
-        def h_inter_scalar(g, b, half):
-            c, n0 = divmod(b * PIECE + half * P, HALF)
-            if half == 0:
-                h_gr[g, b] = keep.tile([P, PIECE, T4], BF16, name="h_gs%d%d" % (g, b), align_bytes=64)
-            interleave(nc.scalar.copy, h_gr[g, b][:, half * P : (half + 1) * P], h_pl[g, c][:, :, n0 : n0 + P])
-
-        def h_quant(g, b):
-            hq[g, b] = quantise("h%d%d" % (g, b), h_gr[g, b][:].rearrange("p n t -> p (n t)"), PIECE)
-
-        last_b = K // PIECE - 1
-        by_scalar = [(g, b) for b in (last_b, last_b - 1) for g in range(GROUPS)][:SCALAR_PIECES]
-        pieces = [(g, b) for g in range(GROUPS) for b in range(K // PIECE) if (g, b) not in by_scalar]
-        taken = []
-
-        def h_pieces(chosen):
-            for g, b in chosen:
-                h_inter(g, b)
-                if taken:
-                    h_quant(*taken[-1])
-                taken.append((g, b))
-
-        def store(bank, dst, copy):
-            w = outp.tile(list(bank.shape), F32, name="res%d" % bank.shape[1], bufs={HALF: 4, R: 7, P: 2}[bank.shape[1]])
+        def store(bank, to, copy):
+            w = ring.tile(list(bank.shape), F32, name="res%d" % bank.shape[1], bufs=RES_BUFS[bank.shape[1]])
             copy(out=w[:], in_=bank[:])
-            nc.sync.dma_start(out=dst, in_=w[:])
+            nc.sync.dma_start(out=to, in_=w[:])
 
-        def gb_mm(units):
-            banks = [new_bank([P, HALF]) for u in units]
+        def gb_mm(units, banks):
+            tiles = [bank_tile(b, [P, HALF]) for b in banks]
             for groups in (range(GROUPS - 1), (GROUPS - 1,)):
-                for u, bank in zip(units, banks):
+                for u, bank in zip(units, tiles):
                     rb, nb = divmod(u, N // HALF)
                     for g in groups:
                         mx(
@@ -309,18 +347,17 @@ def tile_protected_adapter_gradients_s13_kernel(
                             g == 0,
                             g == GROUPS - 1,
                         )
-            for u, bank in zip(units, banks):
+            for u, bank in zip(units, tiles):
                 rb, nb = divmod(u, N // HALF)
-                store(bank, out_1[rb * P : (rb + 1) * P, nb * HALF : (nb + 1) * HALF], nc.scalar.copy)
+                store(bank, out_1[rb * P : (rb + 1) * P, nb * HALF : (nb + 1) * HALF], on_s)
 
-        def ga_mm(kb, c0=0, width=R, copy=nc.scalar.copy):
-            b, n0 = divmod(kb * P, PIECE)
-            bank = new_bank([P, width])
+        def ga_mm(kb, b, c0=0, width=R, copy=on_s):
+            bank = bank_tile(b, [P, width])
             for g in range(GROUPS):
                 mx(
                     bank[:],
-                    hq[g, b],
-                    slice(n0, n0 + P),
+                    hq[g],
+                    slice(kb * P, (kb + 1) * P),
                     ew[:, g, 2 * c0 : 2 * (c0 + width)].bitcast(E2M1X4),
                     es[:, g, c0 : c0 + width],
                     g == 0,
@@ -328,118 +365,150 @@ def tile_protected_adapter_gradients_s13_kernel(
                 )
             store(bank, out_0[kb * P : (kb + 1) * P, c0 : c0 + width], copy)
 
-        on_v, on_s = nc.vector.tensor_copy, nc.scalar.copy
-        halves = [(g, b, half) for g, b in by_scalar for half in range(2)]
+        load_small()
+        load_x(0, 2)
+        load_x(2, 2)
+        load_proj(0, 0)
+        load_proj(0, 1)
+        load_x(4, 4)
+        load_proj(1, 0)
+        load_proj(1, 1)
+        load_x(8, 4)
+        load_a()
+        load_x(12, 4)
+        constants()
+        load_second_stage()
 
-        def scalar_halves(count):
-            for half in halves[:count]:
-                h_inter_scalar(*half)
-                halves.remove(half)
+        used = []
 
-        def vector_pieces(count):
-            h_pieces(pieces[len(taken) : len(taken) + count])
+        def mm_bank():
+            used.append(0)
+            return MM_BANKS[(len(used) - 1) % len(MM_BANKS)]
+
+        def both(i):
+            for c in range(2):
+                h_mm(i, c, mm_bank())
+
+        def turn_pair(s):
+            for j in range(2):
+                x_turn(2 * s + j, TURN_BANK[s] + j)
 
         nc.scalar.activation(out=r32[:], in_=r16[:, :, :T4], func=COPY)
-        x_widen_sorted(0)
+        for kp in range(KP):
+            x_widen_sorted_pass(0, kp)
         x_widen_sorted(1)
-        x_widen(2)
-        x_widen(3)
-        for i in range(3):
-            x_turn(i)
-        pool_copy(proj_tile(0, 0)[:, : 2 * P], p_raw[0, 0][:, :, : 2 * P])
-        for q in (2, 3):
-            proj_inter(0, 0, on_s, (q,))
-        for i in (0, 1):
-            x_mult(i)
-        x_turn(3)
-        proj_quant(0, 0)
+        x_widen(2, 2)
+        for i in range(4):
+            x_turn(i, i)
+        s00, g00 = proj_part(0, 0, 0, CUT0), proj_part(0, 0, CUT0, HALF)
+        s01, v01 = proj_part(0, 1, 0, CUTV), proj_part(0, 1, CUTV, HALF)
+        s10, g10 = proj_part(1, 0, 0, CUT1), proj_part(1, 0, CUT1, HALF)
+        s11, g11 = proj_part(1, 1, 0, CUT2), proj_part(1, 1, CUT2, HALF)
+        weave(s00, "s")
+        weave(g00, "g", tag="weave_first")
+        x_mult(0)
+        x_mult(1)
+        weave(s01, "s", tag="weave_g")
+        weave(v01, "v")
+        x_widen(4, 2)
+        quant(s00)
         x_quant(0)
-        proj_inter(0, 1, on_v, (0, 1))
-        for q in (2, 3):
-            proj_inter(1, 0, on_s, (q,))
-        for q in range(2, 4):
-            proj_inter(0, 1, on_s, (q,))
-        proj_quant(0, 1)
-        x_quant(1)
-        pool_copy(proj_tile(1, 1)[:, : 2 * P], p_raw[1, 1][:, :, : 2 * P])
-        x_widen(4)
-        x_widen(5)
-        for q in (0, 1):
-            proj_inter(1, 0, on_s, (q,))
-        for q in (2, 3):
-            proj_inter(1, 1, on_s, (q,))
-        for i in (2, 3):
-            x_mult(i)
+        quant(g00)
+        quant(s01)
+        weave(g10, "g")
+        quant(v01)
+        x_mult(2)
+        x_mult(3)
+        x_widen(6, 2)
+        weave(s10, "s")
+        if TURN_FIRST:
+            turn_pair(2)
+        for kp in range(KP):
+            for i in range(2):
+                h_pass(i, 0, kp, 6 + i)
+        if not TURN_FIRST:
+            turn_pair(2)
+        x_widen(8, 2)
         for i in range(2):
-            h_mm(i, 0)
+            h_out(i, 0)
+        turn_pair(3)
+        quant(g10)
+        weave(g11, "g")
         x_quant(2)
-        x_quant(3)
-        proj_quant(1, 1)
-        proj_quant(1, 0)
+        x_mult(4)
+        x_mult(5)
+        weave(s11, "s")
+        h_mm(2, 0, 2)
+        h_mm(3, 0, 3)
+        turn_pair(4)
+        quant(s10)
+        quant(s11)
+        quant(g11)
+        weave(("a", 0), "g")
+        x_quant(4)
+        x_mult(6)
+        x_mult(7)
+        x_widen(10)
+        for i in range(4):
+            h_mm(i, 1, mm_bank())
+        both(4)
+        both(5)
+        x_widen_sorted(11)
+        if 5 in SORT_PAIRS:
+            x_sort(10, 1)
+        quant(("a", 0))
+        x_quant(6)
 
-        z_ready = []
-        for s in range(1, PAIRS):
-            now, ahead, far = [[i for i in (2 * k, 2 * k + 1) if i < TILES] for k in (s, s + 1, s + 2)]
-            for i in ahead:
-                x_turn(i)
-            if s <= KP:
-                pooled = pool_interleave(a_raw[:, s - 1])
-            elif ahead:
-                zg = z_ready.pop(0) if z_ready else None
-                if zg is None:
-                    g, b = pieces.pop(0)
-                    c, n0 = divmod(b * PIECE, HALF)
-                    pooled = pool_interleave(h_pl[g, c][:, :, n0 : n0 + PIECE])
-                else:
-                    pooled = pool_interleave(z_pl[zg][:])
-            for i in far[:1]:
-                if SORTED[s]:
-                    x_widen_sorted(i)
-                else:
-                    x_widen(i)
-            for i in far[1:]:
-                if SORTED[s] < 2:
-                    x_widen(i)
-            scalar_halves(S_STEP[s])
-            for i in ahead:
-                x_mult(i)
-            z_pairs = [k for k in range(PAIRS) if max(k, Z0 + k // 2) == s]
-            z_ready.extend(k // 2 for k in z_pairs if k % 2)
-            first_half = [(2, 0), (3, 0)] if s == 1 else [(i, 0) for i in now]
-            second_half = [(i, 1) for i in (range(4) if s == 1 else now)]
-            if ahead:
-                for i, c in first_half:
-                    h_mm(i, c)
-            for k in z_pairs:
-                z_mm(k)
-            for i, c in second_half if ahead else first_half + second_half:
-                h_mm(i, c)
-            for i in ahead:
-                x_quant(i)
-            for i in far[1:]:
-                if SORTED[s] == 2:
-                    x_widen_sorted(i)
-            if s <= KP:
-                aq[s - 1] = quantise("a%d" % s, pooled, R)
-            elif ahead and zg is None:
-                hq[g, b] = quantise("h%d%d" % (g, b), pooled, PIECE)
-            elif ahead:
-                zq[zg] = quantise("z%d" % zg, pooled, R)
-            vector_pieces(PER_STEP[s])
-        for g in z_ready:
-            z_inter(g)
-            vector_pieces(1)
-            z_quant(g)
-        scalar_halves(S_LATE)
+        pool_jobs = {4: ("a", 1), 5: ("h", 0, 0), 6: ("z", 0), 7: ("z", 1)}
+        for s in range(4, 8):
+            if s + 2 < 8:
+                x_widen(2 * s + 4)
+            if s + 1 < 8:
+                turn_pair(s + 1)
+            weave(pool_jobs[s], "g")
+            x_mult(2 * s)
+            x_mult(2 * s + 1)
+            both(2 * s - 2)
+            both(2 * s - 1)
+            if s + 2 < 8:
+                x_widen_sorted(2 * s + 5)
+                if s + 2 in SORT_PAIRS:
+                    x_sort(2 * s + 4, 1)
+            quant(pool_jobs[s])
+            for i in Z_AFTER.get(s, ()):
+                z_mm(i, mm_bank())
+            x_quant(2 * s)
+        for h in range(2):
+            z_mm_direct(2, h, 6 + h)
+        for h in range(2):
+            z_mm_direct(3, h, h)
+        weave(("h", 0, 1), "g")
+        for g in (2, 3):
+            for h in range(2):
+                z_out_direct(g, h)
+        quant(("z", 2))
+        quant(("z", 3))
+        quant(("h", 0, 1))
+        both(14)
+        both(15)
 
-        gb_mm(range(GB_OPEN))
-        for u in range(GB_OPEN, 2 * N // HALF):
-            scalar_halves(1)
-            gb_mm((u,))
-        h_pieces(sorted(pieces[len(taken) :], key=lambda piece: piece[1]))
-        for piece in taken[-1:] + by_scalar:
-            h_quant(*piece)
+        by_scalar = [("h", g, 3) for g in range(SCALAR_PIECES)]
+        rest = [("h", g, b) for b in range(4) for g in range(GROUPS) if ("h", g, b) not in woven and ("h", g, b) not in by_scalar]
+        last = None
+        for key in rest:
+            weave(key, "v")
+            if last:
+                quant(last)
+            last = key
+        quant(last)
+        halves = [(key, h) for key in by_scalar for h in range(2)]
+        for u in range(2 * N // HALF):
+            gb_mm((u,), ((u + 4) % BANKS,))
+            for key, h in halves[u : u + 1]:
+                weave(key, "s", part=(h * P, (h + 1) * P))
+                if h:
+                    quant(key)
         for kb in range(K // P - 1):
-            ga_mm(kb)
-        ga_mm(K // P - 1, 0, P)
-        ga_mm(K // P - 1, P, P, nc.vector.tensor_copy)
+            ga_mm(kb, (kb + 4) % BANKS)
+        ga_mm(K // P - 1, 3, 0, P)
+        ga_mm(K // P - 1, 4, P, P, on_v)

@@ -28,22 +28,17 @@ HALF = 512
 PIECE = 256
 BANKS = 8
 
-WEAVE_BUFS = {"weave_v": 3, "weave_s": 4, "weave_g": 1, "weave_first": 1}
-XBF_BUFS = {1: 2, 2: 2}
+WEAVE_BUFS = {"weave_v": 3, "weave_s": 3, "weave_g": 1, "weave_first": 1}
+XBF_BUFS = {1: 3, 2: 2}
 SORTED_BUFS = 2
-SORT_BUFS = 2
-CUT0 = 256
-CUTV = 384
-CUT1 = 256
-CUT2 = 128
-TURN_FIRST = 1
-SORT_PAIRS = (5, 6, 7)
-Z_AFTER = {4: (0, 2, 4), 5: (6,)}
-RES_BUFS = {HALF: 4, R: 7, P: 2}
+RES_BUFS = {HALF: 4, R: 6, P: 2}
 MM_BANKS = (4, 5, 2, 3)
 TURN_BANK = {2: 4, 3: 0, 4: 6, 5: 0, 6: 6, 7: 0}
 SCALAR_PIECES = 3
-SORT_FROM = 4
+CUT0 = 256
+CUTV = 128
+CUT1 = 256
+CUT2 = 128
 
 
 def tile_protected_adapter_gradients_s13_kernel(
@@ -187,7 +182,6 @@ def tile_protected_adapter_gradients_s13_kernel(
             return key
 
         x_words = {}
-        x_wide = {}
         x_bank = {}
         x_gr = {}
         xq = {}
@@ -195,25 +189,12 @@ def tile_protected_adapter_gradients_s13_kernel(
         def x_widen(i, count=1):
             w = ring.tile([P, count * K], BF16, name="x_bf%d" % count, bufs=XBF_BUFS[count])
             nc.scalar.copy(out=w[:], in_=x_bytes_of(i, count))
-            x_wide[i] = w[:]
             words = w[:].bitcast(F32)
             for j in range(count):
                 for kp in range(KP):
                     for u in range(2):
                         w0 = 2 * P * (KP * j + kp)
                         x_words[i + j, kp, u] = words[:, w0 + u : w0 + 2 * P : 2]
-
-        def x_sort(i, count):
-            w = ring.tile([P, 2, count * K // 2], BF16, name="x_sort%d" % count, bufs=SORT_BUFS)
-            nc.vector.tensor_copy(
-                out=w[:].rearrange("p u (w e) -> p u w e", e=2),
-                in_=x_wide[i].rearrange("p (w u e) -> p u w e", u=2, e=2),
-            )
-            for j in range(count):
-                for kp in range(KP):
-                    for u in range(2):
-                        w0 = P * (KP * j + kp)
-                        x_words[i + j, kp, u] = w[:, u].bitcast(F32)[:, w0 : w0 + P]
 
         def x_widen_sorted(i):
             w = ring.tile([P, K], BF16, name="x_sorted", bufs=SORTED_BUFS)
@@ -229,17 +210,11 @@ def tile_protected_adapter_gradients_s13_kernel(
                 for u in range(2):
                     x_words[i, kp, u] = words[:, (u * KP + kp) * P : (u * KP + kp + 1) * P]
 
-        def x_widen_sorted_pass(i, kp):
-            w = keep.tile([P, PASS], BF16, name="x_first%d" % kp)
-            nc.vector.tensor_scalar(
-                out=w[:].rearrange("p (u w e) -> p w u e", u=2, e=2),
-                in0=x_bytes_of(i, 1)[:, kp * PASS : (kp + 1) * PASS],
-                scalar1=one[:],
-                scalar2=None,
-                op0=MULT,
-            )
+        def x_widen_vector(i, kp):
+            w = keep.tile([P, PASS], BF16, name="x_head%d%d" % (i, kp))
+            nc.vector.tensor_copy(out=w[:], in_=x_bytes_of(i, 1)[:, kp * PASS : (kp + 1) * PASS])
             for u in range(2):
-                x_words[i, kp, u] = w[:].bitcast(F32)[:, u * P : (u + 1) * P]
+                x_words[i, kp, u] = w[:].bitcast(F32)[:, u::2]
 
         def x_turn(i, b):
             x_bank[i] = bank_tile(b, [P, 2, KP, P])
@@ -370,10 +345,12 @@ def tile_protected_adapter_gradients_s13_kernel(
         load_x(2, 2)
         load_proj(0, 0)
         load_proj(0, 1)
-        load_x(4, 4)
+        load_x(4, 2)
+        load_x(6, 2)
         load_proj(1, 0)
+        load_x(8, 2)
         load_proj(1, 1)
-        load_x(8, 4)
+        load_x(10, 2)
         load_a()
         load_x(12, 4)
         constants()
@@ -393,10 +370,15 @@ def tile_protected_adapter_gradients_s13_kernel(
             for j in range(2):
                 x_turn(2 * s + j, TURN_BANK[s] + j)
 
+        def first_pair(c, banks):
+            for kp in range(KP):
+                for i in range(2):
+                    h_pass(i, c, kp, banks[i])
+
         nc.scalar.activation(out=r32[:], in_=r16[:, :, :T4], func=COPY)
-        for kp in range(KP):
-            x_widen_sorted_pass(0, kp)
-        x_widen_sorted(1)
+        for i in range(2):
+            for kp in range(KP):
+                x_widen_vector(i, kp)
         x_widen(2, 2)
         for i in range(4):
             x_turn(i, i)
@@ -410,7 +392,8 @@ def tile_protected_adapter_gradients_s13_kernel(
         x_mult(1)
         weave(s01, "s", tag="weave_g")
         weave(v01, "v")
-        x_widen(4, 2)
+        x_widen(4)
+        x_widen(5)
         quant(s00)
         x_quant(0)
         quant(g00)
@@ -421,14 +404,10 @@ def tile_protected_adapter_gradients_s13_kernel(
         x_mult(3)
         x_widen(6, 2)
         weave(s10, "s")
-        if TURN_FIRST:
-            turn_pair(2)
-        for kp in range(KP):
-            for i in range(2):
-                h_pass(i, 0, kp, 6 + i)
-        if not TURN_FIRST:
-            turn_pair(2)
+        turn_pair(2)
+        first_pair(0, (6, 7))
         x_widen(8, 2)
+        weave(s11, "s")
         for i in range(2):
             h_out(i, 0)
         turn_pair(3)
@@ -437,7 +416,6 @@ def tile_protected_adapter_gradients_s13_kernel(
         x_quant(2)
         x_mult(4)
         x_mult(5)
-        weave(s11, "s")
         h_mm(2, 0, 2)
         h_mm(3, 0, 3)
         turn_pair(4)
@@ -449,13 +427,14 @@ def tile_protected_adapter_gradients_s13_kernel(
         x_mult(6)
         x_mult(7)
         x_widen(10)
-        for i in range(4):
+        first_pair(1, (mm_bank(), mm_bank()))
+        for i in range(2):
+            h_out(i, 1)
+        for i in range(2, 4):
             h_mm(i, 1, mm_bank())
         both(4)
         both(5)
         x_widen_sorted(11)
-        if 5 in SORT_PAIRS:
-            x_sort(10, 1)
         quant(("a", 0))
         x_quant(6)
 
@@ -468,15 +447,17 @@ def tile_protected_adapter_gradients_s13_kernel(
             weave(pool_jobs[s], "g")
             x_mult(2 * s)
             x_mult(2 * s + 1)
+            if s == 5:
+                z_mm(0, mm_bank())
+                z_mm(2, mm_bank())
             both(2 * s - 2)
             both(2 * s - 1)
             if s + 2 < 8:
                 x_widen_sorted(2 * s + 5)
-                if s + 2 in SORT_PAIRS:
-                    x_sort(2 * s + 4, 1)
             quant(pool_jobs[s])
-            for i in Z_AFTER.get(s, ()):
-                z_mm(i, mm_bank())
+            if s == 5:
+                z_mm(4, mm_bank())
+                z_mm(6, mm_bank())
             x_quant(2 * s)
         for h in range(2):
             z_mm_direct(2, h, 6 + h)

@@ -35,10 +35,13 @@ RES_BUFS = {HALF: 4, R: 6, P: 2}
 MM_BANKS = (4, 5, 2, 3)
 TURN_BANK = {2: 4, 3: 0, 4: 6, 5: 0, 6: 6, 7: 0}
 SCALAR_PIECES = 3
-CUT0 = 256
+CUT0 = 384
 CUTV = 128
 CUT1 = 256
-CUT2 = 128
+CUT2 = 256
+SPREAD = 1
+SORT_PAIRS = (5, 7)
+SORT_BUFS = 1
 
 
 def tile_protected_adapter_gradients_s13_kernel(
@@ -182,6 +185,7 @@ def tile_protected_adapter_gradients_s13_kernel(
             return key
 
         x_words = {}
+        x_wide = {}
         x_bank = {}
         x_gr = {}
         xq = {}
@@ -189,12 +193,25 @@ def tile_protected_adapter_gradients_s13_kernel(
         def x_widen(i, count=1):
             w = ring.tile([P, count * K], BF16, name="x_bf%d" % count, bufs=XBF_BUFS[count])
             nc.scalar.copy(out=w[:], in_=x_bytes_of(i, count))
+            x_wide[i] = w[:]
             words = w[:].bitcast(F32)
             for j in range(count):
                 for kp in range(KP):
                     for u in range(2):
                         w0 = 2 * P * (KP * j + kp)
                         x_words[i + j, kp, u] = words[:, w0 + u : w0 + 2 * P : 2]
+
+        def x_sort(i, count):
+            w = ring.tile([P, 2, count * K // 2], BF16, name="x_sort%d" % count, bufs=SORT_BUFS)
+            nc.vector.tensor_copy(
+                out=w[:].rearrange("p u (w e) -> p u w e", e=2),
+                in_=x_wide[i].rearrange("p (w u e) -> p u w e", u=2, e=2),
+            )
+            for j in range(count):
+                for kp in range(KP):
+                    for u in range(2):
+                        w0 = P * (KP * j + kp)
+                        x_words[i + j, kp, u] = w[:, u].bitcast(F32)[:, w0 : w0 + P]
 
         def x_widen_sorted(i):
             w = ring.tile([P, K], BF16, name="x_sorted", bufs=SORTED_BUFS)
@@ -261,7 +278,8 @@ def tile_protected_adapter_gradients_s13_kernel(
             g, t = divmod(i, T4)
             bank = h_bank[i, c]
             if (g, c) not in h_pl:
-                h_pl[g, c] = keep.tile([P, T4, HALF], BF16, name="h_pl%d%d" % (g, c))
+                tag = "h_pl%d%d" % (g, c) if g < 2 else "p_raw%d%d" % (g - 2, c)
+                h_pl[g, c] = keep.tile([P, T4, HALF], BF16, name=tag)
                 for h in range(2):
                     src["h", g, 2 * c + h] = h_pl[g, c][:, :, h * PIECE : (h + 1) * PIECE]
                     dst["h", g, 2 * c + h] = (hq[g], (2 * c + h) * PIECE)
@@ -405,12 +423,16 @@ def tile_protected_adapter_gradients_s13_kernel(
         x_widen(6, 2)
         weave(s10, "s")
         turn_pair(2)
-        first_pair(0, (6, 7))
+        for kp in range(KP):
+            for i in range(2):
+                h_pass(i, 0, kp, 6 + i)
+            if kp == 1 - SPREAD:
+                turn_pair(3)
         x_widen(8, 2)
         weave(s11, "s")
         for i in range(2):
             h_out(i, 0)
-        turn_pair(3)
+        quant(s10)
         quant(g10)
         weave(g11, "g")
         x_quant(2)
@@ -419,7 +441,6 @@ def tile_protected_adapter_gradients_s13_kernel(
         h_mm(2, 0, 2)
         h_mm(3, 0, 3)
         turn_pair(4)
-        quant(s10)
         quant(s11)
         quant(g11)
         weave(("a", 0), "g")
@@ -434,6 +455,8 @@ def tile_protected_adapter_gradients_s13_kernel(
             h_mm(i, 1, mm_bank())
         both(4)
         both(5)
+        if 5 in SORT_PAIRS:
+            x_sort(10, 1)
         x_widen_sorted(11)
         quant(("a", 0))
         x_quant(6)
@@ -452,6 +475,8 @@ def tile_protected_adapter_gradients_s13_kernel(
                 z_mm(2, mm_bank())
             both(2 * s - 2)
             both(2 * s - 1)
+            if s + 2 in SORT_PAIRS:
+                x_sort(2 * s + 4, 1)
             if s + 2 < 8:
                 x_widen_sorted(2 * s + 5)
             quant(pool_jobs[s])

@@ -28,20 +28,22 @@ HALF = 512
 PIECE = 256
 BANKS = 8
 
-WEAVE_BUFS = {"weave_v": 3, "weave_s": 3, "weave_g": 1, "weave_first": 1}
+WEAVE_BUFS = {"weave_v": 3, "weave_s": 3, "weave_g": 1, "panel": 1}
 XBF_BUFS = {1: 3, 2: 2}
 SORTED_BUFS = 2
+SORT_BUFS = 2
 RES_BUFS = {HALF: 4, R: 6, P: 2}
 MM_BANKS = (4, 5, 2, 3)
 TURN_BANK = {2: 4, 3: 0, 4: 6, 5: 0, 6: 6, 7: 0}
-SCALAR_PIECES = 3
-CUT0 = 384
-CUTV = 128
+CUT0 = 256
+CUTV = 256
 CUT1 = 256
 CUT2 = 256
-SPREAD = 1
-SORT_PAIRS = (5, 7)
-SORT_BUFS = 1
+HOW = {10: "s", 11: "w", 12: "s", 13: "w", 14: "s", 15: "w"}
+POOL_COLS = 256
+SCALAR_COLS = 768
+EARLY = {}
+SPLIT_FIRST = 0
 
 
 def tile_protected_adapter_gradients_s13_kernel(
@@ -86,6 +88,7 @@ def tile_protected_adapter_gradients_s13_kernel(
         r16 = keep.tile([P, GROUPS, 4 * T4], BF16, name="r16")
         sc_col = keep.tile([P, KP, 2 * T4], F32, name="sc_col")
         ident = keep.tile([P, P], F32, name="ident")
+        half = keep.tile([P, 1], F32, name="half")
         one = keep.tile([P, 1], F32, name="one")
         es = keep.tile([P, GROUPS, R], U8, name="es", align_bytes=256)
         ds = keep.tile([P, GROUPS, N], U8, name="ds", align_bytes=256)
@@ -98,9 +101,10 @@ def tile_protected_adapter_gradients_s13_kernel(
             nc.scalar.dma_start(out=r16[:, :, :T4], in_=r.rearrange("(g p t) -> p g t", p=P, t=T4))
 
         def constants():
+            nc.vector.memset(half[:], 0.5)
+            nc.scalar.activation(out=one[:], in_=half[:], func=COPY, scale=2.0)
             nc.vector.memset(ident[:], 0.0)
             make_identity(nc, ident[:], nomemset=True)
-            nc.vector.memset(one[:], 1.0)
             nc.vector.memset(es[:].rearrange("p g n -> p (g n)").bitcast(I32), 0)
             nc.vector.memset(ds[:].rearrange("p g n -> p (g n)").bitcast(I32), 0)
 
@@ -178,10 +182,17 @@ def tile_protected_adapter_gradients_s13_kernel(
         hq = {g: mx_tiles("h%d" % g, K) for g in range(GROUPS)}
         zq = {g: mx_tiles("z%d" % g, R) for g in range(GROUPS)}
 
-        def proj_part(c, kp, lo, hi):
-            key = ("p", c, kp, lo)
-            src[key] = p_raw[c, kp][:, :, lo:hi]
-            dst[key] = (pq[c, kp], lo)
+        def proj_panel(c, kp):
+            key = ("p", c, kp)
+            src[key] = p_raw[c, kp][:]
+            dst[key] = (pq[c, kp], 0)
+            return key
+
+        def h_piece(g, lo, hi):
+            c, n0 = divmod(lo, HALF)
+            key = ("h", g, lo, hi)
+            src[key] = h_pl[g, c][:, :, n0 : n0 + hi - lo]
+            dst[key] = (hq[g], lo)
             return key
 
         x_words = {}
@@ -213,6 +224,12 @@ def tile_protected_adapter_gradients_s13_kernel(
                         w0 = P * (KP * j + kp)
                         x_words[i + j, kp, u] = w[:, u].bitcast(F32)[:, w0 : w0 + P]
 
+        def x_widen_pass(i, kp):
+            w = keep.tile([P, PASS], BF16, name="x_first%d" % kp)
+            nc.scalar.copy(out=w[:], in_=x_bytes_of(i, 1)[:, kp * PASS : (kp + 1) * PASS])
+            for u in range(2):
+                x_words[i, kp, u] = w[:].bitcast(F32)[:, u::2]
+
         def x_widen_sorted(i):
             w = ring.tile([P, K], BF16, name="x_sorted", bufs=SORTED_BUFS)
             nc.vector.tensor_scalar(
@@ -226,12 +243,6 @@ def tile_protected_adapter_gradients_s13_kernel(
             for kp in range(KP):
                 for u in range(2):
                     x_words[i, kp, u] = words[:, (u * KP + kp) * P : (u * KP + kp + 1) * P]
-
-        def x_widen_vector(i, kp):
-            w = keep.tile([P, PASS], BF16, name="x_head%d%d" % (i, kp))
-            nc.vector.tensor_copy(out=w[:], in_=x_bytes_of(i, 1)[:, kp * PASS : (kp + 1) * PASS])
-            for u in range(2):
-                x_words[i, kp, u] = w[:].bitcast(F32)[:, u::2]
 
         def x_turn(i, b):
             x_bank[i] = bank_tile(b, [P, 2, KP, P])
@@ -280,9 +291,6 @@ def tile_protected_adapter_gradients_s13_kernel(
             if (g, c) not in h_pl:
                 tag = "h_pl%d%d" % (g, c) if g < 2 else "p_raw%d%d" % (g - 2, c)
                 h_pl[g, c] = keep.tile([P, T4, HALF], BF16, name=tag)
-                for h in range(2):
-                    src["h", g, 2 * c + h] = h_pl[g, c][:, :, h * PIECE : (h + 1) * PIECE]
-                    dst["h", g, 2 * c + h] = (hq[g], (2 * c + h) * PIECE)
             nc.scalar.activation(out=h_pl[g, c][:, t, :], in_=bank[:], func=COPY, scale=r32[:, g, t : t + 1])
 
         def z_mm(i, b):
@@ -359,7 +367,11 @@ def tile_protected_adapter_gradients_s13_kernel(
             store(bank, out_0[kb * P : (kb + 1) * P, c0 : c0 + width], copy)
 
         load_small()
-        load_x(0, 2)
+        if SPLIT_FIRST:
+            load_x(0, 1)
+            load_x(1, 1)
+        else:
+            load_x(0, 2)
         load_x(2, 2)
         load_proj(0, 0)
         load_proj(0, 1)
@@ -393,61 +405,68 @@ def tile_protected_adapter_gradients_s13_kernel(
                 for i in range(2):
                     h_pass(i, c, kp, banks[i])
 
-        nc.scalar.activation(out=r32[:], in_=r16[:, :, :T4], func=COPY)
-        for i in range(2):
-            for kp in range(KP):
-                x_widen_vector(i, kp)
+
+        def widen_on_scalar(s):
+            mine = [i for i in (2 * s, 2 * s + 1) if HOW[i] != "w"]
+            if mine:
+                x_widen(mine[0], len(mine))
+
+        def widen_on_vector(s):
+            if HOW[2 * s] == HOW[2 * s + 1] == "ss":
+                x_sort(2 * s, 2)
+            elif HOW[2 * s] == "ss":
+                x_sort(2 * s, 1)
+            for i in (2 * s, 2 * s + 1):
+                if HOW[i] == "w":
+                    x_widen_sorted(i)
+
+        for kp in range(KP):
+            x_widen_pass(0, kp)
+        x_widen_sorted(1)
+        nc.vector.tensor_copy(out=r32[:], in_=r16[:, :, :T4])
         x_widen(2, 2)
         for i in range(4):
             x_turn(i, i)
-        s00, g00 = proj_part(0, 0, 0, CUT0), proj_part(0, 0, CUT0, HALF)
-        s01, v01 = proj_part(0, 1, 0, CUTV), proj_part(0, 1, CUTV, HALF)
-        s10, g10 = proj_part(1, 0, 0, CUT1), proj_part(1, 0, CUT1, HALF)
-        s11, g11 = proj_part(1, 1, 0, CUT2), proj_part(1, 1, CUT2, HALF)
-        weave(s00, "s")
-        weave(g00, "g", tag="weave_first")
+        p00, p01, p10, p11 = [proj_panel(c, kp) for c in range(2) for kp in range(KP)]
+        weave(p00, "s", tag="panel", part=(0, CUT0))
+        weave(p00, "g", part=(CUT0, HALF))
         x_mult(0)
         x_mult(1)
-        weave(s01, "s", tag="weave_g")
-        weave(v01, "v")
+        weave(p01, "s", tag="weave_g", part=(0, CUTV))
+        weave(p01, "v", part=(CUTV, HALF))
         x_widen(4)
         x_widen(5)
-        quant(s00)
+        quant(p00)
+        quant(p01)
+        weave(p10, "g", part=(CUT1, HALF))
         x_quant(0)
-        quant(g00)
-        quant(s01)
-        weave(g10, "g")
-        quant(v01)
         x_mult(2)
         x_mult(3)
         x_widen(6, 2)
-        weave(s10, "s")
+        weave(p10, "s", part=(0, CUT1))
         turn_pair(2)
         for kp in range(KP):
             for i in range(2):
                 h_pass(i, 0, kp, 6 + i)
-            if kp == 1 - SPREAD:
-                turn_pair(3)
+        turn_pair(3)
         x_widen(8, 2)
-        weave(s11, "s")
         for i in range(2):
             h_out(i, 0)
-        quant(s10)
-        quant(g10)
-        weave(g11, "g")
+        quant(p10)
+        weave(p11, "g", part=(CUT2, HALF))
+        weave(p11, "s", part=(0, CUT2))
         x_quant(2)
         x_mult(4)
         x_mult(5)
         h_mm(2, 0, 2)
         h_mm(3, 0, 3)
         turn_pair(4)
-        quant(s11)
-        quant(g11)
+        quant(p11)
         weave(("a", 0), "g")
         x_quant(4)
         x_mult(6)
         x_mult(7)
-        x_widen(10)
+        widen_on_scalar(5)
         first_pair(1, (mm_bank(), mm_bank()))
         for i in range(2):
             h_out(i, 1)
@@ -455,30 +474,32 @@ def tile_protected_adapter_gradients_s13_kernel(
             h_mm(i, 1, mm_bank())
         both(4)
         both(5)
-        if 5 in SORT_PAIRS:
-            x_sort(10, 1)
-        x_widen_sorted(11)
+        widen_on_vector(5)
         quant(("a", 0))
         x_quant(6)
 
-        pool_jobs = {4: ("a", 1), 5: ("h", 0, 0), 6: ("z", 0), 7: ("z", 1)}
+        pool_jobs = {4: ("a", 1), 5: h_piece(0, 0, POOL_COLS), 7: ("z", 0)}
+        early = []
         for s in range(4, 8):
             if s + 2 < 8:
-                x_widen(2 * s + 4)
+                widen_on_scalar(s + 2)
             if s + 1 < 8:
                 turn_pair(s + 1)
-            weave(pool_jobs[s], "g")
-            x_mult(2 * s)
-            x_mult(2 * s + 1)
             if s == 5:
                 z_mm(0, mm_bank())
                 z_mm(2, mm_bank())
+            if s == 6:
+                pool_jobs[s] = h_piece(1, 0, POOL_COLS)
+            weave(pool_jobs[s], "g")
+            x_mult(2 * s)
+            x_mult(2 * s + 1)
             both(2 * s - 2)
             both(2 * s - 1)
-            if s + 2 in SORT_PAIRS:
-                x_sort(2 * s + 4, 1)
             if s + 2 < 8:
-                x_widen_sorted(2 * s + 5)
+                widen_on_vector(s + 2)
+            for g, lo, hi in EARLY.get(s, ()):
+                early.append(h_piece(g, lo, hi))
+                weave(early[-1], "v")
             quant(pool_jobs[s])
             if s == 5:
                 z_mm(4, mm_bank())
@@ -488,20 +509,22 @@ def tile_protected_adapter_gradients_s13_kernel(
             z_mm_direct(2, h, 6 + h)
         for h in range(2):
             z_mm_direct(3, h, h)
-        weave(("h", 0, 1), "g")
+        weave(("z", 1), "g")
         for g in (2, 3):
             for h in range(2):
                 z_out_direct(g, h)
-        quant(("z", 2))
-        quant(("z", 3))
-        quant(("h", 0, 1))
+        for g in (1, 2, 3):
+            quant(("z", g))
+        for key in early[:-1]:
+            quant(key)
+        last = early[-1] if early else None
         both(14)
         both(15)
 
-        by_scalar = [("h", g, 3) for g in range(SCALAR_PIECES)]
-        rest = [("h", g, b) for b in range(4) for g in range(GROUPS) if ("h", g, b) not in woven and ("h", g, b) not in by_scalar]
-        last = None
-        for key in rest:
+        by_scalar = [h_piece(g, K - PIECE, K) for g in range(SCALAR_COLS // PIECE)]
+        rest = [h_piece(g, POOL_COLS if g < 2 else 0, HALF) for g in range(GROUPS)]
+        rest = rest + [h_piece(g, HALF, K - PIECE if g < len(by_scalar) else K) for g in range(GROUPS)]
+        for key in [k for k in rest if k not in early]:
             weave(key, "v")
             if last:
                 quant(last)

@@ -28,7 +28,7 @@ HALF = 512
 PIECE = 256
 BANKS = 8
 
-WEAVE_BUFS = {"weave_v": 3, "weave_s": 3, "weave_g": 1, "panel": 1}
+WEAVE_BUFS = {"weave_v": 4, "weave_s": 3, "weave_g": 1, "panel": 1}
 XBF_BUFS = {1: 3, 2: 2}
 SORTED_BUFS = 2
 SORT_BUFS = 2
@@ -39,11 +39,14 @@ CUT0 = 256
 CUTV = 256
 CUT1 = 256
 CUT2 = 256
-HOW = {10: "s", 11: "w", 12: "s", 13: "w", 14: "s", 15: "w"}
+HOW = {8: "s", 9: "s", 10: "ss", 11: "w", 12: "s", 13: "w", 14: "ss", 15: "w"}
 POOL_COLS = 256
-SCALAR_COLS = 768
+SCALAR_COLS = 512
 EARLY = {}
 SPLIT_FIRST = 0
+Z_DIRECT = 0
+GB_OPEN = 2
+SPLIT_LAST = 1
 
 
 def tile_protected_adapter_gradients_s13_kernel(
@@ -386,11 +389,11 @@ def tile_protected_adapter_gradients_s13_kernel(
         constants()
         load_second_stage()
 
-        used = []
+        banks = list(MM_BANKS)
 
         def mm_bank():
-            used.append(0)
-            return MM_BANKS[(len(used) - 1) % len(MM_BANKS)]
+            banks.append(banks.pop(0))
+            return banks[-1]
 
         def both(i):
             for c in range(2):
@@ -449,9 +452,10 @@ def tile_protected_adapter_gradients_s13_kernel(
             for i in range(2):
                 h_pass(i, 0, kp, 6 + i)
         turn_pair(3)
-        x_widen(8, 2)
+        widen_on_scalar(4)
         for i in range(2):
             h_out(i, 0)
+        widen_on_vector(4)
         quant(p10)
         weave(p11, "g", part=(CUT2, HALF))
         weave(p11, "s", part=(0, CUT2))
@@ -479,6 +483,8 @@ def tile_protected_adapter_gradients_s13_kernel(
         x_quant(6)
 
         pool_jobs = {4: ("a", 1), 5: h_piece(0, 0, POOL_COLS), 7: ("z", 0)}
+        if not Z_DIRECT:
+            pool_jobs.update({6: ("z", 0), 7: ("z", 1)})
         early = []
         for s in range(4, 8):
             if s + 2 < 8:
@@ -488,11 +494,15 @@ def tile_protected_adapter_gradients_s13_kernel(
             if s == 5:
                 z_mm(0, mm_bank())
                 z_mm(2, mm_bank())
-            if s == 6:
+            if s == 6 and Z_DIRECT:
                 pool_jobs[s] = h_piece(1, 0, POOL_COLS)
             weave(pool_jobs[s], "g")
             x_mult(2 * s)
             x_mult(2 * s + 1)
+            if s == 7 and not Z_DIRECT:
+                banks[:0] = [6, 7]
+                z_mm(8, mm_bank())
+                z_mm(10, mm_bank())
             both(2 * s - 2)
             both(2 * s - 1)
             if s + 2 < 8:
@@ -505,24 +515,36 @@ def tile_protected_adapter_gradients_s13_kernel(
                 z_mm(4, mm_bank())
                 z_mm(6, mm_bank())
             x_quant(2 * s)
-        for h in range(2):
-            z_mm_direct(2, h, 6 + h)
-        for h in range(2):
-            z_mm_direct(3, h, h)
-        weave(("z", 1), "g")
-        for g in (2, 3):
+        if Z_DIRECT:
             for h in range(2):
-                z_out_direct(g, h)
-        for g in (1, 2, 3):
-            quant(("z", g))
-        for key in early[:-1]:
-            quant(key)
-        last = early[-1] if early else None
+                z_mm_direct(2, h, 6 + h)
+            for h in range(2):
+                z_mm_direct(3, h, h)
+            weave(("z", 1), "g")
+            for g in (2, 3):
+                for h in range(2):
+                    z_out_direct(g, h)
+            for g in (1, 2, 3):
+                quant(("z", g))
+            last = None
+        else:
+            banks[:0] = [0, 1]
+            z_mm(12, mm_bank())
+            z_mm(14, mm_bank())
+            early = [h_piece(1, 0, HALF), h_piece(0, POOL_COLS, HALF)]
+            weave(("z", 2), "v")
+            weave(early[0], "v")
+            quant(("z", 2))
+            weave(early[1], "v")
+            weave(("z", 3), "v")
+            quant(early[1])
+            quant(("z", 3))
+            last = early[0]
         both(14)
         both(15)
 
         by_scalar = [h_piece(g, K - PIECE, K) for g in range(SCALAR_COLS // PIECE)]
-        rest = [h_piece(g, POOL_COLS if g < 2 else 0, HALF) for g in range(GROUPS)]
+        rest = [h_piece(g, POOL_COLS if g < 1 + bool(Z_DIRECT) else 0, HALF) for g in range(GROUPS)]
         rest = rest + [h_piece(g, HALF, K - PIECE if g < len(by_scalar) else K) for g in range(GROUPS)]
         for key in [k for k in rest if k not in early]:
             weave(key, "v")
@@ -531,13 +553,19 @@ def tile_protected_adapter_gradients_s13_kernel(
             last = key
         quant(last)
         halves = [(key, h) for key in by_scalar for h in range(2)]
+        banks[:] = banks + [b for b in range(BANKS) if b not in banks]
+        gb_mm(range(GB_OPEN), [mm_bank() for u in range(GB_OPEN)])
         for u in range(2 * N // HALF):
-            gb_mm((u,), ((u + 4) % BANKS,))
+            if u >= GB_OPEN:
+                gb_mm((u,), (mm_bank(),))
             for key, h in halves[u : u + 1]:
                 weave(key, "s", part=(h * P, (h + 1) * P))
                 if h:
                     quant(key)
         for kb in range(K // P - 1):
-            ga_mm(kb, (kb + 4) % BANKS)
-        ga_mm(K // P - 1, 3, 0, P)
-        ga_mm(K // P - 1, 4, P, P, on_v)
+            ga_mm(kb, mm_bank())
+        if SPLIT_LAST:
+            ga_mm(K // P - 1, mm_bank(), 0, P)
+            ga_mm(K // P - 1, mm_bank(), P, P, on_v)
+        else:
+            ga_mm(K // P - 1, mm_bank(), copy=on_v)

@@ -36,7 +36,7 @@ RES_BUFS = {HALF: 4, R: 6, P: 2}
 MM_BANKS = (4, 5, 2, 3)
 TURN_BANK = {2: 4, 3: 0, 4: 6, 5: 0, 6: 6, 7: 0}
 CUT0 = 256
-CUTV = 256
+CUTV = 128
 CUT1 = 256
 CUT2 = 256
 HOW = {8: "s", 9: "s", 10: "ss", 11: "w", 12: "s", 13: "w", 14: "ss", 15: "w"}
@@ -47,6 +47,9 @@ SPLIT_FIRST = 0
 Z_DIRECT = 0
 GB_OPEN = 2
 SPLIT_LAST = 1
+SPLIT_END = 1
+OUT_FIRST = 2
+ORDER = 1
 
 
 def tile_protected_adapter_gradients_s13_kernel(
@@ -99,9 +102,11 @@ def tile_protected_adapter_gradients_s13_kernel(
         ew = keep.tile([P, GROUPS, 2 * R], U8, name="ew", align_bytes=256)
         dw = keep.tile([P, GROUPS, 2 * N], U8, name="dw", align_bytes=256)
 
-        def load_small():
-            nc.scalar.dma_start(out=sc_col[:, :, :T4], in_=x_scale.rearrange("o (a p j) -> p (o a) j", p=P, j=T4))
-            nc.scalar.dma_start(out=r16[:, :, :T4], in_=r.rearrange("(g p t) -> p g t", p=P, t=T4))
+        def load_scales():
+            nc.sync.dma_start(out=sc_col[:, :, :T4], in_=x_scale.rearrange("o (a p j) -> p (o a) j", p=P, j=T4))
+
+        def load_r():
+            nc.sync.dma_start(out=r16[:, :, :T4], in_=r.rearrange("(g p t) -> p g t", p=P, t=T4))
 
         def constants():
             nc.vector.memset(half[:], 0.5)
@@ -369,17 +374,23 @@ def tile_protected_adapter_gradients_s13_kernel(
                 )
             store(bank, out_0[kb * P : (kb + 1) * P, c0 : c0 + width], copy)
 
-        load_small()
-        if SPLIT_FIRST:
-            load_x(0, 1)
-            load_x(1, 1)
+        load_x(0, 1)
+        load_x(1, 1)
+        load_scales()
+        if ORDER == 0:
+            load_x(2, 2)
+            load_proj(0, 0)
+        elif ORDER == 1:
+            load_proj(0, 0)
+            load_x(2, 2)
         else:
-            load_x(0, 2)
-        load_x(2, 2)
-        load_proj(0, 0)
+            load_x(2, 1)
+            load_proj(0, 0)
+            load_x(3, 1)
         load_proj(0, 1)
         load_x(4, 2)
         load_x(6, 2)
+        load_r()
         load_proj(1, 0)
         load_x(8, 2)
         load_proj(1, 1)
@@ -426,13 +437,21 @@ def tile_protected_adapter_gradients_s13_kernel(
         for kp in range(KP):
             x_widen_pass(0, kp)
         x_widen_sorted(1)
-        nc.vector.tensor_copy(out=r32[:], in_=r16[:, :, :T4])
-        x_widen(2, 2)
-        for i in range(4):
+        if ORDER == 0:
+            x_widen(2, 2)
+        elif ORDER == 2:
+            x_widen(2)
+        for i in range((4, 2, 3)[ORDER]):
             x_turn(i, i)
         p00, p01, p10, p11 = [proj_panel(c, kp) for c in range(2) for kp in range(KP)]
         weave(p00, "s", tag="panel", part=(0, CUT0))
         weave(p00, "g", part=(CUT0, HALF))
+        if ORDER == 1:
+            x_widen(2, 2)
+        elif ORDER == 2:
+            x_widen(3)
+        for i in range((4, 2, 3)[ORDER], 4):
+            x_turn(i, i)
         x_mult(0)
         x_mult(1)
         weave(p01, "s", tag="weave_g", part=(0, CUTV))
@@ -445,6 +464,7 @@ def tile_protected_adapter_gradients_s13_kernel(
         x_quant(0)
         x_mult(2)
         x_mult(3)
+        nc.vector.tensor_copy(out=r32[:], in_=r16[:, :, :T4])
         x_widen(6, 2)
         weave(p10, "s", part=(0, CUT1))
         turn_pair(2)
@@ -453,12 +473,14 @@ def tile_protected_adapter_gradients_s13_kernel(
                 h_pass(i, 0, kp, 6 + i)
         turn_pair(3)
         widen_on_scalar(4)
-        for i in range(2):
+        for i in range(OUT_FIRST):
             h_out(i, 0)
         widen_on_vector(4)
         quant(p10)
         weave(p11, "g", part=(CUT2, HALF))
         weave(p11, "s", part=(0, CUT2))
+        for i in range(OUT_FIRST, 2):
+            h_out(i, 0)
         x_quant(2)
         x_mult(4)
         x_mult(5)
@@ -545,7 +567,11 @@ def tile_protected_adapter_gradients_s13_kernel(
 
         by_scalar = [h_piece(g, K - PIECE, K) for g in range(SCALAR_COLS // PIECE)]
         rest = [h_piece(g, POOL_COLS if g < 1 + bool(Z_DIRECT) else 0, HALF) for g in range(GROUPS)]
-        rest = rest + [h_piece(g, HALF, K - PIECE if g < len(by_scalar) else K) for g in range(GROUPS)]
+        if SPLIT_END:
+            rest = rest + [h_piece(g, HALF, K - PIECE) for g in range(GROUPS)]
+            rest = rest + [h_piece(g, K - PIECE, K) for g in range(len(by_scalar), GROUPS)]
+        else:
+            rest = rest + [h_piece(g, HALF, K - PIECE if g < len(by_scalar) else K) for g in range(GROUPS)]
         for key in [k for k in rest if k not in early]:
             weave(key, "v")
             if last:

@@ -28,11 +28,11 @@ HALF = 512
 PIECE = 256
 BANKS = 8
 
-WEAVE_BUFS = {"weave_v": 4, "weave_s": 3, "weave_g": 1, "panel": 1}
+WEAVE_BUFS = {"weave_v": 4, "weave_s": 4, "weave_g": 1, "panel": 1}
 XBF_BUFS = {1: 3, 2: 2}
 SORTED_BUFS = 2
 SORT_BUFS = 2
-RES_BUFS = {HALF: 4, R: 6, P: 2}
+RES_BUFS = {HALF: 5, R: 6, P: 2}
 MM_BANKS = (4, 5, 2, 3)
 TURN_BANK = {2: 4, 3: 0, 4: 6, 5: 0, 6: 6, 7: 0}
 CUT0 = 256
@@ -41,7 +41,8 @@ CUT1 = 256
 CUT2 = 256
 HOW = {8: "s", 9: "s", 10: "ss", 11: "w", 12: "s", 13: "w", 14: "ss", 15: "w"}
 POOL_COLS = 256
-SCALAR_COLS = 512
+SCALAR_COLS = 768
+EARLY_HALVES = 4
 EARLY = {}
 SPLIT_FIRST = 0
 Z_DIRECT = 0
@@ -50,6 +51,7 @@ SPLIT_LAST = 1
 SPLIT_END = 1
 OUT_FIRST = 2
 ORDER = 1
+QUAD = 1
 
 
 def tile_protected_adapter_gradients_s13_kernel(
@@ -388,13 +390,23 @@ def tile_protected_adapter_gradients_s13_kernel(
             load_proj(0, 0)
             load_x(3, 1)
         load_proj(0, 1)
-        load_x(4, 2)
-        load_x(6, 2)
+        if QUAD & 1:
+            load_x(4, 4)
+        else:
+            load_x(4, 2)
+            load_x(6, 2)
         load_r()
         load_proj(1, 0)
-        load_x(8, 2)
-        load_proj(1, 1)
-        load_x(10, 2)
+        if QUAD & 2:
+            load_x(8, 4)
+            load_proj(1, 1)
+        elif QUAD & 4:
+            load_proj(1, 1)
+            load_x(8, 4)
+        else:
+            load_x(8, 2)
+            load_proj(1, 1)
+            load_x(10, 2)
         load_a()
         load_x(12, 4)
         constants()
@@ -584,11 +596,15 @@ def tile_protected_adapter_gradients_s13_kernel(
         for u in range(2 * N // HALF):
             if u >= GB_OPEN:
                 gb_mm((u,), (mm_bank(),))
-            for key, h in halves[u : u + 1]:
+            for key, h in halves[u : u + 1] if u < EARLY_HALVES else ():
                 weave(key, "s", part=(h * P, (h + 1) * P))
-                if h:
-                    quant(key)
+        late = halves[EARLY_HALVES:]
         for kb in range(K // P - 1):
+            for key, h in late[kb : kb + 1]:
+                weave(key, "s", part=(h * P, (h + 1) * P))
+            if kb == len(late):
+                for key in by_scalar:
+                    quant(key)
             ga_mm(kb, mm_bank())
         if SPLIT_LAST:
             ga_mm(K // P - 1, mm_bank(), 0, P)

@@ -22,36 +22,24 @@ P = 128
 T4 = 4
 PASS = P * T4
 GROUPS = M // PASS
-TILES = GROUPS * T4
+PAIRS = GROUPS * T4 // 2
 KP = K // PASS
 HALF = 512
 PIECE = 256
-BANKS = 8
+
+SHARE_BESIDE_GPSIMD = 256
+SHARE_BESIDE_VECTOR = 128
+SCALAR_PIECES = 3
+EARLY_HALVES = 4
+OPEN_BLOCKS = 2
+FIRST_SORTED_PAIR = 5
+
+TURN_BANK = {2: 4, 3: 0, 4: 6, 5: 0, 6: 6, 7: 0}
+MM_BANKS = (4, 5, 2, 3)
 
 WEAVE_BUFS = {"weave_v": 4, "weave_s": 4, "weave_g": 1, "panel": 1}
-XBF_BUFS = {1: 3, 2: 2}
-SORTED_BUFS = 2
-SORT_BUFS = 2
-RES_BUFS = {HALF: 5, R: 6, P: 2}
-MM_BANKS = (4, 5, 2, 3)
-TURN_BANK = {2: 4, 3: 0, 4: 6, 5: 0, 6: 6, 7: 0}
-CUT0 = 256
-CUTV = 128
-CUT1 = 256
-CUT2 = 256
-HOW = {8: "s", 9: "s", 10: "ss", 11: "w", 12: "s", 13: "w", 14: "ss", 15: "w"}
-POOL_COLS = 256
-SCALAR_COLS = 768
-EARLY_HALVES = 4
-EARLY = {}
-SPLIT_FIRST = 0
-Z_DIRECT = 0
-GB_OPEN = 2
-SPLIT_LAST = 1
-SPLIT_END = 1
-OUT_FIRST = 2
-ORDER = 1
-QUAD = 1
+WIDE_BUFS = {1: 3, 2: 2}
+RESULT_BUFS = {HALF: 5, R: 6, P: 2}
 
 
 def tile_protected_adapter_gradients_s13_kernel(
@@ -63,35 +51,6 @@ def tile_protected_adapter_gradients_s13_kernel(
         ring = ctx.enter_context(tc.tile_pool(name="ring", bufs=2))
         psum = ctx.enter_context(tc.psum_pool(name="psum", bufs=1))
         ctx.enter_context(tc.manual_schedule())
-        on_v, on_s = nc.vector.tensor_copy, nc.scalar.copy
-
-        proj_v = proj.rearrange("(a p j) n -> a p j n", p=P, j=T4)
-        xb_v = x_bytes.rearrange("(g p t) k -> g p t k", p=P, t=T4)
-        p_raw = {}
-        x_in = {}
-
-        def load_proj(c, kp):
-            w = keep.tile([P, T4, HALF], BF16, name="p_raw%d%d" % (c, kp))
-            nc.sync.dma_start(out=w[:], in_=proj_v[kp][:, :, c * HALF : (c + 1) * HALF])
-            p_raw[c, kp] = w
-
-        def load_a():
-            w = keep.tile([P, KP, T4, R], BF16, name="a_raw")
-            nc.sync.dma_start(out=w[:], in_=a.rearrange("(a p j) n -> p a j n", p=P, j=T4))
-            for kp in range(KP):
-                src["a", kp] = w[:, kp]
-                dst["a", kp] = (aq[kp], 0)
-
-        def load_x(first, count):
-            g, t0 = divmod(first, T4)
-            xt = keep.tile([P, count * K], U8, name="x_in%d" % first)
-            nc.sync.dma_start(out=xt[:].rearrange("p (t k) -> p t k", k=K), in_=xb_v[g, :, t0 : t0 + count, :])
-            for t in range(count):
-                x_in[first + t] = (xt, t)
-
-        def x_bytes_of(i, count):
-            xt, t = x_in[i]
-            return xt[:, t * K : (t + count) * K].bitcast(E4M3)
 
         r16 = keep.tile([P, GROUPS, 4 * T4], BF16, name="r16")
         sc_col = keep.tile([P, KP, 2 * T4], F32, name="sc_col")
@@ -104,45 +63,81 @@ def tile_protected_adapter_gradients_s13_kernel(
         ew = keep.tile([P, GROUPS, 2 * R], U8, name="ew", align_bytes=256)
         dw = keep.tile([P, GROUPS, 2 * N], U8, name="dw", align_bytes=256)
 
-        def load_scales():
-            nc.sync.dma_start(out=sc_col[:, :, :T4], in_=x_scale.rearrange("o (a p j) -> p (o a) j", p=P, j=T4))
-
-        def load_r():
-            nc.sync.dma_start(out=r16[:, :, :T4], in_=r.rearrange("(g p t) -> p g t", p=P, t=T4))
-
-        def constants():
-            nc.vector.memset(half[:], 0.5)
-            nc.scalar.activation(out=one[:], in_=half[:], func=COPY, scale=2.0)
-            nc.vector.memset(ident[:], 0.0)
-            make_identity(nc, ident[:], nomemset=True)
-            nc.vector.memset(es[:].rearrange("p g n -> p (g n)").bitcast(I32), 0)
-            nc.vector.memset(ds[:].rearrange("p g n -> p (g n)").bitcast(I32), 0)
-
-        def load_second_stage():
-            for g in range(GROUPS):
-                nc.sync.dma_start(out=dw[:, g, :].bitcast(I32), in_=d_words[g].bitcast(I32))
-            nc.sync.dma_start(out=ew[:].bitcast(I32), in_=e_words.bitcast(I32).rearrange("g p n -> p g n"))
-            for q in range(4):
-                nc.sync.dma_start(
-                    out=ds[32 * q : 32 * q + 4].bitcast(I32),
-                    in_=d_scales[:, 4 * q : 4 * q + 4, :].bitcast(I32).rearrange("g q n -> q g n"),
-                )
-                nc.sync.dma_start(
-                    out=es[32 * q : 32 * q + 4].bitcast(I32),
-                    in_=e_scales[:, 4 * q : 4 * q + 4, :].bitcast(I32).rearrange("g q n -> q g n"),
-                )
-
-        def bank_tile(b, shape):
-            return psum.tile(shape, F32, name="bank%d" % b)
-
         def mx_tiles(name, width):
             codes = keep.tile([P, width], U32, name=name + "_q", align_bytes=256)
             scales = keep.tile([P, width], U8, name=name + "_s", align_bytes=256)
             return codes, scales
 
-        def quantise(dst, c0, grouped):
-            cols = slice(c0, c0 + grouped.shape[1] // T4)
-            nc.vector.quantize_mx(out=dst[0][:, cols].bitcast(E4M3X4), scales=dst[1][:, cols], in_=grouped)
+        pq = {(c, kp): mx_tiles("p%d%d" % (c, kp), HALF) for c in range(2) for kp in range(KP)}
+        aq = {kp: mx_tiles("a%d" % kp, R) for kp in range(KP)}
+        hq = {g: mx_tiles("h%d" % g, K) for g in range(GROUPS)}
+        zq = {g: mx_tiles("z%d" % g, R) for g in range(GROUPS)}
+
+        planes = {}
+        woven = {}
+        target = {}
+
+        proj_v = proj.rearrange("(a p j) n -> a p j n", p=P, j=T4)
+        xb_v = x_bytes.rearrange("(g p t) k -> g p t k", p=P, t=T4)
+        x_in = {}
+
+        def load_x(first, count):
+            g, t0 = divmod(first, T4)
+            xt = keep.tile([P, count * K], U8, name="x_in%d" % first)
+            nc.sync.dma_start(out=xt[:].rearrange("p (t k) -> p t k", k=K), in_=xb_v[g, :, t0 : t0 + count, :])
+            for t in range(count):
+                x_in[first + t] = (xt, t)
+
+        def load_panel(c, kp):
+            w = keep.tile([P, T4, HALF], BF16, name="p_raw%d%d" % (c, kp))
+            nc.sync.dma_start(out=w[:], in_=proj_v[kp][:, :, c * HALF : (c + 1) * HALF])
+            planes["p", c, kp] = w[:]
+            target["p", c, kp] = (pq[c, kp], 0)
+
+        load_x(0, 1)
+        load_x(1, 1)
+        nc.sync.dma_start(out=sc_col[:, :, :T4], in_=x_scale.rearrange("o (a p j) -> p (o a) j", p=P, j=T4))
+        load_panel(0, 0)
+        load_x(2, 2)
+        load_panel(0, 1)
+        load_x(4, 4)
+        nc.sync.dma_start(out=r16[:, :, :T4], in_=r.rearrange("(g p t) -> p g t", p=P, t=T4))
+        load_panel(1, 0)
+        load_x(8, 2)
+        load_panel(1, 1)
+        load_x(10, 2)
+        a_raw = keep.tile([P, KP, T4, R], BF16, name="a_raw")
+        nc.sync.dma_start(out=a_raw[:], in_=a.rearrange("(a p j) n -> p a j n", p=P, j=T4))
+        for kp in range(KP):
+            planes["a", kp] = a_raw[:, kp]
+            target["a", kp] = (aq[kp], 0)
+        load_x(12, 4)
+
+        nc.vector.memset(half[:], 0.5)
+        nc.scalar.activation(out=one[:], in_=half[:], func=COPY, scale=2.0)
+        nc.vector.memset(ident[:], 0.0)
+        make_identity(nc, ident[:], nomemset=True)
+        nc.vector.memset(es[:].rearrange("p g n -> p (g n)").bitcast(I32), 0)
+        nc.vector.memset(ds[:].rearrange("p g n -> p (g n)").bitcast(I32), 0)
+
+        for g in range(GROUPS):
+            nc.sync.dma_start(out=dw[:, g, :].bitcast(I32), in_=d_words[g].bitcast(I32))
+        nc.sync.dma_start(out=ew[:].bitcast(I32), in_=e_words.bitcast(I32).rearrange("g p n -> p g n"))
+        for q in range(4):
+            for tile, rows in ((ds, d_scales), (es, e_scales)):
+                nc.sync.dma_start(
+                    out=tile[32 * q : 32 * q + 4].bitcast(I32),
+                    in_=rows[:, 4 * q : 4 * q + 4, :].bitcast(I32).rearrange("g q n -> q g n"),
+                )
+
+        def bank_tile(b, shape):
+            return psum.tile(shape, F32, name="bank%d" % b)
+
+        banks = list(MM_BANKS)
+
+        def mm_bank():
+            banks.append(banks.pop(0))
+            return banks[-1]
 
         def mx(out, lhs, lcols, rhs, rhs_scale, start, stop):
             nc.tensor.matmul_mx(
@@ -155,459 +150,282 @@ def tile_protected_adapter_gradients_s13_kernel(
                 stop=stop,
             )
 
-        def interleave(copy, out, in_):
-            copy(
-                out=out.rearrange("p (n i) t -> p n t i", i=4),
-                in_=in_.rearrange("p t (n i) -> p n t i", i=4),
+        def quantise(codes_scales, c0, values):
+            cols = slice(c0, c0 + values.shape[1] // T4)
+            nc.vector.quantize_mx(
+                out=codes_scales[0][:, cols].bitcast(E4M3X4), scales=codes_scales[1][:, cols], in_=values
             )
-
-        def pool_copy(out, in_):
-            nc.gpsimd.tensor_scalar(
-                out=out, in0=in_.rearrange("p t n -> p n t"), scalar1=1.0, scalar2=0.0, op0=MULT, op1=ADD
-            )
-
-        def flat(w):
-            return w.rearrange("p n t -> p (n t)")
-
-        src = {}
-        dst = {}
-        woven = {}
-
-        def weave(key, who, tag=None, part=None):
-            n = src[key].shape[2]
-            if key not in woven:
-                tag = tag or {"v": "weave_v", "s": "weave_s", "g": "weave_g"}[who]
-                woven[key] = ring.tile([P, n, T4], BF16, name=tag, align_bytes=64, bufs=WEAVE_BUFS[tag])
-            cols = slice(0, n) if part is None else slice(part[0], part[1])
-            if who == "g":
-                pool_copy(woven[key][:, cols], src[key][:, :, cols])
-            else:
-                interleave(on_v if who == "v" else on_s, woven[key][:, cols], src[key][:, :, cols])
 
         def quant(key):
-            quantise(dst[key][0], dst[key][1], flat(woven[key][:]))
+            quantise(target[key][0], target[key][1], woven[key][:].rearrange("p n t -> p (n t)"))
 
-        pq = {(c, kp): mx_tiles("p%d%d" % (c, kp), HALF) for c in range(2) for kp in range(KP)}
-        aq = {kp: mx_tiles("a%d" % kp, R) for kp in range(KP)}
-        hq = {g: mx_tiles("h%d" % g, K) for g in range(GROUPS)}
-        zq = {g: mx_tiles("z%d" % g, R) for g in range(GROUPS)}
+        def weave(key, who, lo=0, hi=None, tag=None):
+            n = planes[key].shape[2]
+            if key not in woven:
+                tag = tag or "weave_" + who
+                woven[key] = ring.tile([P, n, T4], BF16, name=tag, align_bytes=64, bufs=WEAVE_BUFS[tag])
+            out, in_ = woven[key][:, lo : hi or n], planes[key][:, :, lo : hi or n]
+            if who == "g":
+                nc.gpsimd.tensor_scalar(
+                    out=out, in0=in_.rearrange("p t n -> p n t"), scalar1=1.0, scalar2=0.0, op0=MULT, op1=ADD
+                )
+            else:
+                copy = nc.vector.tensor_copy if who == "v" else nc.scalar.copy
+                copy(out=out.rearrange("p (n i) t -> p n t i", i=4), in_=in_.rearrange("p t (n i) -> p n t i", i=4))
 
-        def proj_panel(c, kp):
-            key = ("p", c, kp)
-            src[key] = p_raw[c, kp][:]
-            dst[key] = (pq[c, kp], 0)
-            return key
-
-        def h_piece(g, lo, hi):
-            c, n0 = divmod(lo, HALF)
-            key = ("h", g, lo, hi)
-            src[key] = h_pl[g, c][:, :, n0 : n0 + hi - lo]
-            dst[key] = (hq[g], lo)
-            return key
-
-        x_words = {}
         x_wide = {}
+        x_words = {}
         x_bank = {}
-        x_gr = {}
+        x_woven = {}
         xq = {}
 
-        def x_widen(i, count=1):
-            w = ring.tile([P, count * K], BF16, name="x_bf%d" % count, bufs=XBF_BUFS[count])
-            nc.scalar.copy(out=w[:], in_=x_bytes_of(i, count))
+        def x_fp8(i, count):
+            xt, t = x_in[i]
+            return xt[:, t * K : (t + count) * K].bitcast(E4M3)
+
+        def widen_first(kp):
+            w = keep.tile([P, PASS], BF16, name="x_first%d" % kp)
+            nc.scalar.copy(out=w[:], in_=x_fp8(0, 1)[:, kp * PASS : (kp + 1) * PASS])
+            for u in range(2):
+                x_words[0, kp, u] = w[:].bitcast(F32)[:, u::2]
+
+        def widen(i, count=1):
+            w = ring.tile([P, count * K], BF16, name="x_bf%d" % count, bufs=WIDE_BUFS[count])
+            nc.scalar.copy(out=w[:], in_=x_fp8(i, count))
             x_wide[i] = w[:]
-            words = w[:].bitcast(F32)
             for j in range(count):
                 for kp in range(KP):
                     for u in range(2):
                         w0 = 2 * P * (KP * j + kp)
-                        x_words[i + j, kp, u] = words[:, w0 + u : w0 + 2 * P : 2]
+                        x_words[i + j, kp, u] = w[:].bitcast(F32)[:, w0 + u : w0 + 2 * P : 2]
 
-        def x_sort(i, count):
-            w = ring.tile([P, 2, count * K // 2], BF16, name="x_sort%d" % count, bufs=SORT_BUFS)
-            nc.vector.tensor_copy(
-                out=w[:].rearrange("p u (w e) -> p u w e", e=2),
-                in_=x_wide[i].rearrange("p (w u e) -> p u w e", u=2, e=2),
-            )
-            for j in range(count):
-                for kp in range(KP):
-                    for u in range(2):
-                        w0 = P * (KP * j + kp)
-                        x_words[i + j, kp, u] = w[:, u].bitcast(F32)[:, w0 : w0 + P]
-
-        def x_widen_pass(i, kp):
-            w = keep.tile([P, PASS], BF16, name="x_first%d" % kp)
-            nc.scalar.copy(out=w[:], in_=x_bytes_of(i, 1)[:, kp * PASS : (kp + 1) * PASS])
-            for u in range(2):
-                x_words[i, kp, u] = w[:].bitcast(F32)[:, u::2]
-
-        def x_widen_sorted(i):
-            w = ring.tile([P, K], BF16, name="x_sorted", bufs=SORTED_BUFS)
+        def widen_sorted(i):
+            w = ring.tile([P, K], BF16, name="x_sorted")
             nc.vector.tensor_scalar(
                 out=w[:].rearrange("p (u w e) -> p w u e", u=2, e=2),
-                in0=x_bytes_of(i, 1),
+                in0=x_fp8(i, 1),
                 scalar1=one[:],
                 scalar2=None,
                 op0=MULT,
             )
-            words = w[:].bitcast(F32)
             for kp in range(KP):
                 for u in range(2):
-                    x_words[i, kp, u] = words[:, (u * KP + kp) * P : (u * KP + kp + 1) * P]
+                    x_words[i, kp, u] = w[:].bitcast(F32)[:, (u * KP + kp) * P : (u * KP + kp + 1) * P]
 
-        def x_turn(i, b):
+        def sort_words(i):
+            w = ring.tile([P, 2, K // 2], BF16, name="x_sort1")
+            nc.vector.tensor_copy(
+                out=w[:].rearrange("p u (w e) -> p u w e", e=2),
+                in_=x_wide[i].rearrange("p (w u e) -> p u w e", u=2, e=2),
+            )
+            for kp in range(KP):
+                for u in range(2):
+                    x_words[i, kp, u] = w[:, u].bitcast(F32)[:, kp * P : (kp + 1) * P]
+
+        def turn(i, b):
             x_bank[i] = bank_tile(b, [P, 2, KP, P])
             for kp in range(KP):
                 for u in range(2):
                     nc.tensor.transpose(x_bank[i][:, u, kp, :], x_words[i, kp, u], ident[:])
 
-        def x_mult(i):
-            if i % 2 == 0:
-                x_gr[i // 2] = ring.tile([P, 2, KP * P * T4], BF16, name="x_gr", align_bytes=64, bufs=2)
-                xq[i // 2] = mx_tiles("x%d" % i, 2 * KP * P)
-            nc.vector.tensor_tensor(
-                out=x_gr[i // 2][:, i % 2].rearrange("p (a r u e) -> p a r u e", a=KP, u=2, e=2),
-                in0=x_bank[i][:].bitcast(BF16).rearrange("p u a (r e) -> p a r u e", e=2),
-                in1=sc_col[:, :, :T4].rearrange("p a (o u e) -> p a o u e", o=1, e=2).to_broadcast([P, KP, P, 2, 2]),
-                op=MULT,
-            )
+        def turn_pair(s):
+            for j in range(2):
+                turn(2 * s + j, TURN_BANK[s] + j)
 
-        def x_quant(i, count=2):
-            j = i % 2
-            quantise(xq[i // 2], j * KP * P, x_gr[i // 2][:, j : j + count].rearrange("p a n -> p (a n)"))
+        def scale_pair(s):
+            x_woven[s] = ring.tile([P, 2, KP * P * T4], BF16, name="x_gr", align_bytes=64)
+            xq[s] = mx_tiles("x%d" % (2 * s), 2 * KP * P)
+            for j in range(2):
+                nc.vector.tensor_tensor(
+                    out=x_woven[s][:, j].rearrange("p (a m u e) -> p a m u e", a=KP, u=2, e=2),
+                    in0=x_bank[2 * s + j][:].bitcast(BF16).rearrange("p u a (m e) -> p a m u e", e=2),
+                    in1=sc_col[:, :, :T4].rearrange("p a (o u e) -> p a o u e", o=1, e=2).to_broadcast([P, KP, P, 2, 2]),
+                    op=MULT,
+                )
 
-        def x_cols(i, kp):
+        def quant_pair(s):
+            quantise(xq[s], 0, x_woven[s][:].rearrange("p j n -> p (j n)"))
+
+        def x_mx(out, i, kp, weights, cols):
             c0 = ((i % 2) * KP + kp) * P
-            return slice(c0, c0 + P)
-
-        h_pl = {}
-        z_pl = {}
+            codes, scales = weights
+            mx(out, xq[i // 2], slice(c0, c0 + P), codes[:, cols].bitcast(E4M3X4), scales[:, cols], kp == 0, kp == KP - 1)
 
         h_bank = {}
+        h_planes = {}
+        z_planes = {}
 
-        def h_pass(i, c, kp, b=None):
+        def h_pass(i, c, kp, b):
             if kp == 0:
                 h_bank[i, c] = bank_tile(b, [P, HALF])
-            codes, scales = pq[c, kp]
-            mx(h_bank[i, c][:], xq[i // 2], x_cols(i, kp), codes[:].bitcast(E4M3X4), scales[:], kp == 0, kp == KP - 1)
+            x_mx(h_bank[i, c][:], i, kp, pq[c, kp], slice(0, HALF))
+
+        def h_out(i, c):
+            g, t = divmod(i, T4)
+            if t == 0:
+                name = "h_pl%d%d" % (g, c) if g < 2 else "p_raw%d%d" % (g - 2, c)
+                h_planes[g, c] = keep.tile([P, T4, HALF], BF16, name=name)
+            nc.scalar.activation(out=h_planes[g, c][:, t, :], in_=h_bank[i, c][:], func=COPY, scale=r32[:, g, t : t + 1])
 
         def h_mm(i, c, b):
             for kp in range(KP):
                 h_pass(i, c, kp, b)
             h_out(i, c)
 
-        def h_out(i, c):
-            g, t = divmod(i, T4)
-            bank = h_bank[i, c]
-            if (g, c) not in h_pl:
-                tag = "h_pl%d%d" % (g, c) if g < 2 else "p_raw%d%d" % (g - 2, c)
-                h_pl[g, c] = keep.tile([P, T4, HALF], BF16, name=tag)
-            nc.scalar.activation(out=h_pl[g, c][:, t, :], in_=bank[:], func=COPY, scale=r32[:, g, t : t + 1])
-
-        def z_mm(i, b):
-            g, t0 = divmod(i, T4)
-            bank = bank_tile(b, [P, 2, R])
-            for j in range(2):
-                for kp in range(KP):
-                    mx(bank[:, j, :], xq[i // 2], x_cols(i + j, kp), aq[kp][0][:].bitcast(E4M3X4), aq[kp][1][:], kp == 0, kp == KP - 1)
-            if g not in z_pl:
-                z_pl[g] = keep.tile([P, T4, R], BF16, name="z_pl%d" % g)
-                src["z", g] = z_pl[g][:]
-                dst["z", g] = (zq[g], 0)
-            for j in range(2):
-                t = t0 + j
-                nc.scalar.activation(out=z_pl[g][:, t, :], in_=bank[:, j, :], func=COPY, scale=r32[:, g, t : t + 1])
-
-        z_bank = {}
-
-        def z_mm_direct(g, h, b):
-            z_bank[g, h] = bank_tile(b, [P, T4, P])
-            cols = slice(h * P, (h + 1) * P)
-            for t in range(T4):
-                i = T4 * g + t
-                for kp in range(KP):
-                    mx(z_bank[g, h][:, t, :], xq[i // 2], x_cols(i, kp), aq[kp][0][:, cols].bitcast(E4M3X4), aq[kp][1][:, cols], kp == 0, kp == KP - 1)
-
-        def z_out_direct(g, h):
-            if h == 0:
-                woven["z", g] = ring.tile([P, R, T4], BF16, name="z_direct", align_bytes=64, bufs=2)
-                dst["z", g] = (zq[g], 0)
-            nc.vector.tensor_tensor(
-                out=woven["z", g][:, h * P : (h + 1) * P, :],
-                in0=z_bank[g, h][:].rearrange("p t n -> p n t"),
-                in1=r32[:, g : g + 1, :].to_broadcast([P, P, T4]),
-                op=MULT,
-            )
-
-        def store(bank, to, copy):
-            w = ring.tile(list(bank.shape), F32, name="res%d" % bank.shape[1], bufs=RES_BUFS[bank.shape[1]])
-            copy(out=w[:], in_=bank[:])
-            nc.sync.dma_start(out=to, in_=w[:])
-
-        def gb_mm(units, banks):
-            tiles = [bank_tile(b, [P, HALF]) for b in banks]
-            for groups in (range(GROUPS - 1), (GROUPS - 1,)):
-                for u, bank in zip(units, tiles):
-                    rb, nb = divmod(u, N // HALF)
-                    for g in groups:
-                        mx(
-                            bank[:],
-                            zq[g],
-                            slice(rb * P, (rb + 1) * P),
-                            dw[:, g, 2 * HALF * nb : 2 * HALF * (nb + 1)].bitcast(E2M1X4),
-                            ds[:, g, HALF * nb : HALF * (nb + 1)],
-                            g == 0,
-                            g == GROUPS - 1,
-                        )
-            for u, bank in zip(units, tiles):
-                rb, nb = divmod(u, N // HALF)
-                store(bank, out_1[rb * P : (rb + 1) * P, nb * HALF : (nb + 1) * HALF], on_s)
-
-        def ga_mm(kb, b, c0=0, width=R, copy=on_s):
-            bank = bank_tile(b, [P, width])
-            for g in range(GROUPS):
-                mx(
-                    bank[:],
-                    hq[g],
-                    slice(kb * P, (kb + 1) * P),
-                    ew[:, g, 2 * c0 : 2 * (c0 + width)].bitcast(E2M1X4),
-                    es[:, g, c0 : c0 + width],
-                    g == 0,
-                    g == GROUPS - 1,
-                )
-            store(bank, out_0[kb * P : (kb + 1) * P, c0 : c0 + width], copy)
-
-        load_x(0, 1)
-        load_x(1, 1)
-        load_scales()
-        if ORDER == 0:
-            load_x(2, 2)
-            load_proj(0, 0)
-        elif ORDER == 1:
-            load_proj(0, 0)
-            load_x(2, 2)
-        else:
-            load_x(2, 1)
-            load_proj(0, 0)
-            load_x(3, 1)
-        load_proj(0, 1)
-        if QUAD & 1:
-            load_x(4, 4)
-        else:
-            load_x(4, 2)
-            load_x(6, 2)
-        load_r()
-        load_proj(1, 0)
-        if QUAD & 2:
-            load_x(8, 4)
-            load_proj(1, 1)
-        elif QUAD & 4:
-            load_proj(1, 1)
-            load_x(8, 4)
-        else:
-            load_x(8, 2)
-            load_proj(1, 1)
-            load_x(10, 2)
-        load_a()
-        load_x(12, 4)
-        constants()
-        load_second_stage()
-
-        banks = list(MM_BANKS)
-
-        def mm_bank():
-            banks.append(banks.pop(0))
-            return banks[-1]
-
-        def both(i):
-            for c in range(2):
-                h_mm(i, c, mm_bank())
-
-        def turn_pair(s):
-            for j in range(2):
-                x_turn(2 * s + j, TURN_BANK[s] + j)
-
-        def first_pair(c, banks):
+        def h_first_pair(c, two_banks):
             for kp in range(KP):
                 for i in range(2):
-                    h_pass(i, c, kp, banks[i])
+                    h_pass(i, c, kp, two_banks[i])
 
-
-        def widen_on_scalar(s):
-            mine = [i for i in (2 * s, 2 * s + 1) if HOW[i] != "w"]
-            if mine:
-                x_widen(mine[0], len(mine))
-
-        def widen_on_vector(s):
-            if HOW[2 * s] == HOW[2 * s + 1] == "ss":
-                x_sort(2 * s, 2)
-            elif HOW[2 * s] == "ss":
-                x_sort(2 * s, 1)
+        def h_pair(s):
             for i in (2 * s, 2 * s + 1):
-                if HOW[i] == "w":
-                    x_widen_sorted(i)
+                for c in range(2):
+                    h_mm(i, c, mm_bank())
+
+        def h_piece(g, lo, hi):
+            c, n0 = divmod(lo, HALF)
+            key = ("h", g, lo, hi)
+            planes[key] = h_planes[g, c][:, :, n0 : n0 + hi - lo]
+            target[key] = (hq[g], lo)
+            return key
+
+        def z_group(g):
+            z_planes[g] = keep.tile([P, T4, R], BF16, name="z_pl%d" % g)
+            planes["z", g] = z_planes[g][:]
+            target["z", g] = (zq[g], 0)
+            for t0 in (0, 2):
+                bank = bank_tile(mm_bank(), [P, 2, R])
+                for j in range(2):
+                    for kp in range(KP):
+                        x_mx(bank[:, j, :], T4 * g + t0 + j, kp, aq[kp], slice(0, R))
+                for j in range(2):
+                    t = t0 + j
+                    nc.scalar.activation(out=z_planes[g][:, t, :], in_=bank[:, j, :], func=COPY, scale=r32[:, g, t : t + 1])
+
+        def second_stage(lhs, words, scales, width, to, blocks, copy=nc.scalar.copy):
+            block_banks = [bank_tile(mm_bank(), [P, width]) for block in blocks]
+            for groups in (range(GROUPS - 1), (GROUPS - 1,)):
+                for (r0, c0), bank in zip(blocks, block_banks):
+                    for g in groups:
+                        rhs = words[:, g, 2 * c0 : 2 * (c0 + width)].bitcast(E2M1X4)
+                        mx(bank[:], lhs[g], slice(r0, r0 + P), rhs, scales[:, g, c0 : c0 + width], g == 0, g == GROUPS - 1)
+            for (r0, c0), bank in zip(blocks, block_banks):
+                result = ring.tile([P, width], F32, name="res%d" % width, bufs=RESULT_BUFS[width])
+                copy(out=result[:], in_=bank[:])
+                nc.sync.dma_start(out=to[r0 : r0 + P, c0 : c0 + width], in_=result[:])
+
 
         for kp in range(KP):
-            x_widen_pass(0, kp)
-        x_widen_sorted(1)
-        if ORDER == 0:
-            x_widen(2, 2)
-        elif ORDER == 2:
-            x_widen(2)
-        for i in range((4, 2, 3)[ORDER]):
-            x_turn(i, i)
-        p00, p01, p10, p11 = [proj_panel(c, kp) for c in range(2) for kp in range(KP)]
-        weave(p00, "s", tag="panel", part=(0, CUT0))
-        weave(p00, "g", part=(CUT0, HALF))
-        if ORDER == 1:
-            x_widen(2, 2)
-        elif ORDER == 2:
-            x_widen(3)
-        for i in range((4, 2, 3)[ORDER], 4):
-            x_turn(i, i)
-        x_mult(0)
-        x_mult(1)
-        weave(p01, "s", tag="weave_g", part=(0, CUTV))
-        weave(p01, "v", part=(CUTV, HALF))
-        x_widen(4)
-        x_widen(5)
-        quant(p00)
-        quant(p01)
-        weave(p10, "g", part=(CUT1, HALF))
-        x_quant(0)
-        x_mult(2)
-        x_mult(3)
+            widen_first(kp)
+        widen_sorted(1)
+        for i in range(2):
+            turn(i, i)
+        weave(("p", 0, 0), "s", 0, SHARE_BESIDE_GPSIMD, tag="panel")
+        weave(("p", 0, 0), "g", SHARE_BESIDE_GPSIMD)
+        widen(2, 2)
+        for i in range(2, 4):
+            turn(i, i)
+        scale_pair(0)
+        weave(("p", 0, 1), "s", 0, SHARE_BESIDE_VECTOR, tag="weave_g")
+        weave(("p", 0, 1), "v", SHARE_BESIDE_VECTOR)
+        widen(4)
+        widen(5)
+        quant(("p", 0, 0))
+        quant(("p", 0, 1))
+        weave(("p", 1, 0), "g", SHARE_BESIDE_GPSIMD)
+        quant_pair(0)
+        scale_pair(1)
         nc.vector.tensor_copy(out=r32[:], in_=r16[:, :, :T4])
-        x_widen(6, 2)
-        weave(p10, "s", part=(0, CUT1))
+        widen(6, 2)
+        weave(("p", 1, 0), "s", 0, SHARE_BESIDE_GPSIMD)
         turn_pair(2)
-        for kp in range(KP):
-            for i in range(2):
-                h_pass(i, 0, kp, 6 + i)
+        h_first_pair(0, (6, 7))
         turn_pair(3)
-        widen_on_scalar(4)
-        for i in range(OUT_FIRST):
+        widen(8, 2)
+        for i in range(2):
             h_out(i, 0)
-        widen_on_vector(4)
-        quant(p10)
-        weave(p11, "g", part=(CUT2, HALF))
-        weave(p11, "s", part=(0, CUT2))
-        for i in range(OUT_FIRST, 2):
-            h_out(i, 0)
-        x_quant(2)
-        x_mult(4)
-        x_mult(5)
-        h_mm(2, 0, 2)
-        h_mm(3, 0, 3)
+
+        quant(("p", 1, 0))
+        weave(("p", 1, 1), "g", SHARE_BESIDE_GPSIMD)
+        weave(("p", 1, 1), "s", 0, SHARE_BESIDE_GPSIMD)
+        quant_pair(1)
+        scale_pair(2)
+        for i in (2, 3):
+            h_mm(i, 0, i)
         turn_pair(4)
-        quant(p11)
+        quant(("p", 1, 1))
         weave(("a", 0), "g")
-        x_quant(4)
-        x_mult(6)
-        x_mult(7)
-        widen_on_scalar(5)
-        first_pair(1, (mm_bank(), mm_bank()))
+        quant_pair(2)
+        scale_pair(3)
+        widen(2 * FIRST_SORTED_PAIR)
+        h_first_pair(1, (mm_bank(), mm_bank()))
         for i in range(2):
             h_out(i, 1)
-        for i in range(2, 4):
+        for i in (2, 3):
             h_mm(i, 1, mm_bank())
-        both(4)
-        both(5)
-        widen_on_vector(5)
+        h_pair(2)
+        sort_words(2 * FIRST_SORTED_PAIR)
+        widen_sorted(2 * FIRST_SORTED_PAIR + 1)
         quant(("a", 0))
-        x_quant(6)
+        quant_pair(3)
 
-        pool_jobs = {4: ("a", 1), 5: h_piece(0, 0, POOL_COLS), 7: ("z", 0)}
-        if not Z_DIRECT:
-            pool_jobs.update({6: ("z", 0), 7: ("z", 1)})
-        early = []
-        for s in range(4, 8):
-            if s + 2 < 8:
-                widen_on_scalar(s + 2)
-            if s + 1 < 8:
+        pool_jobs = [("a", 1), h_piece(0, 0, PIECE), ("z", 0), ("z", 1)]
+        for s, job in zip(range(4, PAIRS), pool_jobs):
+            if s + 2 < PAIRS:
+                widen(2 * s + 4)
+            if s + 1 < PAIRS:
                 turn_pair(s + 1)
             if s == 5:
-                z_mm(0, mm_bank())
-                z_mm(2, mm_bank())
-            if s == 6 and Z_DIRECT:
-                pool_jobs[s] = h_piece(1, 0, POOL_COLS)
-            weave(pool_jobs[s], "g")
-            x_mult(2 * s)
-            x_mult(2 * s + 1)
-            if s == 7 and not Z_DIRECT:
-                banks[:0] = [6, 7]
-                z_mm(8, mm_bank())
-                z_mm(10, mm_bank())
-            both(2 * s - 2)
-            both(2 * s - 1)
-            if s + 2 < 8:
-                widen_on_vector(s + 2)
-            for g, lo, hi in EARLY.get(s, ()):
-                early.append(h_piece(g, lo, hi))
-                weave(early[-1], "v")
-            quant(pool_jobs[s])
+                z_group(0)
+            weave(job, "g")
+            scale_pair(s)
+            if s == PAIRS - 1:
+                banks[:0] = [TURN_BANK[s - 1], TURN_BANK[s - 1] + 1]
+                z_group(2)
+            h_pair(s - 1)
+            if s + 2 < PAIRS:
+                sort_words(2 * s + 4)
+                widen_sorted(2 * s + 5)
+            quant(job)
             if s == 5:
-                z_mm(4, mm_bank())
-                z_mm(6, mm_bank())
-            x_quant(2 * s)
-        if Z_DIRECT:
-            for h in range(2):
-                z_mm_direct(2, h, 6 + h)
-            for h in range(2):
-                z_mm_direct(3, h, h)
-            weave(("z", 1), "g")
-            for g in (2, 3):
-                for h in range(2):
-                    z_out_direct(g, h)
-            for g in (1, 2, 3):
-                quant(("z", g))
-            last = None
-        else:
-            banks[:0] = [0, 1]
-            z_mm(12, mm_bank())
-            z_mm(14, mm_bank())
-            early = [h_piece(1, 0, HALF), h_piece(0, POOL_COLS, HALF)]
-            weave(("z", 2), "v")
-            weave(early[0], "v")
-            quant(("z", 2))
-            weave(early[1], "v")
-            weave(("z", 3), "v")
-            quant(early[1])
-            quant(("z", 3))
-            last = early[0]
-        both(14)
-        both(15)
+                z_group(1)
+            quant_pair(s)
+        banks[:0] = [TURN_BANK[PAIRS - 1], TURN_BANK[PAIRS - 1] + 1]
+        z_group(3)
 
-        by_scalar = [h_piece(g, K - PIECE, K) for g in range(SCALAR_COLS // PIECE)]
-        rest = [h_piece(g, POOL_COLS if g < 1 + bool(Z_DIRECT) else 0, HALF) for g in range(GROUPS)]
-        if SPLIT_END:
-            rest = rest + [h_piece(g, HALF, K - PIECE) for g in range(GROUPS)]
-            rest = rest + [h_piece(g, K - PIECE, K) for g in range(len(by_scalar), GROUPS)]
-        else:
-            rest = rest + [h_piece(g, HALF, K - PIECE if g < len(by_scalar) else K) for g in range(GROUPS)]
-        for key in [k for k in rest if k not in early]:
+        first_pieces = [h_piece(1, 0, HALF), h_piece(0, PIECE, HALF)]
+        weave(("z", 2), "v")
+        weave(first_pieces[0], "v")
+        quant(("z", 2))
+        weave(first_pieces[1], "v")
+        weave(("z", 3), "v")
+        quant(first_pieces[1])
+        quant(("z", 3))
+        h_pair(PAIRS - 1)
+        by_scalar = [h_piece(g, K - PIECE, K) for g in range(SCALAR_PIECES)]
+        pieces = [h_piece(g, 0, HALF) for g in range(2, GROUPS)]
+        pieces = pieces + [h_piece(g, HALF, K - PIECE) for g in range(GROUPS)]
+        pieces = pieces + [h_piece(g, K - PIECE, K) for g in range(SCALAR_PIECES, GROUPS)]
+        for before, key in zip(first_pieces[:1] + pieces, pieces):
             weave(key, "v")
-            if last:
-                quant(last)
-            last = key
-        quant(last)
-        halves = [(key, h) for key in by_scalar for h in range(2)]
-        banks[:] = banks + [b for b in range(BANKS) if b not in banks]
-        gb_mm(range(GB_OPEN), [mm_bank() for u in range(GB_OPEN)])
-        for u in range(2 * N // HALF):
-            if u >= GB_OPEN:
-                gb_mm((u,), (mm_bank(),))
-            for key, h in halves[u : u + 1] if u < EARLY_HALVES else ():
-                weave(key, "s", part=(h * P, (h + 1) * P))
+            quant(before)
+        quant(pieces[-1])
+
+        halves = [(key, "s", h * P, (h + 1) * P) for key in by_scalar for h in range(2)]
+        blocks = [(r0, c0) for r0 in range(0, R, P) for c0 in range(0, N, HALF)]
+        second_stage(zq, dw, ds, HALF, out_1, blocks[:OPEN_BLOCKS])
+        for u in range(len(blocks)):
+            if u >= OPEN_BLOCKS:
+                second_stage(zq, dw, ds, HALF, out_1, blocks[u : u + 1])
+            if u < EARLY_HALVES:
+                weave(*halves[u])
         late = halves[EARLY_HALVES:]
         for kb in range(K // P - 1):
-            for key, h in late[kb : kb + 1]:
-                weave(key, "s", part=(h * P, (h + 1) * P))
+            if kb < len(late):
+                weave(*late[kb])
             if kb == len(late):
                 for key in by_scalar:
                     quant(key)
-            ga_mm(kb, mm_bank())
-        if SPLIT_LAST:
-            ga_mm(K // P - 1, mm_bank(), 0, P)
-            ga_mm(K // P - 1, mm_bank(), P, P, on_v)
-        else:
-            ga_mm(K // P - 1, mm_bank(), copy=on_v)
+            second_stage(hq, ew, es, R, out_0, [(kb * P, 0)])
+        for h, copy in enumerate((nc.scalar.copy, nc.vector.tensor_copy)):
+            second_stage(hq, ew, es, P, out_0, [(K - P, h * P)], copy)

@@ -173,7 +173,6 @@ def tile_protected_adapter_gradients_s13_kernel(
                 copy = nc.vector.tensor_copy if who == "v" else nc.scalar.copy
                 copy(out=out.rearrange("p (n i) t -> p n t i", i=4), in_=in_.rearrange("p t (n i) -> p n t i", i=4))
 
-        x_wide = {}
         x_words = {}
         x_bank = {}
         x_woven = {}
@@ -192,7 +191,6 @@ def tile_protected_adapter_gradients_s13_kernel(
         def widen(i, count=1):
             w = ring.tile([P, count * K], BF16, name="x_bf%d" % count, bufs=WIDE_BUFS[count])
             nc.scalar.copy(out=w[:], in_=x_fp8(i, count))
-            x_wide[i] = w[:]
             for j in range(count):
                 for kp in range(KP):
                     for u in range(2):
@@ -211,16 +209,6 @@ def tile_protected_adapter_gradients_s13_kernel(
             for kp in range(KP):
                 for u in range(2):
                     x_words[i, kp, u] = w[:].bitcast(F32)[:, (u * KP + kp) * P : (u * KP + kp + 1) * P]
-
-        def sort_words(i):
-            w = ring.tile([P, 2, K // 2], BF16, name="x_sort1")
-            nc.vector.tensor_copy(
-                out=w[:].rearrange("p u (w e) -> p u w e", e=2),
-                in_=x_wide[i].rearrange("p (w u e) -> p u w e", u=2, e=2),
-            )
-            for kp in range(KP):
-                for u in range(2):
-                    x_words[i, kp, u] = w[:, u].bitcast(F32)[:, kp * P : (kp + 1) * P]
 
         def turn(i, b):
             x_bank[i] = bank_tile(b, [P, 2, KP, P])
@@ -364,7 +352,6 @@ def tile_protected_adapter_gradients_s13_kernel(
         for i in (2, 3):
             h_mm(i, 1, mm_bank())
         h_pair(2)
-        sort_words(2 * FIRST_SORTED_PAIR)
         widen_sorted(2 * FIRST_SORTED_PAIR + 1)
         quant(("a", 0))
         quant_pair(3)
@@ -384,7 +371,6 @@ def tile_protected_adapter_gradients_s13_kernel(
                 z_group(2)
             h_pair(s - 1)
             if s + 2 < PAIRS:
-                sort_words(2 * s + 4)
                 widen_sorted(2 * s + 5)
             quant(job)
             if s == 5:

@@ -34,6 +34,8 @@ EARLY_HALVES = 4
 OPEN_BLOCKS = 2
 FIRST_SORTED_PAIR = 5
 
+MOVING_SCALES_AT = 128
+
 TURN_BANK = {2: 4, 3: 0, 4: 6, 5: 0, 6: 6, 7: 0}
 MM_BANKS = (4, 5, 2, 3)
 
@@ -57,19 +59,22 @@ def tile_protected_adapter_gradients_s13_kernel(
         ident = keep.tile([P, P], F32, name="ident")
         half = keep.tile([P, 1], F32, name="half")
         one = keep.tile([P, 1], F32, name="one")
-        es = keep.tile([P, GROUPS, R], U8, name="es", align_bytes=256)
-        ds = keep.tile([P, GROUPS, N], U8, name="ds", align_bytes=256)
+
+        def scale_tile(name, width, lead):
+            return keep.tile([P, lead + width], U8, name=name, align_bytes=256)[:, lead:]
+
+        es = scale_tile("es", GROUPS * R, MOVING_SCALES_AT).rearrange("p (g n) -> p g n", n=R)
+        ds = scale_tile("ds", GROUPS * N, MOVING_SCALES_AT).rearrange("p (g n) -> p g n", n=N)
         r32 = keep.tile([P, GROUPS, T4], F32, name="r32")
         ew = keep.tile([P, GROUPS, 2 * R], U8, name="ew", align_bytes=256)
         dw = keep.tile([P, GROUPS, 2 * N], U8, name="dw", align_bytes=256)
 
-        def mx_tiles(name, width):
+        def mx_tiles(name, width, lead=0):
             codes = keep.tile([P, width], U32, name=name + "_q", align_bytes=256)
-            scales = keep.tile([P, width], U8, name=name + "_s", align_bytes=256)
-            return codes, scales
+            return codes, scale_tile(name + "_s", width, lead)
 
-        pq = {(c, kp): mx_tiles("p%d%d" % (c, kp), HALF) for c in range(2) for kp in range(KP)}
-        aq = {kp: mx_tiles("a%d" % kp, R) for kp in range(KP)}
+        pq = {(c, kp): mx_tiles("p%d%d" % (c, kp), HALF, MOVING_SCALES_AT) for c in range(2) for kp in range(KP)}
+        aq = {kp: mx_tiles("a%d" % kp, R, MOVING_SCALES_AT) for kp in range(KP)}
         hq = {g: mx_tiles("h%d" % g, K) for g in range(GROUPS)}
         zq = {g: mx_tiles("z%d" % g, R) for g in range(GROUPS)}
 

@@ -33,11 +33,14 @@ SCALAR_PIECES = 3
 EARLY_HALVES = 4
 OPEN_BLOCKS = 2
 FIRST_SORTED_PAIR = 5
+Z_STEP = 5
 
 MOVING_SCALES_AT = 128
 
 TURN_BANK = {2: 4, 3: 0, 4: 6, 5: 0, 6: 6, 7: 0}
 MM_BANKS = (4, 5, 2, 3)
+FIRST_TILE_BANKS = (0, 6)
+FIRST_H_BANKS = (6, 7)
 
 WEAVE_BUFS = {"weave_v": 4, "weave_s": 4, "weave_g": 1, "panel": 1}
 WIDE_BUFS = {1: 3, 2: 2}
@@ -179,7 +182,7 @@ def tile_protected_adapter_gradients_s13_kernel(
                 copy(out=out.rearrange("p (n i) t -> p n t i", i=4), in_=in_.rearrange("p t (n i) -> p n t i", i=4))
 
         x_words = {}
-        x_bank = {}
+        x_banks = {}
         x_woven = {}
         xq = {}
 
@@ -215,11 +218,12 @@ def tile_protected_adapter_gradients_s13_kernel(
                 for u in range(2):
                     x_words[i, kp, u] = w[:].bitcast(F32)[:, (u * KP + kp) * P : (u * KP + kp + 1) * P]
 
-        def turn(i, b):
-            x_bank[i] = bank_tile(b, [P, 2, KP, P])
-            for kp in range(KP):
+        def turn(i, b, kp0=0, passes=KP):
+            bank = bank_tile(b, [P, 2, passes, P])
+            x_banks.setdefault(i, []).append((bank, kp0, passes))
+            for kp in range(passes):
                 for u in range(2):
-                    nc.tensor.transpose(x_bank[i][:, u, kp, :], x_words[i, kp, u], ident[:])
+                    nc.tensor.transpose(bank[:, u, kp, :], x_words[i, kp0 + kp, u], ident[:])
 
         def turn_pair(s):
             for j in range(2):
@@ -229,12 +233,15 @@ def tile_protected_adapter_gradients_s13_kernel(
             x_woven[s] = ring.tile([P, 2, KP * P * T4], BF16, name="x_gr", align_bytes=64)
             xq[s] = mx_tiles("x%d" % (2 * s), 2 * KP * P)
             for j in range(2):
-                nc.vector.tensor_tensor(
-                    out=x_woven[s][:, j].rearrange("p (a m u e) -> p a m u e", a=KP, u=2, e=2),
-                    in0=x_bank[2 * s + j][:].bitcast(BF16).rearrange("p u a (m e) -> p a m u e", e=2),
-                    in1=sc_col[:, :, :T4].rearrange("p a (o u e) -> p a o u e", o=1, e=2).to_broadcast([P, KP, P, 2, 2]),
-                    op=MULT,
-                )
+                for bank, kp0, passes in x_banks[2 * s + j]:
+                    scales = sc_col[:, kp0 : kp0 + passes, :T4].rearrange("p a (o u e) -> p a o u e", o=1, e=2)
+                    values = x_woven[s][:, j, kp0 * PASS : (kp0 + passes) * PASS]
+                    nc.vector.tensor_tensor(
+                        out=values.rearrange("p (a m u e) -> p a m u e", a=passes, u=2, e=2),
+                        in0=bank[:].bitcast(BF16).rearrange("p u a (m e) -> p a m u e", e=2),
+                        in1=scales.to_broadcast([P, passes, P, 2, 2]),
+                        op=MULT,
+                    )
 
         def quant_pair(s):
             quantise(xq[s], 0, x_woven[s][:].rearrange("p j n -> p (j n)"))
@@ -311,8 +318,9 @@ def tile_protected_adapter_gradients_s13_kernel(
         for kp in range(KP):
             widen_first(kp)
         widen_sorted(1)
-        for i in range(2):
-            turn(i, i)
+        for kp, b in enumerate(FIRST_TILE_BANKS):
+            turn(0, b, kp, 1)
+        turn(1, 1)
         weave(("p", 0, 0), "s", 0, SHARE_BESIDE_GPSIMD, tag="panel")
         weave(("p", 0, 0), "g", SHARE_BESIDE_GPSIMD)
         widen(2, 2)
@@ -332,7 +340,7 @@ def tile_protected_adapter_gradients_s13_kernel(
         widen(6, 2)
         weave(("p", 1, 0), "s", 0, SHARE_BESIDE_GPSIMD)
         turn_pair(2)
-        h_first_pair(0, (6, 7))
+        h_first_pair(0, FIRST_H_BANKS)
         turn_pair(3)
         widen(8, 2)
         for i in range(2):
@@ -367,7 +375,7 @@ def tile_protected_adapter_gradients_s13_kernel(
                 widen(2 * s + 4)
             if s + 1 < PAIRS:
                 turn_pair(s + 1)
-            if s == 5:
+            if s == Z_STEP:
                 z_group(0)
             weave(job, "g")
             scale_pair(s)
@@ -378,7 +386,7 @@ def tile_protected_adapter_gradients_s13_kernel(
             if s + 2 < PAIRS:
                 widen_sorted(2 * s + 5)
             quant(job)
-            if s == 5:
+            if s == Z_STEP:
                 z_group(1)
             quant_pair(s)
         banks[:0] = [TURN_BANK[PAIRS - 1], TURN_BANK[PAIRS - 1] + 1]

@@ -25,26 +25,13 @@ GROUPS = M // PASS
 PAIRS = GROUPS * T4 // 2
 KP = K // PASS
 HALF = 512
-PIECE = 256
-
-SHARE_BESIDE_GPSIMD = 256
-SHARE_BESIDE_VECTOR = 128
-SCALAR_PIECES = 3
-EARLY_HALVES = 4
-OPEN_BLOCKS = 2
-FIRST_SORTED_PAIR = 5
-Z_STEP = 5
 
 MOVING_SCALES_AT = 128
-
-TURN_BANK = {2: 4, 3: 0, 4: 6, 5: 0, 6: 6, 7: 0}
-MM_BANKS = (4, 5, 2, 3)
-FIRST_TILE_BANKS = (0, 6)
-FIRST_H_BANKS = (6, 7)
-
-WEAVE_BUFS = {"weave_v": 4, "weave_s": 4, "weave_g": 1, "panel": 1}
-WIDE_BUFS = {1: 3, 2: 2}
+WEAVE_BUFS = {"weave_v": 4, "weave_s": 3, "weave_g": 1, "panel": 1}
+WIDE_BUFS = {1: 2, 2: 2}
+SORTED_BUFS = 4
 RESULT_BUFS = {HALF: 5, R: 6, P: 2}
+PIECE = 256
 
 
 def tile_protected_adapter_gradients_s13_kernel(
@@ -80,6 +67,7 @@ def tile_protected_adapter_gradients_s13_kernel(
         aq = {kp: mx_tiles("a%d" % kp, R, MOVING_SCALES_AT) for kp in range(KP)}
         hq = {g: mx_tiles("h%d" % g, K) for g in range(GROUPS)}
         zq = {g: mx_tiles("z%d" % g, R) for g in range(GROUPS)}
+        xq = {s: mx_tiles("x%d" % (2 * s), 2 * KP * P) for s in range(PAIRS)}
 
         planes = {}
         woven = {}
@@ -102,23 +90,33 @@ def tile_protected_adapter_gradients_s13_kernel(
             planes["p", c, kp] = w[:]
             target["p", c, kp] = (pq[c, kp], 0)
 
+        def load_a():
+            a_raw = keep.tile([P, KP, T4, R], BF16, name="a_raw")
+            nc.sync.dma_start(out=a_raw[:], in_=a.rearrange("(a p j) n -> p a j n", p=P, j=T4))
+            for kp in range(KP):
+                planes["a", kp] = a_raw[:, kp]
+                target["a", kp] = (aq[kp], 0)
+
+        def load_scales():
+            nc.sync.dma_start(out=sc_col[:, :, :T4], in_=x_scale.rearrange("o (a p j) -> p (o a) j", p=P, j=T4))
+
+        def load_r():
+            nc.sync.dma_start(out=r16[:, :, :T4], in_=r.rearrange("(g p t) -> p g t", p=P, t=T4))
+
         load_x(0, 1)
         load_x(1, 1)
-        nc.sync.dma_start(out=sc_col[:, :, :T4], in_=x_scale.rearrange("o (a p j) -> p (o a) j", p=P, j=T4))
-        load_panel(0, 0)
+        load_scales()
         load_x(2, 2)
+        load_panel(0, 0)
         load_panel(0, 1)
-        load_x(4, 4)
-        nc.sync.dma_start(out=r16[:, :, :T4], in_=r.rearrange("(g p t) -> p g t", p=P, t=T4))
+        load_x(4, 2)
         load_panel(1, 0)
-        load_x(8, 2)
+        load_x(6, 2)
+        load_r()
         load_panel(1, 1)
+        load_x(8, 2)
+        load_a()
         load_x(10, 2)
-        a_raw = keep.tile([P, KP, T4, R], BF16, name="a_raw")
-        nc.sync.dma_start(out=a_raw[:], in_=a.rearrange("(a p j) n -> p a j n", p=P, j=T4))
-        for kp in range(KP):
-            planes["a", kp] = a_raw[:, kp]
-            target["a", kp] = (aq[kp], 0)
         load_x(12, 4)
 
         nc.vector.memset(half[:], 0.5)
@@ -138,14 +136,11 @@ def tile_protected_adapter_gradients_s13_kernel(
                     in_=rows[:, 4 * q : 4 * q + 4, :].bitcast(I32).rearrange("g q n -> q g n"),
                 )
 
-        def bank_tile(b, shape):
-            return psum.tile(shape, F32, name="bank%d" % b)
+        free_banks = list(range(8))
 
-        banks = list(MM_BANKS)
-
-        def mm_bank():
-            banks.append(banks.pop(0))
-            return banks[-1]
+        def take_bank(shape):
+            b = free_banks.pop(0)
+            return b, psum.tile(shape, F32, name="bank%d" % b)
 
         def mx(out, lhs, lcols, rhs, rhs_scale, start, stop):
             nc.tensor.matmul_mx(
@@ -181,10 +176,10 @@ def tile_protected_adapter_gradients_s13_kernel(
                 copy = nc.vector.tensor_copy if who == "v" else nc.scalar.copy
                 copy(out=out.rearrange("p (n i) t -> p n t i", i=4), in_=in_.rearrange("p t (n i) -> p n t i", i=4))
 
+        x_wide = {}
         x_words = {}
         x_banks = {}
         x_woven = {}
-        xq = {}
 
         def x_fp8(i, count):
             xt, t = x_in[i]
@@ -200,51 +195,61 @@ def tile_protected_adapter_gradients_s13_kernel(
             w = ring.tile([P, count * K], BF16, name="x_bf%d" % count, bufs=WIDE_BUFS[count])
             nc.scalar.copy(out=w[:], in_=x_fp8(i, count))
             for j in range(count):
+                x_wide[i + j] = w[:, j * K : (j + 1) * K]
                 for kp in range(KP):
                     for u in range(2):
                         w0 = 2 * P * (KP * j + kp)
                         x_words[i + j, kp, u] = w[:].bitcast(F32)[:, w0 + u : w0 + 2 * P : 2]
 
+        def sorted_tile(i):
+            w = ring.tile([P, K], BF16, name="x_sorted", bufs=SORTED_BUFS)
+            for kp in range(KP):
+                for u in range(2):
+                    x_words[i, kp, u] = w[:].bitcast(F32)[:, (u * KP + kp) * P : (u * KP + kp + 1) * P]
+            return w
+
         def widen_sorted(i):
-            w = ring.tile([P, K], BF16, name="x_sorted")
             nc.vector.tensor_scalar(
-                out=w[:].rearrange("p (u w e) -> p w u e", u=2, e=2),
+                out=sorted_tile(i)[:].rearrange("p (u w e) -> p w u e", u=2, e=2),
                 in0=x_fp8(i, 1),
                 scalar1=one[:],
                 scalar2=None,
                 op0=MULT,
             )
-            for kp in range(KP):
-                for u in range(2):
-                    x_words[i, kp, u] = w[:].bitcast(F32)[:, (u * KP + kp) * P : (u * KP + kp + 1) * P]
 
-        def turn(i, b, kp0=0, passes=KP):
-            bank = bank_tile(b, [P, 2, passes, P])
-            x_banks.setdefault(i, []).append((bank, kp0, passes))
+        def sort_words(i):
+            nc.vector.tensor_copy(
+                out=sorted_tile(i)[:].rearrange("p (u w e) -> p u w e", u=2, e=2),
+                in_=x_wide[i].rearrange("p (w u e) -> p u w e", u=2, e=2),
+            )
+
+        def turn(i, kp0=0, passes=KP):
+            b, bank = take_bank([P, 2, passes, P])
+            x_banks.setdefault(i, []).append((b, bank, kp0, passes))
             for kp in range(passes):
                 for u in range(2):
                     nc.tensor.transpose(bank[:, u, kp, :], x_words[i, kp0 + kp, u], ident[:])
 
-        def turn_pair(s):
-            for j in range(2):
-                turn(2 * s + j, TURN_BANK[s] + j)
-
-        def scale_pair(s):
-            x_woven[s] = ring.tile([P, 2, KP * P * T4], BF16, name="x_gr", align_bytes=64)
-            xq[s] = mx_tiles("x%d" % (2 * s), 2 * KP * P)
-            for j in range(2):
-                for bank, kp0, passes in x_banks[2 * s + j]:
-                    scales = sc_col[:, kp0 : kp0 + passes, :T4].rearrange("p a (o u e) -> p a o u e", o=1, e=2)
-                    values = x_woven[s][:, j, kp0 * PASS : (kp0 + passes) * PASS]
-                    nc.vector.tensor_tensor(
-                        out=values.rearrange("p (a m u e) -> p a m u e", a=passes, u=2, e=2),
-                        in0=bank[:].bitcast(BF16).rearrange("p u a (m e) -> p a m u e", e=2),
-                        in1=scales.to_broadcast([P, passes, P, 2, 2]),
-                        op=MULT,
-                    )
+        def scale(i):
+            s, j = divmod(i, 2)
+            if j == 0:
+                x_woven[s] = ring.tile([P, 2, KP * P * T4], BF16, name="x_gr", align_bytes=64)
+            for b, bank, kp0, passes in x_banks[i]:
+                scales = sc_col[:, kp0 : kp0 + passes, :T4].rearrange("p a (o u e) -> p a o u e", o=1, e=2)
+                values = x_woven[s][:, j, kp0 * PASS : (kp0 + passes) * PASS]
+                nc.vector.tensor_tensor(
+                    out=values.rearrange("p (a m u e) -> p a m u e", a=passes, u=2, e=2),
+                    in0=bank[:].bitcast(BF16).rearrange("p u a (m e) -> p a m u e", e=2),
+                    in1=scales.to_broadcast([P, passes, P, 2, 2]),
+                    op=MULT,
+                )
+                free_banks.append(b)
 
         def quant_pair(s):
             quantise(xq[s], 0, x_woven[s][:].rearrange("p j n -> p (j n)"))
+
+        def quant_tile(i):
+            quantise(xq[i // 2], (i % 2) * KP * P, x_woven[i // 2][:, i % 2])
 
         def x_mx(out, i, kp, weights, cols):
             c0 = ((i % 2) * KP + kp) * P
@@ -253,34 +258,30 @@ def tile_protected_adapter_gradients_s13_kernel(
 
         h_bank = {}
         h_planes = {}
+        z_bank = {}
         z_planes = {}
 
-        def h_pass(i, c, kp, b):
+        def h_pass(i, c, kp):
             if kp == 0:
-                h_bank[i, c] = bank_tile(b, [P, HALF])
-            x_mx(h_bank[i, c][:], i, kp, pq[c, kp], slice(0, HALF))
+                h_bank[i, c] = take_bank([P, HALF])
+            x_mx(h_bank[i, c][1][:], i, kp, pq[c, kp], slice(0, HALF))
 
         def h_out(i, c):
             g, t = divmod(i, T4)
             if t == 0:
                 name = "h_pl%d%d" % (g, c) if g < 2 else "p_raw%d%d" % (g - 2, c)
                 h_planes[g, c] = keep.tile([P, T4, HALF], BF16, name=name)
-            nc.scalar.activation(out=h_planes[g, c][:, t, :], in_=h_bank[i, c][:], func=COPY, scale=r32[:, g, t : t + 1])
+            b, bank = h_bank[i, c]
+            nc.scalar.activation(out=h_planes[g, c][:, t, :], in_=bank[:], func=COPY, scale=r32[:, g, t : t + 1])
+            free_banks.append(b)
 
-        def h_mm(i, c, b):
+        def h_passes(i, c):
             for kp in range(KP):
-                h_pass(i, c, kp, b)
+                h_pass(i, c, kp)
+
+        def h_mm(i, c):
+            h_passes(i, c)
             h_out(i, c)
-
-        def h_first_pair(c, two_banks):
-            for kp in range(KP):
-                for i in range(2):
-                    h_pass(i, c, kp, two_banks[i])
-
-        def h_pair(s):
-            for i in (2 * s, 2 * s + 1):
-                for c in range(2):
-                    h_mm(i, c, mm_bank())
 
         def h_piece(g, lo, hi):
             c, n0 = divmod(lo, HALF)
@@ -289,142 +290,199 @@ def tile_protected_adapter_gradients_s13_kernel(
             target[key] = (hq[g], lo)
             return key
 
-        def z_group(g):
-            z_planes[g] = keep.tile([P, T4, R], BF16, name="z_pl%d" % g)
-            planes["z", g] = z_planes[g][:]
-            target["z", g] = (zq[g], 0)
-            for t0 in (0, 2):
-                bank = bank_tile(mm_bank(), [P, 2, R])
-                for j in range(2):
-                    for kp in range(KP):
-                        x_mx(bank[:, j, :], T4 * g + t0 + j, kp, aq[kp], slice(0, R))
-                for j in range(2):
-                    t = t0 + j
-                    nc.scalar.activation(out=z_planes[g][:, t, :], in_=bank[:, j, :], func=COPY, scale=r32[:, g, t : t + 1])
+        def z_pair(s):
+            g, t0 = divmod(2 * s, T4)
+            if t0 == 0:
+                z_planes[g] = keep.tile([P, T4, R], BF16, name="z_pl%d" % g)
+                planes["z", g] = z_planes[g][:]
+                target["z", g] = (zq[g], 0)
+            b, bank = take_bank([P, 2, R])
+            for j in range(2):
+                for kp in range(KP):
+                    x_mx(bank[:, j, :], 2 * s + j, kp, aq[kp], slice(0, R))
+            for j in range(2):
+                t = t0 + j
+                nc.scalar.activation(out=z_planes[g][:, t, :], in_=bank[:, j, :], func=COPY, scale=r32[:, g, t : t + 1])
+            free_banks.append(b)
 
-        def second_stage(lhs, words, scales, width, to, blocks, copy=nc.scalar.copy):
-            block_banks = [bank_tile(mm_bank(), [P, width]) for block in blocks]
-            for groups in (range(GROUPS - 1), (GROUPS - 1,)):
-                for (r0, c0), bank in zip(blocks, block_banks):
-                    for g in groups:
-                        rhs = words[:, g, 2 * c0 : 2 * (c0 + width)].bitcast(E2M1X4)
-                        mx(bank[:], lhs[g], slice(r0, r0 + P), rhs, scales[:, g, c0 : c0 + width], g == 0, g == GROUPS - 1)
-            for (r0, c0), bank in zip(blocks, block_banks):
-                result = ring.tile([P, width], F32, name="res%d" % width, bufs=RESULT_BUFS[width])
-                copy(out=result[:], in_=bank[:])
-                nc.sync.dma_start(out=to[r0 : r0 + P, c0 : c0 + width], in_=result[:])
+        block_bank = {}
 
+        def block_passes(job, groups):
+            (lhs, words, scales, to), r0, c0, width = job
+            key = (r0, c0, to.shape[1])
+            if key not in block_bank:
+                block_bank[key] = take_bank([P, width])
+            for g in groups:
+                rhs = words[:, g, 2 * c0 : 2 * (c0 + width)].bitcast(E2M1X4)
+                mx(block_bank[key][1][:], lhs[g], slice(r0, r0 + P), rhs, scales[:, g, c0 : c0 + width], g == 0, g == GROUPS - 1)
+
+        def block_out(job, copy=nc.scalar.copy):
+            (lhs, words, scales, to), r0, c0, width = job
+            b, bank = block_bank[r0, c0, to.shape[1]]
+            result = ring.tile([P, width], F32, name="res%d" % width, bufs=RESULT_BUFS[width])
+            copy(out=result[:], in_=bank[:])
+            free_banks.append(b)
+            nc.sync.dma_start(out=to[r0 : r0 + P, c0 : c0 + width], in_=result[:])
+
+        def block(job, copy=nc.scalar.copy):
+            block_passes(job, range(GROUPS))
+            block_out(job, copy)
+
+        grad_b = [((zq, dw, ds, out_1), r0, c0, HALF) for r0 in range(0, R, P) for c0 in range(0, N, HALF)]
+        grad_a = [((hq, ew, es, out_0), r0, 0, R) for r0 in range(0, K, P)]
 
         for kp in range(KP):
             widen_first(kp)
         widen_sorted(1)
-        for kp, b in enumerate(FIRST_TILE_BANKS):
-            turn(0, b, kp, 1)
-        turn(1, 1)
-        weave(("p", 0, 0), "s", 0, SHARE_BESIDE_GPSIMD, tag="panel")
-        weave(("p", 0, 0), "g", SHARE_BESIDE_GPSIMD)
+        for kp in range(KP):
+            turn(0, kp, 1)
+        turn(1)
         widen(2, 2)
-        for i in range(2, 4):
-            turn(i, i)
-        scale_pair(0)
-        weave(("p", 0, 1), "s", 0, SHARE_BESIDE_VECTOR, tag="weave_g")
-        weave(("p", 0, 1), "v", SHARE_BESIDE_VECTOR)
-        widen(4)
-        widen(5)
-        quant(("p", 0, 0))
-        quant(("p", 0, 1))
-        weave(("p", 1, 0), "g", SHARE_BESIDE_GPSIMD)
+        turn(2)
+        turn(3)
+        weave(("p", 0, 0), "s", 0, 256, tag="weave_g")
+        weave(("p", 0, 0), "g", 256)
+        for i in range(3):
+            scale(i)
+        weave(("p", 0, 1), "s", 0, 256, tag="panel")
+        widen(4, 2)
         quant_pair(0)
-        scale_pair(1)
+        quant(("p", 0, 0))
+        weave(("p", 0, 1), "v", 256)
+        h_pass(0, 0, 0)
+        h_pass(1, 0, 0)
+        turn(4)
+        turn(5)
+        weave(("p", 1, 0), "g", 384, tag="weave_g")
+        scale(3)
         nc.vector.tensor_copy(out=r32[:], in_=r16[:, :, :T4])
+        quant(("p", 0, 1))
+        h_pass(0, 0, 1)
+        h_pass(1, 0, 1)
         widen(6, 2)
-        weave(("p", 1, 0), "s", 0, SHARE_BESIDE_GPSIMD)
-        turn_pair(2)
-        h_first_pair(0, FIRST_H_BANKS)
-        turn_pair(3)
-        widen(8, 2)
-        for i in range(2):
-            h_out(i, 0)
-
-        quant(("p", 1, 0))
-        weave(("p", 1, 1), "g", SHARE_BESIDE_GPSIMD)
-        weave(("p", 1, 1), "s", 0, SHARE_BESIDE_GPSIMD)
         quant_pair(1)
-        scale_pair(2)
-        for i in (2, 3):
-            h_mm(i, 0, i)
-        turn_pair(4)
-        quant(("p", 1, 1))
-        weave(("a", 0), "g")
+        weave(("p", 1, 1), "g", 192, tag="panel")
+        scale(4)
+        scale(5)
+        weave(("p", 1, 0), "s", 0, 256)
+        widen(8, 2)
+        h_passes(2, 0)
+        h_passes(3, 0)
+        for i in range(6, 10):
+            turn(i)
+        weave(("p", 1, 0), "v", 256, 384)
         quant_pair(2)
-        scale_pair(3)
-        widen(2 * FIRST_SORTED_PAIR)
-        h_first_pair(1, (mm_bank(), mm_bank()))
-        for i in range(2):
-            h_out(i, 1)
-        for i in (2, 3):
-            h_mm(i, 1, mm_bank())
-        h_pair(2)
-        widen_sorted(2 * FIRST_SORTED_PAIR + 1)
-        quant(("a", 0))
+        weave(("p", 1, 1), "v", 0, 192)
+        quant(("p", 1, 0))
+        weave(("a", 0), "g")
+        quant(("p", 1, 1))
+        for i in range(4):
+            h_out(i, 0)
+        widen(10)
+        h_mm(4, 0)
+        h_mm(5, 0)
+        scale(6)
+        h_mm(0, 1)
+        h_mm(1, 1)
+        scale(7)
+        for i in range(2, 6):
+            h_mm(i, 1)
+        jobs = [("a", 0), ("a", 1), h_piece(0, 0, PIECE), ("z", 0), ("z", 1)]
+        late_h = []
+        quant(jobs[0])
+        weave(jobs[1], "g")
         quant_pair(3)
-
-        pool_jobs = [("a", 1), h_piece(0, 0, PIECE), ("z", 0), ("z", 1)]
-        for s, job in zip(range(4, PAIRS), pool_jobs):
-            if s + 2 < PAIRS:
-                widen(2 * s + 4)
-            if s + 1 < PAIRS:
-                turn_pair(s + 1)
-            if s == Z_STEP:
-                z_group(0)
-            weave(job, "g")
-            scale_pair(s)
-            if s == PAIRS - 1:
-                banks[:0] = [TURN_BANK[s - 1], TURN_BANK[s - 1] + 1]
-                z_group(2)
-            h_pair(s - 1)
-            if s + 2 < PAIRS:
-                widen_sorted(2 * s + 5)
-            quant(job)
-            if s == Z_STEP:
-                z_group(1)
-            quant_pair(s)
-        banks[:0] = [TURN_BANK[PAIRS - 1], TURN_BANK[PAIRS - 1] + 1]
-        z_group(3)
-
-        first_pieces = [h_piece(1, 0, HALF), h_piece(0, PIECE, HALF)]
-        weave(("z", 2), "v")
-        weave(first_pieces[0], "v")
-        quant(("z", 2))
-        weave(first_pieces[1], "v")
-        weave(("z", 3), "v")
-        quant(first_pieces[1])
-        quant(("z", 3))
-        h_pair(PAIRS - 1)
-        by_scalar = [h_piece(g, K - PIECE, K) for g in range(SCALAR_PIECES)]
-        pieces = [h_piece(g, 0, HALF) for g in range(2, GROUPS)]
+        widen(12)
+        for c in range(2):
+            for i in (6, 7):
+                h_mm(i, c)
+        scale(8)
+        scale(9)
+        sort_words(10)
+        quant_pair(4)
+        widen_sorted(11)
+        sort_words(12)
+        quant(jobs[1])
+        weave(jobs[2], "g")
+        widen_sorted(13)
+        widen(14)
+        for i in (8, 9):
+            h_mm(i, 0)
+        turn(10)
+        turn(11)
+        z_pair(0)
+        z_pair(1)
+        for i in (8, 9):
+            h_mm(i, 1)
+        scale(10)
+        turn(12)
+        turn(13)
+        scale(11)
+        sort_words(14)
+        quant_pair(5)
+        quant(jobs[2])
+        weave(jobs[3], "g")
+        widen_sorted(15)
+        z_pair(2)
+        z_pair(3)
+        for i in (10, 11):
+            h_mm(i, 0)
+        turn(14)
+        turn(15)
+        for i in (10, 11):
+            h_mm(i, 1)
+        scale(12)
+        scale(13)
+        quant(jobs[3])
+        quant_pair(6)
+        weave(jobs[4], "g")
+        z_pair(4)
+        z_pair(5)
+        z_pair(6)
+        for c in range(2):
+            for i in (12, 13):
+                h_passes(i, c)
+        h_out(12, 0)
+        h_out(13, 0)
+        scale(14)
+        scale(15)
+        quant(jobs[4])
+        quant_pair(7)
+        z_pair(7)
+        h_out(12, 1)
+        h_out(13, 1)
+        for c in range(2):
+            for i in (14, 15):
+                h_mm(i, c)
+        by_scalar = [h_piece(g, K - PIECE, K) for g in range(2)]
+        halves = [(key, "s", h * P, (h + 1) * P) for key in by_scalar for h in range(2)]
+        first = [("z", 2), h_piece(0, PIECE, HALF), ("z", 3), h_piece(1, 0, HALF), h_piece(2, 0, HALF)]
+        weave(first[0], "v")
+        for before, key in zip(first, first[1:]):
+            weave(key, "v")
+            quant(before)
+        for job in grad_b[:2]:
+            block_passes(job, range(3))
+        for job in grad_b[:2]:
+            block_passes(job, (3,))
+        for u, job in enumerate(grad_b):
+            if u >= 2:
+                block_passes(job, range(4))
+            block_out(job)
+            if 1 <= u <= len(late_h):
+                h_mm(*late_h[u - 1])
+            if 4 <= u < 4 + len(halves):
+                weave(*halves[u - 4])
+        pieces = [h_piece(3, 0, HALF)]
         pieces = pieces + [h_piece(g, HALF, K - PIECE) for g in range(GROUPS)]
-        pieces = pieces + [h_piece(g, K - PIECE, K) for g in range(SCALAR_PIECES, GROUPS)]
-        for before, key in zip(first_pieces[:1] + pieces, pieces):
+        pieces = pieces + [h_piece(g, K - PIECE, K) for g in range(len(by_scalar), GROUPS)]
+        for before, key in zip(first[-1:] + pieces, pieces):
             weave(key, "v")
             quant(before)
         quant(pieces[-1])
-
-        halves = [(key, "s", h * P, (h + 1) * P) for key in by_scalar for h in range(2)]
-        blocks = [(r0, c0) for r0 in range(0, R, P) for c0 in range(0, N, HALF)]
-        second_stage(zq, dw, ds, HALF, out_1, blocks[:OPEN_BLOCKS])
-        for u in range(len(blocks)):
-            if u >= OPEN_BLOCKS:
-                second_stage(zq, dw, ds, HALF, out_1, blocks[u : u + 1])
-            if u < EARLY_HALVES:
-                weave(*halves[u])
-        late = halves[EARLY_HALVES:]
-        for kb in range(K // P - 1):
-            if kb < len(late):
-                weave(*late[kb])
-            if kb == len(late):
-                for key in by_scalar:
-                    quant(key)
-            second_stage(hq, ew, es, R, out_0, [(kb * P, 0)])
+        for key in by_scalar:
+            quant(key)
+        for kb, job in enumerate(grad_a[:-1]):
+            block(job)
         for h, copy in enumerate((nc.scalar.copy, nc.vector.tensor_copy)):
-            second_stage(hq, ew, es, P, out_0, [(K - P, h * P)], copy)
+            block((grad_a[0][0], K - P, h * P, P), copy)

@@ -27,10 +27,10 @@ KP = K // PASS
 HALF = 512
 
 MOVING_SCALES_AT = 128
-WEAVE_BUFS = {"weave_v": 4, "weave_s": 3, "weave_g": 1, "panel": 1}
+WEAVE_BUFS = {"weave_v": 4, "weave_s": 3, "weave_g": 1, "panel": 2, "weave_h": 1}
 WIDE_BUFS = {1: 2, 2: 2}
 SORTED_BUFS = 4
-RESULT_BUFS = {HALF: 5, R: 6, P: 2}
+RESULT_BUFS = {HALF: 4, R: 7, P: 2}
 PIECE = 256
 
 
@@ -113,8 +113,8 @@ def tile_protected_adapter_gradients_s13_kernel(
         load_panel(1, 0)
         load_x(6, 2)
         load_r()
-        load_panel(1, 1)
         load_x(8, 2)
+        load_panel(1, 1)
         load_a()
         load_x(10, 2)
         load_x(12, 4)
@@ -180,13 +180,14 @@ def tile_protected_adapter_gradients_s13_kernel(
         x_words = {}
         x_banks = {}
         x_woven = {}
+        pair_woven = {}
 
         def x_fp8(i, count):
             xt, t = x_in[i]
             return xt[:, t * K : (t + count) * K].bitcast(E4M3)
 
         def widen_first(kp):
-            w = keep.tile([P, PASS], BF16, name="x_first%d" % kp)
+            w = ring.tile([P, PASS], BF16, name="x_bf1", bufs=WIDE_BUFS[1])
             nc.scalar.copy(out=w[:], in_=x_fp8(0, 1)[:, kp * PASS : (kp + 1) * PASS])
             for u in range(2):
                 x_words[0, kp, u] = w[:].bitcast(F32)[:, u::2]
@@ -230,13 +231,17 @@ def tile_protected_adapter_gradients_s13_kernel(
                 for u in range(2):
                     nc.tensor.transpose(bank[:, u, kp, :], x_words[i, kp0 + kp, u], ident[:])
 
-        def scale(i):
+        def scale(i, tag=None):
             s, j = divmod(i, 2)
-            if j == 0:
-                x_woven[s] = ring.tile([P, 2, KP * P * T4], BF16, name="x_gr", align_bytes=64)
+            if tag:
+                x_woven[i] = ring.tile([P, K], BF16, name=tag, align_bytes=64, bufs=WEAVE_BUFS[tag])[:]
+            else:
+                if j == 0:
+                    pair_woven[s] = ring.tile([P, 2, K], BF16, name="x_gr", align_bytes=64)
+                x_woven[i] = pair_woven[s][:, j]
             for b, bank, kp0, passes in x_banks[i]:
                 scales = sc_col[:, kp0 : kp0 + passes, :T4].rearrange("p a (o u e) -> p a o u e", o=1, e=2)
-                values = x_woven[s][:, j, kp0 * PASS : (kp0 + passes) * PASS]
+                values = x_woven[i][:, kp0 * PASS : (kp0 + passes) * PASS]
                 nc.vector.tensor_tensor(
                     out=values.rearrange("p (a m u e) -> p a m u e", a=passes, u=2, e=2),
                     in0=bank[:].bitcast(BF16).rearrange("p u a (m e) -> p a m u e", e=2),
@@ -246,10 +251,10 @@ def tile_protected_adapter_gradients_s13_kernel(
                 free_banks.append(b)
 
         def quant_pair(s):
-            quantise(xq[s], 0, x_woven[s][:].rearrange("p j n -> p (j n)"))
+            quantise(xq[s], 0, pair_woven[s][:].rearrange("p j n -> p (j n)"))
 
         def quant_tile(i):
-            quantise(xq[i // 2], (i % 2) * KP * P, x_woven[i // 2][:, i % 2])
+            quantise(xq[i // 2], (i % 2) * KP * P, x_woven[i])
 
         def x_mx(out, i, kp, weights, cols):
             c0 = ((i % 2) * KP + kp) * P
@@ -340,10 +345,11 @@ def tile_protected_adapter_gradients_s13_kernel(
         widen(2, 2)
         turn(2)
         turn(3)
-        weave(("p", 0, 0), "s", 0, 256, tag="weave_g")
+        weave(("p", 0, 0), "s", 0, 256, tag="panel")
         weave(("p", 0, 0), "g", 256)
-        for i in range(3):
-            scale(i)
+        scale(0)
+        scale(1)
+        scale(2, "weave_g")
         weave(("p", 0, 1), "s", 0, 256, tag="panel")
         widen(4, 2)
         quant_pair(0)
@@ -353,112 +359,124 @@ def tile_protected_adapter_gradients_s13_kernel(
         h_pass(1, 0, 0)
         turn(4)
         turn(5)
-        weave(("p", 1, 0), "g", 384, tag="weave_g")
-        scale(3)
-        nc.vector.tensor_copy(out=r32[:], in_=r16[:, :, :T4])
+        quant_tile(2)
         quant(("p", 0, 1))
+        weave(("p", 1, 0), "g", 64, tag="weave_g")
         h_pass(0, 0, 1)
         h_pass(1, 0, 1)
         widen(6, 2)
-        quant_pair(1)
-        weave(("p", 1, 1), "g", 192, tag="panel")
+        scale(3, "weave_v")
         scale(4)
         scale(5)
-        weave(("p", 1, 0), "s", 0, 256)
+        weave(("p", 1, 0), "s", 0, 64)
         widen(8, 2)
+        weave(("p", 1, 1), "s", 0, 256, tag="panel")
+        turn(6)
+        turn(7)
         h_passes(2, 0)
-        h_passes(3, 0)
-        for i in range(6, 10):
-            turn(i)
-        weave(("p", 1, 0), "v", 256, 384)
+        turn(8)
+        turn(9)
+        nc.vector.tensor_copy(out=r32[:], in_=r16[:, :, :T4])
+        quant_tile(3)
         quant_pair(2)
-        weave(("p", 1, 1), "v", 0, 192)
+        weave(("p", 1, 1), "v", 256)
         quant(("p", 1, 0))
         weave(("a", 0), "g")
         quant(("p", 1, 1))
-        for i in range(4):
+        for i in range(3):
             h_out(i, 0)
+        for i in range(3, 6):
+            h_mm(i, 0)
         widen(10)
-        h_mm(4, 0)
-        h_mm(5, 0)
-        scale(6)
+        scale(6, "weave_h")
         h_mm(0, 1)
         h_mm(1, 1)
-        scale(7)
+        scale(7, "weave_v")
         for i in range(2, 6):
             h_mm(i, 1)
         jobs = [("a", 0), ("a", 1), h_piece(0, 0, PIECE), ("z", 0), ("z", 1)]
         late_h = []
-        quant(jobs[0])
-        weave(jobs[1], "g")
-        quant_pair(3)
+        quant_tile(6)
+        weave(jobs[1], "g", tag="weave_h")
+        quant_tile(7)
+        scale(8)
+        scale(9)
         widen(12)
         for c in range(2):
             for i in (6, 7):
                 h_mm(i, c)
-        scale(8)
-        scale(9)
+        quant_tile(8)
+        quant_tile(9)
         sort_words(10)
-        quant_pair(4)
         widen_sorted(11)
+        quant(jobs[0])
         sort_words(12)
         quant(jobs[1])
-        weave(jobs[2], "g")
+        weave(jobs[2], "g", tag="weave_h")
         widen_sorted(13)
         widen(14)
-        for i in (8, 9):
-            h_mm(i, 0)
+        h_mm(8, 0)
+        h_mm(9, 0)
+        h_passes(8, 1)
         turn(10)
         turn(11)
+        scale(10)
+        scale(11)
         z_pair(0)
         z_pair(1)
-        for i in (8, 9):
-            h_mm(i, 1)
-        scale(10)
+        h_out(8, 1)
+        h_mm(9, 1)
         turn(12)
         turn(13)
-        scale(11)
         sort_words(14)
         quant_pair(5)
         quant(jobs[2])
-        weave(jobs[3], "g")
+        weave(jobs[3], "g", tag="weave_h")
         widen_sorted(15)
         z_pair(2)
+        scale(12)
         z_pair(3)
-        for i in (10, 11):
-            h_mm(i, 0)
+        h_mm(10, 0)
+        scale(13)
+        h_mm(11, 0)
         turn(14)
         turn(15)
+        quant_tile(12)
+        quant(jobs[3])
+        quant_tile(13)
+        weave(jobs[4], "g", tag="weave_h")
         for i in (10, 11):
             h_mm(i, 1)
-        scale(12)
-        scale(13)
-        quant(jobs[3])
-        quant_pair(6)
-        weave(jobs[4], "g")
+        scale(14)
         z_pair(4)
         z_pair(5)
+        scale(15)
         z_pair(6)
         for c in range(2):
             for i in (12, 13):
                 h_passes(i, c)
         h_out(12, 0)
         h_out(13, 0)
-        scale(14)
-        scale(15)
+        quant_tile(14)
+        quant_tile(15)
         quant(jobs[4])
-        quant_pair(7)
         z_pair(7)
         h_out(12, 1)
         h_out(13, 1)
         for c in range(2):
             for i in (14, 15):
                 h_mm(i, c)
-        by_scalar = [h_piece(g, K - PIECE, K) for g in range(2)]
+        by_scalar = [h_piece(g, K - PIECE, K) for g in range(3)]
         halves = [(key, "s", h * P, (h + 1) * P) for key in by_scalar for h in range(2)]
-        first = [("z", 2), h_piece(0, PIECE, HALF), ("z", 3), h_piece(1, 0, HALF), h_piece(2, 0, HALF)]
+        first = [("z", 2), h_piece(0, PIECE, HALF), ("z", 3), h_piece(1, 0, PIECE), h_piece(1, PIECE, HALF), h_piece(2, 0, HALF)]
         weave(first[0], "v")
-        for before, key in zip(first, first[1:]):
+        weave(first[1], "v")
+        quant(first[0])
+        quant(first[1])
+        weave(first[2], "v")
+        weave(first[3], "v")
+        quant(first[2])
+        for before, key in zip(first[3:], first[4:]):
             weave(key, "v")
             quant(before)
         for job in grad_b[:2]:
@@ -471,8 +489,8 @@ def tile_protected_adapter_gradients_s13_kernel(
             block_out(job)
             if 1 <= u <= len(late_h):
                 h_mm(*late_h[u - 1])
-            if 4 <= u < 4 + len(halves):
-                weave(*halves[u - 4])
+            if 2 <= u < 2 + len(halves):
+                weave(*halves[u - 2])
         pieces = [h_piece(3, 0, HALF)]
         pieces = pieces + [h_piece(g, HALF, K - PIECE) for g in range(GROUPS)]
         pieces = pieces + [h_piece(g, K - PIECE, K) for g in range(len(by_scalar), GROUPS)]

@@ -27,7 +27,7 @@ KP = K // PASS
 HALF = 512
 
 MOVING_SCALES_AT = 128
-WEAVE_BUFS = {"weave_v": 4, "weave_s": 3, "weave_g": 1, "panel": 2, "weave_h": 1}
+WEAVE_BUFS = {"weave_v": 4, "weave_s": 3, "weave_g": 1, "panel": 2, "weave_h": 1, "x_gr": 2}
 WIDE_BUFS = {1: 2, 2: 2}
 SORTED_BUFS = 4
 RESULT_BUFS = {HALF: 4, R: 7, P: 2}
@@ -105,15 +105,15 @@ def tile_protected_adapter_gradients_s13_kernel(
 
         load_x(0, 1)
         load_x(1, 1)
-        load_scales()
         load_x(2, 2)
+        load_scales()
+        load_x(4, 2)
         load_panel(0, 0)
         load_panel(0, 1)
-        load_x(4, 2)
-        load_panel(1, 0)
         load_x(6, 2)
-        load_r()
         load_x(8, 2)
+        load_panel(1, 0)
+        load_r()
         load_panel(1, 1)
         load_a()
         load_x(10, 2)
@@ -192,8 +192,11 @@ def tile_protected_adapter_gradients_s13_kernel(
             for u in range(2):
                 x_words[0, kp, u] = w[:].bitcast(F32)[:, u::2]
 
-        def widen(i, count=1):
-            w = ring.tile([P, count * K], BF16, name="x_bf%d" % count, bufs=WIDE_BUFS[count])
+        def widen(i, count=1, tag=None):
+            if tag:
+                w = ring.tile([P, count * K], BF16, name=tag, align_bytes=64, bufs=WEAVE_BUFS[tag])
+            else:
+                w = ring.tile([P, count * K], BF16, name="x_bf%d" % count, bufs=WIDE_BUFS[count])
             nc.scalar.copy(out=w[:], in_=x_fp8(i, count))
             for j in range(count):
                 x_wide[i + j] = w[:, j * K : (j + 1) * K]
@@ -231,13 +234,13 @@ def tile_protected_adapter_gradients_s13_kernel(
                 for u in range(2):
                     nc.tensor.transpose(bank[:, u, kp, :], x_words[i, kp0 + kp, u], ident[:])
 
-        def scale(i, tag=None):
+        def scale(i, tag=None, pair_tag="x_gr"):
             s, j = divmod(i, 2)
             if tag:
                 x_woven[i] = ring.tile([P, K], BF16, name=tag, align_bytes=64, bufs=WEAVE_BUFS[tag])[:]
             else:
                 if j == 0:
-                    pair_woven[s] = ring.tile([P, 2, K], BF16, name="x_gr", align_bytes=64)
+                    pair_woven[s] = ring.tile([P, 2, K], BF16, name=pair_tag, align_bytes=64, bufs=WEAVE_BUFS[pair_tag])
                 x_woven[i] = pair_woven[s][:, j]
             for b, bank, kp0, passes in x_banks[i]:
                 scales = sc_col[:, kp0 : kp0 + passes, :T4].rearrange("p a (o u e) -> p a o u e", o=1, e=2)
@@ -345,52 +348,56 @@ def tile_protected_adapter_gradients_s13_kernel(
         widen(2, 2)
         turn(2)
         turn(3)
+        widen(4, 2)
+        scale(0)
+        turn(4)
+        turn(5)
         weave(("p", 0, 0), "s", 0, 256, tag="panel")
         weave(("p", 0, 0), "g", 256)
-        scale(0)
         scale(1)
-        scale(2, "weave_g")
+        scale(2, pair_tag="weave_g")
+        scale(3)
         weave(("p", 0, 1), "s", 0, 256, tag="panel")
-        widen(4, 2)
+        widen(6, 2)
         quant_pair(0)
         quant(("p", 0, 0))
         weave(("p", 0, 1), "v", 256)
         h_pass(0, 0, 0)
         h_pass(1, 0, 0)
-        turn(4)
-        turn(5)
-        quant_tile(2)
-        quant(("p", 0, 1))
-        weave(("p", 1, 0), "g", 64, tag="weave_g")
-        h_pass(0, 0, 1)
-        h_pass(1, 0, 1)
-        widen(6, 2)
-        scale(3, "weave_v")
-        scale(4)
-        scale(5)
-        weave(("p", 1, 0), "s", 0, 64)
-        widen(8, 2)
-        weave(("p", 1, 1), "s", 0, 256, tag="panel")
         turn(6)
         turn(7)
+        quant_pair(1)
+        quant(("p", 0, 1))
+        weave(("p", 1, 0), "g", 224, tag="weave_g")
+        h_pass(0, 0, 1)
+        h_pass(1, 0, 1)
+        scale(4)
+        scale(5)
+        widen(8, 2, "weave_v")
+        nc.scalar.copy(out=r32[:], in_=r16[:, :, :T4])
+        weave(("p", 1, 0), "s", 0, 224)
+        weave(("p", 1, 1), "s", 0, 256, tag="panel")
         h_passes(2, 0)
+        h_passes(3, 0)
         turn(8)
         turn(9)
-        nc.vector.tensor_copy(out=r32[:], in_=r16[:, :, :T4])
-        quant_tile(3)
-        quant_pair(2)
+
         weave(("p", 1, 1), "v", 256)
+        quant_pair(2)
         quant(("p", 1, 0))
         weave(("a", 0), "g")
         quant(("p", 1, 1))
-        for i in range(3):
+        for i in range(4):
             h_out(i, 0)
-        for i in range(3, 6):
+        for i in range(4, 6):
             h_mm(i, 0)
         widen(10)
         scale(6, "weave_h")
-        h_mm(0, 1)
-        h_mm(1, 1)
+        for kp in range(KP):
+            for i in range(2):
+                h_pass(i, 1, kp)
+        h_out(0, 1)
+        h_out(1, 1)
         scale(7, "weave_v")
         for i in range(2, 6):
             h_mm(i, 1)
@@ -414,7 +421,6 @@ def tile_protected_adapter_gradients_s13_kernel(
         quant(jobs[1])
         weave(jobs[2], "g", tag="weave_h")
         widen_sorted(13)
-        widen(14)
         h_mm(8, 0)
         h_mm(9, 0)
         h_passes(8, 1)
@@ -423,28 +429,28 @@ def tile_protected_adapter_gradients_s13_kernel(
         scale(10)
         scale(11)
         z_pair(0)
+        widen(14, 1, "weave_g")
         z_pair(1)
         h_out(8, 1)
         h_mm(9, 1)
-        turn(12)
-        turn(13)
+        quant_tile(10)
+        quant_tile(11)
         sort_words(14)
-        quant_pair(5)
-        quant(jobs[2])
-        weave(jobs[3], "g", tag="weave_h")
+        weave(jobs[3], "g", tag="weave_g")
         widen_sorted(15)
         z_pair(2)
-        scale(12)
+        turn(12)
+        turn(13)
+        scale(12, "panel")
         z_pair(3)
         h_mm(10, 0)
-        scale(13)
+        scale(13, "panel")
         h_mm(11, 0)
         turn(14)
         turn(15)
         quant_tile(12)
-        quant(jobs[3])
+        weave(jobs[4], "g", tag="panel")
         quant_tile(13)
-        weave(jobs[4], "g", tag="weave_h")
         for i in (10, 11):
             h_mm(i, 1)
         scale(14)
@@ -459,6 +465,7 @@ def tile_protected_adapter_gradients_s13_kernel(
         h_out(13, 0)
         quant_tile(14)
         quant_tile(15)
+        quant(jobs[3])
         quant(jobs[4])
         z_pair(7)
         h_out(12, 1)
@@ -468,17 +475,17 @@ def tile_protected_adapter_gradients_s13_kernel(
                 h_mm(i, c)
         by_scalar = [h_piece(g, K - PIECE, K) for g in range(3)]
         halves = [(key, "s", h * P, (h + 1) * P) for key in by_scalar for h in range(2)]
-        first = [("z", 2), h_piece(0, PIECE, HALF), ("z", 3), h_piece(1, 0, PIECE), h_piece(1, PIECE, HALF), h_piece(2, 0, HALF)]
+        first = [("z", 2), h_piece(0, PIECE, HALF), ("z", 3), h_piece(1, 0, HALF), h_piece(2, 0, HALF)]
         weave(first[0], "v")
-        weave(first[1], "v")
+        quant(jobs[2])
         quant(first[0])
-        quant(first[1])
+        weave(first[1], "v")
         weave(first[2], "v")
-        weave(first[3], "v")
+        quant(first[1])
         quant(first[2])
-        for before, key in zip(first[3:], first[4:]):
-            weave(key, "v")
-            quant(before)
+        weave(first[3], "v")
+        weave(first[4], "v")
+        quant(first[3])
         for job in grad_b[:2]:
             block_passes(job, range(3))
         for job in grad_b[:2]:

@@ -107,10 +107,11 @@ def tile_protected_adapter_gradients_s13_kernel(
         load_x(1, 1)
         load_x(2, 2)
         load_scales()
-        load_x(4, 2)
+        load_x(4, 1)
         load_panel(0, 0)
-        load_panel(0, 1)
+        load_x(5, 1)
         load_x(6, 2)
+        load_panel(0, 1)
         load_x(8, 2)
         load_panel(1, 0)
         load_r()
@@ -348,24 +349,27 @@ def tile_protected_adapter_gradients_s13_kernel(
         widen(2, 2)
         turn(2)
         turn(3)
-        widen(4, 2)
+        widen(4)
         scale(0)
         turn(4)
+        weave(("p", 0, 0), "s", 0, 128, tag="panel")
+        weave(("p", 0, 0), "g", 128, tag="panel")
+        widen(5)
         turn(5)
-        weave(("p", 0, 0), "s", 0, 256, tag="panel")
-        weave(("p", 0, 0), "g", 256)
         scale(1)
+        widen(6, 2)
         scale(2, pair_tag="weave_g")
         scale(3)
-        weave(("p", 0, 1), "s", 0, 256, tag="panel")
-        widen(6, 2)
-        quant_pair(0)
-        quant(("p", 0, 0))
-        weave(("p", 0, 1), "v", 256)
-        h_pass(0, 0, 0)
-        h_pass(1, 0, 0)
         turn(6)
         turn(7)
+        weave(("p", 0, 1), "s", 0, 320, tag="panel")
+        quant_pair(0)
+        quant(("p", 0, 0))
+        weave(("p", 0, 1), "v", 320)
+        h_pass(0, 0, 0)
+        h_pass(1, 0, 0)
+        widen(8, 2, "weave_v")
+
         quant_pair(1)
         quant(("p", 0, 1))
         weave(("p", 1, 0), "g", 224, tag="weave_g")
@@ -373,21 +377,21 @@ def tile_protected_adapter_gradients_s13_kernel(
         h_pass(1, 0, 1)
         scale(4)
         scale(5)
-        widen(8, 2, "weave_v")
         nc.scalar.copy(out=r32[:], in_=r16[:, :, :T4])
         weave(("p", 1, 0), "s", 0, 224)
         weave(("p", 1, 1), "s", 0, 256, tag="panel")
         h_passes(2, 0)
-        h_passes(3, 0)
         turn(8)
         turn(9)
-
+        for i in range(2):
+            h_out(i, 0)
+        h_passes(3, 0)
         weave(("p", 1, 1), "v", 256)
         quant_pair(2)
         quant(("p", 1, 0))
         weave(("a", 0), "g")
         quant(("p", 1, 1))
-        for i in range(4):
+        for i in range(2, 4):
             h_out(i, 0)
         for i in range(4, 6):
             h_mm(i, 0)

@@ -316,14 +316,14 @@ def tile_protected_adapter_gradients_s13_kernel(
 
         block_bank = {}
 
-        def block_passes(job, groups):
+        def block_passes(job, groups, last=GROUPS - 1):
             (lhs, words, scales, to), r0, c0, width = job
             key = (r0, c0, to.shape[1])
             if key not in block_bank:
                 block_bank[key] = take_bank([P, width])
             for g in groups:
                 rhs = words[:, g, 2 * c0 : 2 * (c0 + width)].bitcast(E2M1X4)
-                mx(block_bank[key][1][:], lhs[g], slice(r0, r0 + P), rhs, scales[:, g, c0 : c0 + width], g == 0, g == GROUPS - 1)
+                mx(block_bank[key][1][:], lhs[g], slice(r0, r0 + P), rhs, scales[:, g, c0 : c0 + width], g == 0, g == last)
 
         def block_out(job, copy=nc.scalar.copy):
             (lhs, words, scales, to), r0, c0, width = job
@@ -333,8 +333,8 @@ def tile_protected_adapter_gradients_s13_kernel(
             free_banks.append(b)
             nc.sync.dma_start(out=to[r0 : r0 + P, c0 : c0 + width], in_=result[:])
 
-        def block(job, copy=nc.scalar.copy):
-            block_passes(job, range(GROUPS))
+        def block(job, copy=nc.scalar.copy, order=range(GROUPS)):
+            block_passes(job, order, order[-1])
             block_out(job, copy)
 
         grad_b = [((zq, dw, ds, out_1), r0, c0, HALF) for r0 in range(0, R, P) for c0 in range(0, N, HALF)]
@@ -352,8 +352,8 @@ def tile_protected_adapter_gradients_s13_kernel(
         widen(4)
         scale(0)
         turn(4)
-        weave(("p", 0, 0), "s", 0, 128, tag="panel")
-        weave(("p", 0, 0), "g", 128, tag="panel")
+        weave(("p", 0, 0), "s", 0, 160, tag="panel")
+        weave(("p", 0, 0), "g", 160, tag="panel")
         widen(5)
         turn(5)
         scale(1)
@@ -372,13 +372,13 @@ def tile_protected_adapter_gradients_s13_kernel(
 
         quant_pair(1)
         quant(("p", 0, 1))
-        weave(("p", 1, 0), "g", 224, tag="weave_g")
+        weave(("p", 1, 0), "g", 240, tag="weave_g")
         h_pass(0, 0, 1)
         h_pass(1, 0, 1)
         scale(4)
         scale(5)
         nc.scalar.copy(out=r32[:], in_=r16[:, :, :T4])
-        weave(("p", 1, 0), "s", 0, 224)
+        weave(("p", 1, 0), "s", 0, 240)
         weave(("p", 1, 1), "s", 0, 256, tag="panel")
         h_passes(2, 0)
         turn(8)
@@ -406,7 +406,6 @@ def tile_protected_adapter_gradients_s13_kernel(
         for i in range(2, 6):
             h_mm(i, 1)
         jobs = [("a", 0), ("a", 1), h_piece(0, 0, PIECE), ("z", 0), ("z", 1)]
-        late_h = []
         quant_tile(6)
         weave(jobs[1], "g", tag="weave_h")
         quant_tile(7)
@@ -490,17 +489,14 @@ def tile_protected_adapter_gradients_s13_kernel(
         weave(first[3], "v")
         weave(first[4], "v")
         quant(first[3])
-        for job in grad_b[:2]:
-            block_passes(job, range(3))
-        for job in grad_b[:2]:
-            block_passes(job, (3,))
+        for g in range(GROUPS):
+            for job in grad_b[:2]:
+                block_passes(job, (g,))
         for u, job in enumerate(grad_b):
             if u >= 2:
                 block_passes(job, range(4))
             block_out(job)
-            if 1 <= u <= len(late_h):
-                h_mm(*late_h[u - 1])
-            if 2 <= u < 2 + len(halves):
+            if 2 <= u < 1 + len(halves):
                 weave(*halves[u - 2])
         pieces = [h_piece(3, 0, HALF)]
         pieces = pieces + [h_piece(g, HALF, K - PIECE) for g in range(GROUPS)]
@@ -508,10 +504,13 @@ def tile_protected_adapter_gradients_s13_kernel(
         for before, key in zip(first[-1:] + pieces, pieces):
             weave(key, "v")
             quant(before)
+        quant(by_scalar[0])
         quant(pieces[-1])
-        for key in by_scalar:
-            quant(key)
+        quant(by_scalar[1])
         for kb, job in enumerate(grad_a[:-1]):
-            block(job)
+            if kb == 2:
+                weave(*halves[-1])
+                quant(by_scalar[2])
+            block(job, order=(0, 3, 1, 2) if kb == 6 else range(GROUPS))
         for h, copy in enumerate((nc.scalar.copy, nc.vector.tensor_copy)):
             block((grad_a[0][0], K - P, h * P, P), copy)

@@ -24,14 +24,26 @@ PASS = P * T4
 GROUPS = M // PASS
 PAIRS = GROUPS * T4 // 2
 KP = K // PASS
+BANKS = 8
 HALF = 512
-
-MOVING_SCALES_AT = 128
-WEAVE_BUFS = {"weave_v": 4, "weave_s": 3, "weave_g": 1, "panel": 2, "weave_h": 1, "x_gr": 2}
-WIDE_BUFS = {1: 2, 2: 2}
-SORTED_BUFS = 4
-RESULT_BUFS = {HALF: 4, R: 7, P: 2}
 PIECE = 256
+
+SCALAR_COLUMNS = {(0, 0): 128, (0, 1): 320, (1, 0): 224, (1, 1): 256}
+SCALAR_PIECES = 3
+OPEN_BLOCKS = 2
+
+RING_BUFS = {
+    "weave_v": 4,
+    "weave_s": SCALAR_PIECES,
+    "weave_g": 1,
+    "weave_h": 1,
+    "panel": 2,
+    "x_pair": 2,
+    "x_wide1": 2,
+    "x_wide2": 2,
+    "x_sorted": 4,
+}
+RESULT_BUFS = {HALF: 4, R: K // P - 1, P: 2}
 
 
 def tile_protected_adapter_gradients_s13_kernel(
@@ -47,24 +59,24 @@ def tile_protected_adapter_gradients_s13_kernel(
         r16 = keep.tile([P, GROUPS, 4 * T4], BF16, name="r16")
         sc_col = keep.tile([P, KP, 2 * T4], F32, name="sc_col")
         ident = keep.tile([P, P], F32, name="ident")
-        half = keep.tile([P, 1], F32, name="half")
+        point_five = keep.tile([P, 1], F32, name="point_five")
         one = keep.tile([P, 1], F32, name="one")
-
-        def scale_tile(name, width, lead):
-            return keep.tile([P, lead + width], U8, name=name, align_bytes=256)[:, lead:]
-
-        es = scale_tile("es", GROUPS * R, MOVING_SCALES_AT).rearrange("p (g n) -> p g n", n=R)
-        ds = scale_tile("ds", GROUPS * N, MOVING_SCALES_AT).rearrange("p (g n) -> p g n", n=N)
+        es = keep.tile([P, GROUPS, R], U8, name="es", align_bytes=256)
+        ds = keep.tile([P, GROUPS, N], U8, name="ds", align_bytes=256)
         r32 = keep.tile([P, GROUPS, T4], F32, name="r32")
         ew = keep.tile([P, GROUPS, 2 * R], U8, name="ew", align_bytes=256)
         dw = keep.tile([P, GROUPS, 2 * N], U8, name="dw", align_bytes=256)
 
-        def mx_tiles(name, width, lead=0):
+        def mx_tiles(name, width):
             codes = keep.tile([P, width], U32, name=name + "_q", align_bytes=256)
-            return codes, scale_tile(name + "_s", width, lead)
+            scales = keep.tile([P, width], U8, name=name + "_s", align_bytes=256)
+            return codes, scales
 
-        pq = {(c, kp): mx_tiles("p%d%d" % (c, kp), HALF, MOVING_SCALES_AT) for c in range(2) for kp in range(KP)}
-        aq = {kp: mx_tiles("a%d" % kp, R, MOVING_SCALES_AT) for kp in range(KP)}
+        def ring_tile(name, shape):
+            return ring.tile(shape, BF16, name=name, align_bytes=64, bufs=RING_BUFS[name])
+
+        pq = {(c, kp): mx_tiles("p%d%d" % (c, kp), HALF) for c in range(2) for kp in range(KP)}
+        aq = {kp: mx_tiles("a%d" % kp, R) for kp in range(KP)}
         hq = {g: mx_tiles("h%d" % g, K) for g in range(GROUPS)}
         zq = {g: mx_tiles("z%d" % g, R) for g in range(GROUPS)}
         xq = {s: mx_tiles("x%d" % (2 * s), 2 * KP * P) for s in range(PAIRS)}
@@ -90,23 +102,10 @@ def tile_protected_adapter_gradients_s13_kernel(
             planes["p", c, kp] = w[:]
             target["p", c, kp] = (pq[c, kp], 0)
 
-        def load_a():
-            a_raw = keep.tile([P, KP, T4, R], BF16, name="a_raw")
-            nc.sync.dma_start(out=a_raw[:], in_=a.rearrange("(a p j) n -> p a j n", p=P, j=T4))
-            for kp in range(KP):
-                planes["a", kp] = a_raw[:, kp]
-                target["a", kp] = (aq[kp], 0)
-
-        def load_scales():
-            nc.sync.dma_start(out=sc_col[:, :, :T4], in_=x_scale.rearrange("o (a p j) -> p (o a) j", p=P, j=T4))
-
-        def load_r():
-            nc.sync.dma_start(out=r16[:, :, :T4], in_=r.rearrange("(g p t) -> p g t", p=P, t=T4))
-
         load_x(0, 1)
         load_x(1, 1)
         load_x(2, 2)
-        load_scales()
+        nc.sync.dma_start(out=sc_col[:, :, :T4], in_=x_scale.rearrange("o (a p j) -> p (o a) j", p=P, j=T4))
         load_x(4, 1)
         load_panel(0, 0)
         load_x(5, 1)
@@ -114,14 +113,18 @@ def tile_protected_adapter_gradients_s13_kernel(
         load_panel(0, 1)
         load_x(8, 2)
         load_panel(1, 0)
-        load_r()
+        nc.sync.dma_start(out=r16[:, :, :T4], in_=r.rearrange("(g p t) -> p g t", p=P, t=T4))
         load_panel(1, 1)
-        load_a()
+        a_raw = keep.tile([P, KP, T4, R], BF16, name="a_raw")
+        nc.sync.dma_start(out=a_raw[:], in_=a.rearrange("(a p j) n -> p a j n", p=P, j=T4))
+        for kp in range(KP):
+            planes["a", kp] = a_raw[:, kp]
+            target["a", kp] = (aq[kp], 0)
         load_x(10, 2)
         load_x(12, 4)
 
-        nc.vector.memset(half[:], 0.5)
-        nc.scalar.activation(out=one[:], in_=half[:], func=COPY, scale=2.0)
+        nc.vector.memset(point_five[:], 0.5)
+        nc.scalar.activation(out=one[:], in_=point_five[:], func=COPY, scale=2.0)
         nc.vector.memset(ident[:], 0.0)
         make_identity(nc, ident[:], nomemset=True)
         nc.vector.memset(es[:].rearrange("p g n -> p (g n)").bitcast(I32), 0)
@@ -137,7 +140,7 @@ def tile_protected_adapter_gradients_s13_kernel(
                     in_=rows[:, 4 * q : 4 * q + 4, :].bitcast(I32).rearrange("g q n -> q g n"),
                 )
 
-        free_banks = list(range(8))
+        free_banks = list(range(BANKS))
 
         def take_bank(shape):
             b = free_banks.pop(0)
@@ -163,11 +166,10 @@ def tile_protected_adapter_gradients_s13_kernel(
         def quant(key):
             quantise(target[key][0], target[key][1], woven[key][:].rearrange("p n t -> p (n t)"))
 
-        def weave(key, who, lo=0, hi=None, tag=None):
+        def weave(key, who, lo=0, hi=None, buffer=None):
             n = planes[key].shape[2]
             if key not in woven:
-                tag = tag or "weave_" + who
-                woven[key] = ring.tile([P, n, T4], BF16, name=tag, align_bytes=64, bufs=WEAVE_BUFS[tag])
+                woven[key] = ring_tile(buffer or "weave_" + who, [P, n, T4])
             out, in_ = woven[key][:, lo : hi or n], planes[key][:, :, lo : hi or n]
             if who == "g":
                 nc.gpsimd.tensor_scalar(
@@ -176,6 +178,12 @@ def tile_protected_adapter_gradients_s13_kernel(
             else:
                 copy = nc.vector.tensor_copy if who == "v" else nc.scalar.copy
                 copy(out=out.rearrange("p (n i) t -> p n t i", i=4), in_=in_.rearrange("p t (n i) -> p n t i", i=4))
+
+        def weave_first_columns(c, kp, buffer=None):
+            weave(("p", c, kp), "s", 0, SCALAR_COLUMNS[c, kp], buffer)
+
+        def weave_last_columns(c, kp, who, buffer=None):
+            weave(("p", c, kp), who, SCALAR_COLUMNS[c, kp], HALF, buffer)
 
         x_wide = {}
         x_words = {}
@@ -188,16 +196,13 @@ def tile_protected_adapter_gradients_s13_kernel(
             return xt[:, t * K : (t + count) * K].bitcast(E4M3)
 
         def widen_first(kp):
-            w = ring.tile([P, PASS], BF16, name="x_bf1", bufs=WIDE_BUFS[1])
+            w = ring_tile("x_wide1", [P, PASS])
             nc.scalar.copy(out=w[:], in_=x_fp8(0, 1)[:, kp * PASS : (kp + 1) * PASS])
             for u in range(2):
                 x_words[0, kp, u] = w[:].bitcast(F32)[:, u::2]
 
-        def widen(i, count=1, tag=None):
-            if tag:
-                w = ring.tile([P, count * K], BF16, name=tag, align_bytes=64, bufs=WEAVE_BUFS[tag])
-            else:
-                w = ring.tile([P, count * K], BF16, name="x_bf%d" % count, bufs=WIDE_BUFS[count])
+        def widen(i, count=1, buffer=None):
+            w = ring_tile(buffer or "x_wide%d" % count, [P, count * K])
             nc.scalar.copy(out=w[:], in_=x_fp8(i, count))
             for j in range(count):
                 x_wide[i + j] = w[:, j * K : (j + 1) * K]
@@ -207,7 +212,7 @@ def tile_protected_adapter_gradients_s13_kernel(
                         x_words[i + j, kp, u] = w[:].bitcast(F32)[:, w0 + u : w0 + 2 * P : 2]
 
         def sorted_tile(i):
-            w = ring.tile([P, K], BF16, name="x_sorted", bufs=SORTED_BUFS)
+            w = ring_tile("x_sorted", [P, K])
             for kp in range(KP):
                 for u in range(2):
                     x_words[i, kp, u] = w[:].bitcast(F32)[:, (u * KP + kp) * P : (u * KP + kp + 1) * P]
@@ -235,13 +240,13 @@ def tile_protected_adapter_gradients_s13_kernel(
                 for u in range(2):
                     nc.tensor.transpose(bank[:, u, kp, :], x_words[i, kp0 + kp, u], ident[:])
 
-        def scale(i, tag=None, pair_tag="x_gr"):
+        def scale(i, buffer=None, pair_buffer="x_pair"):
             s, j = divmod(i, 2)
-            if tag:
-                x_woven[i] = ring.tile([P, K], BF16, name=tag, align_bytes=64, bufs=WEAVE_BUFS[tag])[:]
+            if buffer:
+                x_woven[i] = ring_tile(buffer, [P, K])[:]
             else:
                 if j == 0:
-                    pair_woven[s] = ring.tile([P, 2, K], BF16, name=pair_tag, align_bytes=64, bufs=WEAVE_BUFS[pair_tag])
+                    pair_woven[s] = ring_tile(pair_buffer, [P, 2, K])
                 x_woven[i] = pair_woven[s][:, j]
             for b, bank, kp0, passes in x_banks[i]:
                 scales = sc_col[:, kp0 : kp0 + passes, :T4].rearrange("p a (o u e) -> p a o u e", o=1, e=2)
@@ -260,20 +265,22 @@ def tile_protected_adapter_gradients_s13_kernel(
         def quant_tile(i):
             quantise(xq[i // 2], (i % 2) * KP * P, x_woven[i])
 
-        def x_mx(out, i, kp, weights, cols):
+        def x_mx(out, i, kp, weights):
             c0 = ((i % 2) * KP + kp) * P
             codes, scales = weights
-            mx(out, xq[i // 2], slice(c0, c0 + P), codes[:, cols].bitcast(E4M3X4), scales[:, cols], kp == 0, kp == KP - 1)
+            mx(out, xq[i // 2], slice(c0, c0 + P), codes[:].bitcast(E4M3X4), scales[:], kp == 0, kp == KP - 1)
 
         h_bank = {}
         h_planes = {}
-        z_bank = {}
-        z_planes = {}
 
         def h_pass(i, c, kp):
             if kp == 0:
                 h_bank[i, c] = take_bank([P, HALF])
-            x_mx(h_bank[i, c][1][:], i, kp, pq[c, kp], slice(0, HALF))
+            x_mx(h_bank[i, c][1][:], i, kp, pq[c, kp])
+
+        def h_passes(i, c):
+            for kp in range(KP):
+                h_pass(i, c, kp)
 
         def h_out(i, c):
             g, t = divmod(i, T4)
@@ -283,10 +290,6 @@ def tile_protected_adapter_gradients_s13_kernel(
             b, bank = h_bank[i, c]
             nc.scalar.activation(out=h_planes[g, c][:, t, :], in_=bank[:], func=COPY, scale=r32[:, g, t : t + 1])
             free_banks.append(b)
-
-        def h_passes(i, c):
-            for kp in range(KP):
-                h_pass(i, c, kp)
 
         def h_mm(i, c):
             h_passes(i, c)
@@ -302,43 +305,38 @@ def tile_protected_adapter_gradients_s13_kernel(
         def z_pair(s):
             g, t0 = divmod(2 * s, T4)
             if t0 == 0:
-                z_planes[g] = keep.tile([P, T4, R], BF16, name="z_pl%d" % g)
-                planes["z", g] = z_planes[g][:]
+                z_planes = keep.tile([P, T4, R], BF16, name="z_pl%d" % g)
+                planes["z", g] = z_planes[:]
                 target["z", g] = (zq[g], 0)
             b, bank = take_bank([P, 2, R])
             for j in range(2):
                 for kp in range(KP):
-                    x_mx(bank[:, j, :], 2 * s + j, kp, aq[kp], slice(0, R))
+                    x_mx(bank[:, j, :], 2 * s + j, kp, aq[kp])
             for j in range(2):
                 t = t0 + j
-                nc.scalar.activation(out=z_planes[g][:, t, :], in_=bank[:, j, :], func=COPY, scale=r32[:, g, t : t + 1])
+                nc.scalar.activation(out=planes["z", g][:, t, :], in_=bank[:, j, :], func=COPY, scale=r32[:, g, t : t + 1])
             free_banks.append(b)
 
+        operands = {"a": (hq, ew, es, out_0), "b": (zq, dw, ds, out_1)}
         block_bank = {}
 
-        def block_passes(job, groups, last=GROUPS - 1):
-            (lhs, words, scales, to), r0, c0, width = job
-            key = (r0, c0, to.shape[1])
-            if key not in block_bank:
-                block_bank[key] = take_bank([P, width])
+        def block_passes(block, groups, last=GROUPS - 1):
+            result, r0, c0, width = block
+            lhs, words, scales, to = operands[result]
+            if block not in block_bank:
+                block_bank[block] = take_bank([P, width])
             for g in groups:
                 rhs = words[:, g, 2 * c0 : 2 * (c0 + width)].bitcast(E2M1X4)
-                mx(block_bank[key][1][:], lhs[g], slice(r0, r0 + P), rhs, scales[:, g, c0 : c0 + width], g == 0, g == last)
+                mx(block_bank[block][1][:], lhs[g], slice(r0, r0 + P), rhs, scales[:, g, c0 : c0 + width], g == 0, g == last)
 
-        def block_out(job, copy=nc.scalar.copy):
-            (lhs, words, scales, to), r0, c0, width = job
-            b, bank = block_bank[r0, c0, to.shape[1]]
-            result = ring.tile([P, width], F32, name="res%d" % width, bufs=RESULT_BUFS[width])
-            copy(out=result[:], in_=bank[:])
+        def block_out(block, copy=nc.scalar.copy):
+            result, r0, c0, width = block
+            b, bank = block_bank[block]
+            sums = ring.tile([P, width], F32, name="res%d" % width, bufs=RESULT_BUFS[width])
+            copy(out=sums[:], in_=bank[:])
             free_banks.append(b)
-            nc.sync.dma_start(out=to[r0 : r0 + P, c0 : c0 + width], in_=result[:])
+            nc.sync.dma_start(out=operands[result][3][r0 : r0 + P, c0 : c0 + width], in_=sums[:])
 
-        def block(job, copy=nc.scalar.copy, order=range(GROUPS)):
-            block_passes(job, order, order[-1])
-            block_out(job, copy)
-
-        grad_b = [((zq, dw, ds, out_1), r0, c0, HALF) for r0 in range(0, R, P) for c0 in range(0, N, HALF)]
-        grad_a = [((hq, ew, es, out_0), r0, 0, R) for r0 in range(0, K, P)]
 
         for kp in range(KP):
             widen_first(kp)
@@ -352,62 +350,62 @@ def tile_protected_adapter_gradients_s13_kernel(
         widen(4)
         scale(0)
         turn(4)
-        weave(("p", 0, 0), "s", 0, 160, tag="panel")
-        weave(("p", 0, 0), "g", 160, tag="panel")
+        weave_first_columns(0, 0, "panel")
+        weave_last_columns(0, 0, "g")
         widen(5)
         turn(5)
         scale(1)
         widen(6, 2)
-        scale(2, pair_tag="weave_g")
+        scale(2, pair_buffer="weave_g")
         scale(3)
         turn(6)
         turn(7)
-        weave(("p", 0, 1), "s", 0, 320, tag="panel")
+        weave_first_columns(0, 1, "panel")
         quant_pair(0)
         quant(("p", 0, 0))
-        weave(("p", 0, 1), "v", 320)
-        h_pass(0, 0, 0)
-        h_pass(1, 0, 0)
+        weave_last_columns(0, 1, "v")
+        for i in (0, 1):
+            h_pass(i, 0, 0)
         widen(8, 2, "weave_v")
-
         quant_pair(1)
         quant(("p", 0, 1))
-        weave(("p", 1, 0), "g", 240, tag="weave_g")
-        h_pass(0, 0, 1)
-        h_pass(1, 0, 1)
+
+        weave_last_columns(1, 0, "g", "weave_g")
+        for i in (0, 1):
+            h_pass(i, 0, 1)
         scale(4)
         scale(5)
         nc.scalar.copy(out=r32[:], in_=r16[:, :, :T4])
-        weave(("p", 1, 0), "s", 0, 240)
-        weave(("p", 1, 1), "s", 0, 256, tag="panel")
+        weave_first_columns(1, 0)
+        weave_first_columns(1, 1, "panel")
         h_passes(2, 0)
         turn(8)
         turn(9)
-        for i in range(2):
+        for i in (0, 1):
             h_out(i, 0)
         h_passes(3, 0)
-        weave(("p", 1, 1), "v", 256)
+        weave_last_columns(1, 1, "v")
         quant_pair(2)
         quant(("p", 1, 0))
         weave(("a", 0), "g")
         quant(("p", 1, 1))
-        for i in range(2, 4):
+        for i in (2, 3):
             h_out(i, 0)
-        for i in range(4, 6):
+        for i in (4, 5):
             h_mm(i, 0)
+
         widen(10)
         scale(6, "weave_h")
         for kp in range(KP):
-            for i in range(2):
+            for i in (0, 1):
                 h_pass(i, 1, kp)
-        h_out(0, 1)
-        h_out(1, 1)
+        for i in (0, 1):
+            h_out(i, 1)
         scale(7, "weave_v")
         for i in range(2, 6):
             h_mm(i, 1)
-        jobs = [("a", 0), ("a", 1), h_piece(0, 0, PIECE), ("z", 0), ("z", 1)]
         quant_tile(6)
-        weave(jobs[1], "g", tag="weave_h")
+        weave(("a", 1), "g", buffer="weave_h")
         quant_tile(7)
         scale(8)
         scale(9)
@@ -417,15 +415,17 @@ def tile_protected_adapter_gradients_s13_kernel(
                 h_mm(i, c)
         quant_tile(8)
         quant_tile(9)
+
         sort_words(10)
         widen_sorted(11)
-        quant(jobs[0])
+        quant(("a", 0))
         sort_words(12)
-        quant(jobs[1])
-        weave(jobs[2], "g", tag="weave_h")
+        quant(("a", 1))
+        pool_piece = h_piece(0, 0, PIECE)
+        weave(pool_piece, "g", buffer="weave_h")
         widen_sorted(13)
-        h_mm(8, 0)
-        h_mm(9, 0)
+        for i in (8, 9):
+            h_mm(i, 0)
         h_passes(8, 1)
         turn(10)
         turn(11)
@@ -439,7 +439,7 @@ def tile_protected_adapter_gradients_s13_kernel(
         quant_tile(10)
         quant_tile(11)
         sort_words(14)
-        weave(jobs[3], "g", tag="weave_g")
+        weave(("z", 0), "g")
         widen_sorted(15)
         z_pair(2)
         turn(12)
@@ -449,13 +449,13 @@ def tile_protected_adapter_gradients_s13_kernel(
         h_mm(10, 0)
         scale(13, "panel")
         h_mm(11, 0)
-        turn(14)
-        turn(15)
         quant_tile(12)
-        weave(jobs[4], "g", tag="panel")
+        weave(("z", 1), "g", buffer="panel")
         quant_tile(13)
         for i in (10, 11):
             h_mm(i, 1)
+        turn(14)
+        turn(15)
         scale(14)
         z_pair(4)
         z_pair(5)
@@ -464,53 +464,58 @@ def tile_protected_adapter_gradients_s13_kernel(
         for c in range(2):
             for i in (12, 13):
                 h_passes(i, c)
-        h_out(12, 0)
-        h_out(13, 0)
+        for i in (12, 13):
+            h_out(i, 0)
         quant_tile(14)
         quant_tile(15)
-        quant(jobs[3])
-        quant(jobs[4])
+        quant(("z", 0))
+        quant(("z", 1))
         z_pair(7)
-        h_out(12, 1)
-        h_out(13, 1)
+        for i in (12, 13):
+            h_out(i, 1)
         for c in range(2):
             for i in (14, 15):
                 h_mm(i, c)
-        by_scalar = [h_piece(g, K - PIECE, K) for g in range(3)]
-        halves = [(key, "s", h * P, (h + 1) * P) for key in by_scalar for h in range(2)]
-        first = [("z", 2), h_piece(0, PIECE, HALF), ("z", 3), h_piece(1, 0, HALF), h_piece(2, 0, HALF)]
-        weave(first[0], "v")
-        quant(jobs[2])
-        quant(first[0])
-        weave(first[1], "v")
-        weave(first[2], "v")
-        quant(first[1])
-        quant(first[2])
-        weave(first[3], "v")
-        weave(first[4], "v")
-        quant(first[3])
-        for g in range(GROUPS):
-            for job in grad_b[:2]:
-                block_passes(job, (g,))
-        for u, job in enumerate(grad_b):
-            if u >= 2:
-                block_passes(job, range(4))
-            block_out(job)
-            if 2 <= u < 1 + len(halves):
-                weave(*halves[u - 2])
-        pieces = [h_piece(3, 0, HALF)]
+
+        by_scalar = [h_piece(g, K - PIECE, K) for g in range(SCALAR_PIECES)]
+        beside_pool = h_piece(0, PIECE, HALF)
+        weave(("z", 2), "v")
+        quant(pool_piece)
+        quant(("z", 2))
+        weave(beside_pool, "v")
+        weave(("z", 3), "v")
+        quant(beside_pool)
+        quant(("z", 3))
+        pieces = [h_piece(g, 0, HALF) for g in range(1, GROUPS)]
         pieces = pieces + [h_piece(g, HALF, K - PIECE) for g in range(GROUPS)]
-        pieces = pieces + [h_piece(g, K - PIECE, K) for g in range(len(by_scalar), GROUPS)]
-        for before, key in zip(first[-1:] + pieces, pieces):
+        pieces = pieces + [h_piece(g, K - PIECE, K) for g in range(SCALAR_PIECES, GROUPS)]
+        weave(pieces[0], "v")
+        for before, key in zip(pieces, pieces[1:]):
             weave(key, "v")
             quant(before)
+
+        grad_b = [("b", r0, c0, HALF) for r0 in range(0, R, P) for c0 in range(0, N, HALF)]
+        halves = [(key, "s", h * P, (h + 1) * P) for key in by_scalar for h in range(2)]
+        for g in range(GROUPS):
+            for block in grad_b[:OPEN_BLOCKS]:
+                block_passes(block, (g,))
+        for u, block in enumerate(grad_b):
+            if u >= OPEN_BLOCKS:
+                block_passes(block, range(GROUPS))
+            block_out(block)
+            if OPEN_BLOCKS <= u < len(grad_b) - 1:
+                weave(*halves[u - OPEN_BLOCKS])
         quant(by_scalar[0])
         quant(pieces[-1])
         quant(by_scalar[1])
-        for kb, job in enumerate(grad_a[:-1]):
-            if kb == 2:
+
+        for r0 in range(0, K - P, P):
+            if r0 == 2 * P:
                 weave(*halves[-1])
                 quant(by_scalar[2])
-            block(job, order=(0, 3, 1, 2) if kb == 6 else range(GROUPS))
-        for h, copy in enumerate((nc.scalar.copy, nc.vector.tensor_copy)):
-            block((grad_a[0][0], K - P, h * P, P), copy)
+            order = (0, 3, 1, 2) if r0 == K - PIECE else range(GROUPS)
+            block_passes(("a", r0, 0, R), order, order[-1])
+            block_out(("a", r0, 0, R))
+        for c0, copy in ((0, nc.scalar.copy), (P, nc.vector.tensor_copy)):
+            block_passes(("a", K - P, c0, P), range(GROUPS))
+            block_out(("a", K - P, c0, P), copy)

from contextlib import ExitStack

import concourse.mybir as mybir
from concourse.masks import make_identity

M, K, N, R = 2048, 1024, 2048, 256
FLOPS = 2 * M * K * (K + R) + 2 * K * M * R + 2 * R * M * N

F32 = mybir.dt.float32
BF16 = mybir.dt.bfloat16
I32 = mybir.dt.int32
U32 = mybir.dt.uint32
U8 = mybir.dt.uint8
E4M3 = mybir.dt.float8_e4m3fn
E4M3X4 = mybir.dt.float8_e4m3fn_x4
E2M1X4 = mybir.dt.float4_e2m1fn_x4
MULT = mybir.AluOpType.mult
ADD = mybir.AluOpType.add
COPY = mybir.ActivationFunctionType.Copy

P = 128
T4 = 4
PASS = P * T4
GROUPS = M // PASS
PAIRS = GROUPS * T4 // 2
KP = K // PASS
BANKS = 8
HALF = 512
PIECE = 256

SCALAR_COLUMNS = {(0, 0): 128, (0, 1): 320, (1, 0): 224, (1, 1): 256}
SCALAR_PIECES = 3
OPEN_BLOCKS = 2

RING_BUFS = {
    "weave_v": 4,
    "weave_s": SCALAR_PIECES,
    "weave_g": 1,
    "weave_h": 1,
    "panel": 2,
    "x_pair": 2,
    "x_wide1": 2,
    "x_wide2": 2,
    "x_sorted": 4,
}
RESULT_BUFS = {HALF: 4, R: K // P - 1, P: 2}


def tile_protected_adapter_gradients_s13_kernel(
    tc, x_bytes, x_scale, proj, a, r, e_words, e_scales, d_words, d_scales, out_0, out_1
):
    nc = tc.nc
    with ExitStack() as ctx:
        keep = ctx.enter_context(tc.tile_pool(name="keep", bufs=1))
        ring = ctx.enter_context(tc.tile_pool(name="ring", bufs=2))
        psum = ctx.enter_context(tc.psum_pool(name="psum", bufs=1))
        ctx.enter_context(tc.manual_schedule())

        r16 = keep.tile([P, GROUPS, 4 * T4], BF16, name="r16")
        sc_col = keep.tile([P, KP, 2 * T4], F32, name="sc_col")
        ident = keep.tile([P, P], F32, name="ident")
        point_five = keep.tile([P, 1], F32, name="point_five")
        one = keep.tile([P, 1], F32, name="one")
        es = keep.tile([P, GROUPS, R], U8, name="es", align_bytes=256)
        ds = keep.tile([P, GROUPS, N], U8, name="ds", align_bytes=256)
        r32 = keep.tile([P, GROUPS, T4], F32, name="r32")
        ew = keep.tile([P, GROUPS, 2 * R], U8, name="ew", align_bytes=256)
        dw = keep.tile([P, GROUPS, 2 * N], U8, name="dw", align_bytes=256)

        def mx_tiles(name, width):
            codes = keep.tile([P, width], U32, name=name + "_q", align_bytes=256)
            scales = keep.tile([P, width], U8, name=name + "_s", align_bytes=256)
            return codes, scales

        def ring_tile(name, shape):
            return ring.tile(shape, BF16, name=name, align_bytes=64, bufs=RING_BUFS[name])

        pq = {(c, kp): mx_tiles("p%d%d" % (c, kp), HALF) for c in range(2) for kp in range(KP)}
        aq = {kp: mx_tiles("a%d" % kp, R) for kp in range(KP)}
        hq = {g: mx_tiles("h%d" % g, K) for g in range(GROUPS)}
        zq = {g: mx_tiles("z%d" % g, R) for g in range(GROUPS)}
        xq = {s: mx_tiles("x%d" % (2 * s), 2 * KP * P) for s in range(PAIRS)}

        planes = {}
        woven = {}
        target = {}

        proj_v = proj.rearrange("(a p j) n -> a p j n", p=P, j=T4)
        xb_v = x_bytes.rearrange("(g p t) k -> g p t k", p=P, t=T4)
        x_in = {}

        def load_x(first, count):
            g, t0 = divmod(first, T4)
            xt = keep.tile([P, count * K], U8, name="x_in%d" % first)
            nc.sync.dma_start(out=xt[:].rearrange("p (t k) -> p t k", k=K), in_=xb_v[g, :, t0 : t0 + count, :])
            for t in range(count):
                x_in[first + t] = (xt, t)

        def load_panel(c, kp):
            w = keep.tile([P, T4, HALF], BF16, name="p_raw%d%d" % (c, kp))
            nc.sync.dma_start(out=w[:], in_=proj_v[kp][:, :, c * HALF : (c + 1) * HALF])
            planes["p", c, kp] = w[:]
            target["p", c, kp] = (pq[c, kp], 0)

        load_x(0, 1)
        load_x(1, 1)
        load_x(2, 2)
        nc.sync.dma_start(out=sc_col[:, :, :T4], in_=x_scale.rearrange("o (a p j) -> p (o a) j", p=P, j=T4))
        load_x(4, 1)
        load_panel(0, 0)
        load_x(5, 1)
        load_x(6, 2)
        load_panel(0, 1)
        load_x(8, 2)
        load_panel(1, 0)
        nc.sync.dma_start(out=r16[:, :, :T4], in_=r.rearrange("(g p t) -> p g t", p=P, t=T4))
        load_panel(1, 1)
        a_raw = keep.tile([P, KP, T4, R], BF16, name="a_raw")
        nc.sync.dma_start(out=a_raw[:], in_=a.rearrange("(a p j) n -> p a j n", p=P, j=T4))
        for kp in range(KP):
            planes["a", kp] = a_raw[:, kp]
            target["a", kp] = (aq[kp], 0)
        load_x(10, 2)
        load_x(12, 4)

        nc.vector.memset(point_five[:], 0.5)
        nc.scalar.activation(out=one[:], in_=point_five[:], func=COPY, scale=2.0)
        nc.vector.memset(ident[:], 0.0)
        make_identity(nc, ident[:], nomemset=True)
        nc.vector.memset(es[:].rearrange("p g n -> p (g n)").bitcast(I32), 0)
        nc.vector.memset(ds[:].rearrange("p g n -> p (g n)").bitcast(I32), 0)

        for g in range(GROUPS):
            nc.sync.dma_start(out=dw[:, g, :].bitcast(I32), in_=d_words[g].bitcast(I32))
        nc.sync.dma_start(out=ew[:].bitcast(I32), in_=e_words.bitcast(I32).rearrange("g p n -> p g n"))
        for q in range(4):
            for tile, rows in ((ds, d_scales), (es, e_scales)):
                nc.sync.dma_start(
                    out=tile[32 * q : 32 * q + 4].bitcast(I32),
                    in_=rows[:, 4 * q : 4 * q + 4, :].bitcast(I32).rearrange("g q n -> q g n"),
                )

        free_banks = list(range(BANKS))

        def take_bank(shape):
            b = free_banks.pop(0)
            return b, psum.tile(shape, F32, name="bank%d" % b)

        def mx(out, lhs, lcols, rhs, rhs_scale, start, stop):
            nc.tensor.matmul_mx(
                out=out,
                lhsT=lhs[0][:, lcols].bitcast(E4M3X4),
                lhsT_scale=lhs[1][:, lcols],
                rhs=rhs,
                rhs_scale=rhs_scale,
                start=start,
                stop=stop,
            )

        def quantise(codes_scales, c0, values):
            cols = slice(c0, c0 + values.shape[1] // T4)
            nc.vector.quantize_mx(
                out=codes_scales[0][:, cols].bitcast(E4M3X4), scales=codes_scales[1][:, cols], in_=values
            )

        def quant(key):
            quantise(target[key][0], target[key][1], woven[key][:].rearrange("p n t -> p (n t)"))

        def weave(key, who, lo=0, hi=None, buffer=None):
            n = planes[key].shape[2]
            if key not in woven:
                woven[key] = ring_tile(buffer or "weave_" + who, [P, n, T4])
            out, in_ = woven[key][:, lo : hi or n], planes[key][:, :, lo : hi or n]
            if who == "g":
                nc.gpsimd.tensor_scalar(
                    out=out, in0=in_.rearrange("p t n -> p n t"), scalar1=1.0, scalar2=0.0, op0=MULT, op1=ADD
                )
            else:
                copy = nc.vector.tensor_copy if who == "v" else nc.scalar.copy
                copy(out=out.rearrange("p (n i) t -> p n t i", i=4), in_=in_.rearrange("p t (n i) -> p n t i", i=4))

        def weave_first_columns(c, kp, buffer=None):
            weave(("p", c, kp), "s", 0, SCALAR_COLUMNS[c, kp], buffer)

        def weave_last_columns(c, kp, who, buffer=None):
            weave(("p", c, kp), who, SCALAR_COLUMNS[c, kp], HALF, buffer)

        x_wide = {}
        x_words = {}
        x_banks = {}
        x_woven = {}
        pair_woven = {}

        def x_fp8(i, count):
            xt, t = x_in[i]
            return xt[:, t * K : (t + count) * K].bitcast(E4M3)

        def widen_first(kp):
            w = ring_tile("x_wide1", [P, PASS])
            nc.scalar.copy(out=w[:], in_=x_fp8(0, 1)[:, kp * PASS : (kp + 1) * PASS])
            for u in range(2):
                x_words[0, kp, u] = w[:].bitcast(F32)[:, u::2]

        def widen(i, count=1, buffer=None):
            w = ring_tile(buffer or "x_wide%d" % count, [P, count * K])
            nc.scalar.copy(out=w[:], in_=x_fp8(i, count))
            for j in range(count):
                x_wide[i + j] = w[:, j * K : (j + 1) * K]
                for kp in range(KP):
                    for u in range(2):
                        w0 = 2 * P * (KP * j + kp)
                        x_words[i + j, kp, u] = w[:].bitcast(F32)[:, w0 + u : w0 + 2 * P : 2]

        def sorted_tile(i):
            w = ring_tile("x_sorted", [P, K])
            for kp in range(KP):
                for u in range(2):
                    x_words[i, kp, u] = w[:].bitcast(F32)[:, (u * KP + kp) * P : (u * KP + kp + 1) * P]
            return w

        def widen_sorted(i):
            nc.vector.tensor_scalar(
                out=sorted_tile(i)[:].rearrange("p (u w e) -> p w u e", u=2, e=2),
                in0=x_fp8(i, 1),
                scalar1=one[:],
                scalar2=None,
                op0=MULT,
            )

        def sort_words(i):
            nc.vector.tensor_copy(
                out=sorted_tile(i)[:].rearrange("p (u w e) -> p u w e", u=2, e=2),
                in_=x_wide[i].rearrange("p (w u e) -> p u w e", u=2, e=2),
            )

        def turn(i, kp0=0, passes=KP):
            b, bank = take_bank([P, 2, passes, P])
            x_banks.setdefault(i, []).append((b, bank, kp0, passes))
            for kp in range(passes):
                for u in range(2):
                    nc.tensor.transpose(bank[:, u, kp, :], x_words[i, kp0 + kp, u], ident[:])

        def scale(i, buffer=None, pair_buffer="x_pair"):
            s, j = divmod(i, 2)
            if buffer:
                x_woven[i] = ring_tile(buffer, [P, K])[:]
            else:
                if j == 0:
                    pair_woven[s] = ring_tile(pair_buffer, [P, 2, K])
                x_woven[i] = pair_woven[s][:, j]
            for b, bank, kp0, passes in x_banks[i]:
                scales = sc_col[:, kp0 : kp0 + passes, :T4].rearrange("p a (o u e) -> p a o u e", o=1, e=2)
                values = x_woven[i][:, kp0 * PASS : (kp0 + passes) * PASS]
                nc.vector.tensor_tensor(
                    out=values.rearrange("p (a m u e) -> p a m u e", a=passes, u=2, e=2),
                    in0=bank[:].bitcast(BF16).rearrange("p u a (m e) -> p a m u e", e=2),
                    in1=scales.to_broadcast([P, passes, P, 2, 2]),
                    op=MULT,
                )
                free_banks.append(b)

        def quant_pair(s):
            quantise(xq[s], 0, pair_woven[s][:].rearrange("p j n -> p (j n)"))

        def quant_tile(i):
            quantise(xq[i // 2], (i % 2) * KP * P, x_woven[i])

        def x_mx(out, i, kp, weights):
            c0 = ((i % 2) * KP + kp) * P
            codes, scales = weights
            mx(out, xq[i // 2], slice(c0, c0 + P), codes[:].bitcast(E4M3X4), scales[:], kp == 0, kp == KP - 1)

        h_bank = {}
        h_planes = {}

        def h_pass(i, c, kp):
            if kp == 0:
                h_bank[i, c] = take_bank([P, HALF])
            x_mx(h_bank[i, c][1][:], i, kp, pq[c, kp])

        def h_passes(i, c):
            for kp in range(KP):
                h_pass(i, c, kp)

        def h_out(i, c):
            g, t = divmod(i, T4)
            if t == 0:
                name = "h_pl%d%d" % (g, c) if g < 2 else "p_raw%d%d" % (g - 2, c)
                h_planes[g, c] = keep.tile([P, T4, HALF], BF16, name=name)
            b, bank = h_bank[i, c]
            nc.scalar.activation(out=h_planes[g, c][:, t, :], in_=bank[:], func=COPY, scale=r32[:, g, t : t + 1])
            free_banks.append(b)

        def h_mm(i, c):
            h_passes(i, c)
            h_out(i, c)

        def h_piece(g, lo, hi):
            c, n0 = divmod(lo, HALF)
            key = ("h", g, lo, hi)
            planes[key] = h_planes[g, c][:, :, n0 : n0 + hi - lo]
            target[key] = (hq[g], lo)
            return key

        def z_pair(s):
            g, t0 = divmod(2 * s, T4)
            if t0 == 0:
                z_planes = keep.tile([P, T4, R], BF16, name="z_pl%d" % g)
                planes["z", g] = z_planes[:]
                target["z", g] = (zq[g], 0)
            b, bank = take_bank([P, 2, R])
            for j in range(2):
                for kp in range(KP):
                    x_mx(bank[:, j, :], 2 * s + j, kp, aq[kp])
            for j in range(2):
                t = t0 + j
                nc.scalar.activation(out=planes["z", g][:, t, :], in_=bank[:, j, :], func=COPY, scale=r32[:, g, t : t + 1])
            free_banks.append(b)

        operands = {"a": (hq, ew, es, out_0), "b": (zq, dw, ds, out_1)}
        block_bank = {}

        def block_passes(block, groups, last=GROUPS - 1):
            result, r0, c0, width = block
            lhs, words, scales, to = operands[result]
            if block not in block_bank:
                block_bank[block] = take_bank([P, width])
            for g in groups:
                rhs = words[:, g, 2 * c0 : 2 * (c0 + width)].bitcast(E2M1X4)
                mx(block_bank[block][1][:], lhs[g], slice(r0, r0 + P), rhs, scales[:, g, c0 : c0 + width], g == 0, g == last)

        def block_out(block, copy=nc.scalar.copy):
            result, r0, c0, width = block
            b, bank = block_bank[block]
            sums = ring.tile([P, width], F32, name="res%d" % width, bufs=RESULT_BUFS[width])
            copy(out=sums[:], in_=bank[:])
            free_banks.append(b)
            nc.sync.dma_start(out=operands[result][3][r0 : r0 + P, c0 : c0 + width], in_=sums[:])


        for kp in range(KP):
            widen_first(kp)
        widen_sorted(1)
        for kp in range(KP):
            turn(0, kp, 1)
        turn(1)
        widen(2, 2)
        turn(2)
        turn(3)
        widen(4)
        scale(0)
        turn(4)
        weave_first_columns(0, 0, "panel")
        weave_last_columns(0, 0, "g")
        widen(5)
        turn(5)
        scale(1)
        widen(6, 2)
        scale(2, pair_buffer="weave_g")
        scale(3)
        turn(6)
        turn(7)
        weave_first_columns(0, 1, "panel")
        quant_pair(0)
        quant(("p", 0, 0))
        weave_last_columns(0, 1, "v")
        for i in (0, 1):
            h_pass(i, 0, 0)
        widen(8, 2, "weave_v")
        quant_pair(1)
        quant(("p", 0, 1))

        weave_last_columns(1, 0, "g", "weave_g")
        for i in (0, 1):
            h_pass(i, 0, 1)
        scale(4)
        scale(5)
        nc.scalar.copy(out=r32[:], in_=r16[:, :, :T4])
        weave_first_columns(1, 0)
        weave_first_columns(1, 1, "panel")
        h_passes(2, 0)
        turn(8)
        turn(9)
        for i in (0, 1):
            h_out(i, 0)
        h_passes(3, 0)
        weave_last_columns(1, 1, "v")
        quant_pair(2)
        quant(("p", 1, 0))
        weave(("a", 0), "g")
        quant(("p", 1, 1))
        for i in (2, 3):
            h_out(i, 0)
        for i in (4, 5):
            h_mm(i, 0)

        widen(10)
        scale(6, "weave_h")
        for kp in range(KP):
            for i in (0, 1):
                h_pass(i, 1, kp)
        for i in (0, 1):
            h_out(i, 1)
        scale(7, "weave_v")
        for i in range(2, 6):
            h_mm(i, 1)
        quant_tile(6)
        weave(("a", 1), "g", buffer="weave_h")
        quant_tile(7)
        scale(8)
        scale(9)
        widen(12)
        for c in range(2):
            for i in (6, 7):
                h_mm(i, c)
        quant_tile(8)
        quant_tile(9)

        sort_words(10)
        widen_sorted(11)
        quant(("a", 0))
        sort_words(12)
        quant(("a", 1))
        pool_piece = h_piece(0, 0, PIECE)
        weave(pool_piece, "g", buffer="weave_h")
        widen_sorted(13)
        for i in (8, 9):
            h_mm(i, 0)
        h_passes(8, 1)
        turn(10)
        turn(11)
        scale(10)
        scale(11)
        z_pair(0)
        widen(14, 1, "weave_g")
        z_pair(1)
        h_out(8, 1)
        h_mm(9, 1)
        quant_tile(10)
        quant_tile(11)
        sort_words(14)
        weave(("z", 0), "g")
        widen_sorted(15)
        z_pair(2)
        turn(12)
        turn(13)
        scale(12, "panel")
        z_pair(3)
        h_mm(10, 0)
        scale(13, "panel")
        h_mm(11, 0)
        quant_tile(12)
        weave(("z", 1), "g", buffer="panel")
        quant_tile(13)
        for i in (10, 11):
            h_mm(i, 1)
        turn(14)
        turn(15)
        scale(14)
        z_pair(4)
        z_pair(5)
        scale(15)
        z_pair(6)
        for c in range(2):
            for i in (12, 13):
                h_passes(i, c)
        for i in (12, 13):
            h_out(i, 0)
        quant_tile(14)
        quant_tile(15)
        quant(("z", 0))
        quant(("z", 1))
        z_pair(7)
        for i in (12, 13):
            h_out(i, 1)
        for c in range(2):
            for i in (14, 15):
                h_mm(i, c)

        by_scalar = [h_piece(g, K - PIECE, K) for g in range(SCALAR_PIECES)]
        beside_pool = h_piece(0, PIECE, HALF)
        weave(("z", 2), "v")
        quant(pool_piece)
        quant(("z", 2))
        weave(beside_pool, "v")
        weave(("z", 3), "v")
        quant(beside_pool)
        quant(("z", 3))
        pieces = [h_piece(g, 0, HALF) for g in range(1, GROUPS)]
        pieces = pieces + [h_piece(g, HALF, K - PIECE) for g in range(GROUPS)]
        pieces = pieces + [h_piece(g, K - PIECE, K) for g in range(SCALAR_PIECES, GROUPS)]
        weave(pieces[0], "v")
        for before, key in zip(pieces, pieces[1:]):
            weave(key, "v")
            quant(before)

        grad_b = [("b", r0, c0, HALF) for r0 in range(0, R, P) for c0 in range(0, N, HALF)]
        halves = [(key, "s", h * P, (h + 1) * P) for key in by_scalar for h in range(2)]
        for g in range(GROUPS):
            for block in grad_b[:OPEN_BLOCKS]:
                block_passes(block, (g,))
        for u, block in enumerate(grad_b):
            if u >= OPEN_BLOCKS:
                block_passes(block, range(GROUPS))
            block_out(block)
            if OPEN_BLOCKS <= u < len(grad_b) - 1:
                weave(*halves[u - OPEN_BLOCKS])
        quant(by_scalar[0])
        quant(pieces[-1])
        quant(by_scalar[1])

        for r0 in range(0, K - P, P):
            if r0 == 2 * P:
                weave(*halves[-1])
                quant(by_scalar[2])
            order = (0, 3, 1, 2) if r0 == K - PIECE else range(GROUPS)
            block_passes(("a", r0, 0, R), order, order[-1])
            block_out(("a", r0, 0, R))
        for c0, copy in ((0, nc.scalar.copy), (P, nc.vector.tensor_copy)):
            block_passes(("a", K - P, c0, P), range(GROUPS))
            block_out(("a", K - P, c0, P), copy)
